import numpy as np, ml_dtypes
CORES = [9,25,41,57]
N = 4
BF = ml_dtypes.bfloat16
S, CAP, WC, NB, RO, OC, SHO = 192, 64, 4096, 256, 4, 0, 6
MU = (53, 211, 97, 389)
FC, L = 16 * NB, N * CAP
KB = (np.arange(16)[:, None] >> np.arange(4)) & 1
def cells(x):
    p = [(x[..., e, :, None] >> 2) + KB[:, e] for e in range(4)]
    w = [np.where(KB[:, e] == 1, x[..., e, :, None] & 3, 4 - (x[..., e, :, None] & 3)) for e in range(4)]
    i = (((p[0] * (2 * p[1] + 1)) >> 2) + MU[0] * p[2] + MU[1] * p[3]) & (WC - 1)
    b = (((p[2] * (2 * p[3] + 1)) >> 2) + MU[2] * p[0] + MU[3] * p[1]) & (NB - 1)
    return i, b, w[0] * w[1] * w[2] * w[3]
def parts(rng):
    cf = rng.integers(0, 237, (N, 8, 1, WC)) + rng.integers(0, 4, (N, 8, 16, WC))
    ft = rng.integers(0, 256, (N, 8, 16, FC)); ft[:, ::2, :4] = 96 + (ft[:, ::2, :4] >> 2)
    tg = rng.integers(0, 256, (N, 8, 16, S)); x = rng.integers(0, 256, (N, 8, 4, S))
    fav = rng.integers(0, N, (N, 8, 1)); hit = rng.random((N, 8, S)) < rng.choice(np.array([0.0, 0.1, 0.3, 0.5]), (N, 8, 1))
    x[:, :, OC] = np.where(hit, (fav << SHO) + (x[:, :, OC] & ((1 << SHO) - 1)), x[:, :, OC])
    return cf, ft, tg, x
def pack(cf, ft, tg, x):
    b = lambda v, n: np.ascontiguousarray(v.reshape(N, 128, n)).astype(np.float32).astype(BF)
    return {"cf": b(cf, WC), "ft": b(ft, FC), "tg": b(tg, S), "x0": np.ascontiguousarray(x.reshape(N, 32, S)).astype(np.int32)}
def setup_inputs(rng):
    return pack(*parts(rng))
def setup_inputs_spread(rng):
    cf, ft, tg, x = parts(rng)
    cf = np.where(rng.random((N, 8, 1, WC)) < 0.5, rng.integers(0, 241, cf.shape), (241 * rng.random(cf.shape) ** 4).astype(np.int64))
    v = np.minimum(np.exp2(8 * rng.random(ft.shape)).astype(np.int64) - 1, 255); ft = np.where(rng.random((N, 8, 1, FC)) < 0.5, v, 255 - v)
    v = np.minimum(np.exp2(8 * rng.random(tg.shape)).astype(np.int64) - 1, 255); tg = np.where(rng.random((N, 8, 1, S)) < 0.5, v, 255 - v)
    v = np.minimum((256 * rng.random(x.shape) ** 2).astype(np.int64), 255); x = np.where(rng.random((N, 8, 4, 1)) < 0.5, v, 255 - v)
    return pack(cf, ft, tg, x)
def setup_inputs_ends(rng):
    e = lambda top, *shape: top * rng.integers(0, 2, shape)
    cf = e(240, N, 8, 16, WC); kind = rng.integers(0, 4, (N, 8, 1, NB, 1)); fv = e(255, N, 8, 16, NB, 16)
    fv = np.ascontiguousarray(np.where(kind == 0, 0, np.where(kind == 1, 255, fv)))
    rec = rng.integers(0, 3, (N, 8, 1, S)); tg = np.where(rec == 0, 0, np.where(rec == 1, 255, e(255, N, 8, 16, S)))
    x = e(255, N, 8, 4, S); x[:, :, OC] = np.where(rng.random((N, 8, S)) < 0.2, rng.integers(0, 256, (N, 8, S)), x[:, :, OC])
    z = np.zeros((4, 1), np.int64); z[OC] = 255; zi, zb, zw = cells(z); live = zw[0] > 0; zi = zi[0][live]; zb = zb[0][live]
    tb = cells(np.full((4, 1), 255))[1][0]; r = N - 1
    for g in range(8):
        for turn in ((0, 1) if g % 2 else (1, 0)):
            if turn == 0: cf[r, g][:, zi] = 0; cf[r, g][15, zi] = 240; fv[r, g][:, zb] = 255; fv[r, g][:, zb, 15] = 0
            else: fv[r, g][:, tb] = 255
    x[0, :, :, 0] = z[:, 0]; tg[0, :, :, 0] = 255; x[0, :, :, 1] = 255; tg[0, :, :, 1] = 0
    x[r, 7, OC, rng.permutation(S)[:CAP + 4]] = 255
    h = int(np.flatnonzero((x[r, 7, OC] >> SHO) == r)[CAP - 1]); x[r, 7, :, h] = 255; tg[r, 7, :, h] = 0
    return pack(cf, fv, tg, x)
def setup_inputs_corners(rng):
    cf, ft, tg, x = parts(rng)
    mode = rng.integers(0, 4, (N, 8, 1, S)); low = np.where(mode == 0, 0, np.where(mode == 1, 2, np.where(mode == 2, 3, x & 3)))
    hi = np.where(rng.random(x.shape) < 0.3, 252 * rng.integers(0, 2, x.shape), x - (x & 3)); x = hi + low
    own = np.zeros((N, 8, S), np.int64)
    for q in range(N):
        for g in range(8):
            o = int(rng.integers(0, N)); n = int(rng.choice(np.array([0, 1, CAP - 1, CAP, CAP + 1, S])))
            if q == 0: o = 1 + g % (N - 1); n = (CAP, CAP + 1, S, CAP - 1, 1, 0, CAP, CAP + 1)[g]
            own[q, g] = rng.permutation(np.concatenate([np.full(n, o), (o + rng.integers(1, N, S - n)) % N]))
    x[:, :, OC] = (own << SHO) + (hi[:, :, OC] & ((1 << SHO) - 1)) + low[:, :, OC]
    few = np.array([0, 1, 254, 255]); v = rng.choice(np.array([119, 120, 121, 127, 128, 129, 135, 136, 137]), (8, 16))
    v[5, 4:] = rng.choice(np.array([0, 1, 100, 254, 255]), 12)
    for g in (1, 3, 5, 7):
        ft[:, g, :4] = v[g, :4, None]; ft[:, g, 4:] = v[5, 4:, None] if g == 5 else rng.choice(few, (N, 12, FC))
        tg[:, g, :4] = v[g, :4, None] + rng.integers(-1, 2, (N, 4, S)); tg[:, g, 4:] = rng.choice(few, (N, 12, S))
    tg[:, 5] = np.where(rng.random((N, 1, S)) < 0.25, v[5][:, None], tg[:, 5])
    for o in range(N):
        two = np.flatnonzero(own[0, 5] == o)[:2]
        if len(two) == 2: x[0, 5, :, two[1]] = x[0, 5, :, two[0]]; tg[0, 5, :, two[0]] = v[5]; tg[0, 5, :, two[1]] = 255
    return pack(cf, ft, tg, x)
def setup_inputs_crowd(rng):
    cf, ft, tg, x = parts(rng); turn = int(rng.integers(0, N)); e = (OC + 1) % 4
    for g in range(8):
        o = (g + turn) % N
        for again in range(64):
            pt = 4 * rng.integers(0, 64, 4); pt[OC] = (o << SHO) + 4 * rng.integers(0, 1 << (SHO - 2))
            two = np.stack([pt, pt], axis=1); two[e, 1] = (two[e, 1] + 64) & 255; zi, zb, zw = cells(two)
            if zi[0, 0] != zi[1, 0] and zb[0, 0] != zb[1, 0]: break
        v = pt[None, :, None] + rng.integers(0, 3, (N, 4, S))
        if g == 1: v[N - 1, e, CAP - 1] = (v[N - 1, e, CAP - 1] + 64) & 255
        if g == 5: v[0, e, 0] = (v[0, e, 0] + 64) & 255
        if g % 4 == 2: v[:, e] = (v[:, e] + 64 * rng.integers(0, 3, (N, S))) & 255
        if g % 4 == 3: v[:, :, 1::2] = x[:, g, :, 1::2]
        x[:, g] = v
    return pack(cf, ft, tg, x)
def setup_inputs_calm(rng):
    cf, ft, tg, x = parts(rng)
    cf = 235 * rng.integers(0, 2, (N, 8, 1, WC)) + rng.integers(0, 6, (N, 8, 16, WC))
    step = 128 + (np.arange(8)[:, None] & 3) * (1 - 2 * rng.integers(0, 2, (8, 4)))
    ft[:, :, :4] = step[None, :, :, None]; tg[:, :, :4] = step[None, :, :, None]
    ft[:, 1::2, 4:] = rng.choice(np.array([0, 1, 2, 3, 252, 253, 254, 255]), (N, 4, 12, FC))
    tg[:, :, 4:] = 255 * rng.integers(0, 2, (N, 8, 12, S))
    for g in (0, 4):
        low = rng.integers(0, 2 if g == 0 else 1, (N, 16, WC)); low[:, 0] = 0
        cf[:, g] = np.where(rng.random((N, 1, WC)) < 0.5, low, cf[:, g]); tg[:, g, 4:] = np.where(rng.random((N, 1, S)) < 0.5, 0, tg[:, g, 4:])
        if g == 0: x[0, g, :, 0] = x[0, g, :, 0] - (x[0, g, :, 0] & 3)
        i, b, w = cells(x[0, g, :, :1]); tg[0, g, 4:, 0] = 0
        cf[int(x[0, g, OC, 0]) >> SHO, g, :, int(i[0, np.argmax(w[0])])] = 0 if g == 4 else (np.arange(16) >= int(rng.integers(1, 16))).astype(np.int64)
    for q, g in ((0, 3), (N - 1, 6)):
        o = (q + 1 + int(rng.integers(0, N - 1))) % N; r = (x[q, g, OC] - (o << SHO)) & 255
        r = np.where((r < (1 << SHO) + 12) | (r >= 244), (r + 128) & 255, r)
        s = rng.permutation(S)[:8]; r[s] = (1 << SHO) - 1 if step[g, OC] > 128 else 0
        x[q, g, OC] = ((o << SHO) + r) & 255; tg[q, g, 4:, s] = 255
    return pack(cf, ft, tg, x)
def check_inputs(d):
    bad = []
    for k, top in (("cf", 240), ("ft", 255), ("tg", 255), ("x0", 255)):
        v = np.asarray(d[k]).astype(np.float64)
        if not (np.min(v) >= 0 and np.max(v) <= top): bad.append("range of " + k)
        if np.any(v != np.floor(v)): bad.append("whole numbers of " + k)
    return bad
def firsts(lanes, key):
    return lanes[np.unique(key[lanes], return_index=True)[1]]
def reference(cf, ft, tg, x0):
    C = cf.astype(np.float32).astype(np.int64).reshape(N, 8, 16, WC); F = ft.astype(np.float32).astype(np.int64).reshape(N, 8, 16, FC)
    t = tg.astype(np.float32).astype(np.int64).reshape(N, 8, 16, S); x = x0.astype(np.int64).reshape(N, 8, 4, S); ys = np.zeros((N, 8, 16, S), np.int64)
    for rnd in range(RO):
        own = x[:, :, OC] >> SHO
        h = (own[:, :, None, :] == np.arange(N)[:, None]).astype(np.int64)
        place = np.take_along_axis(np.add.accumulate(h, axis=3) - h, own[:, :, None, :], 2)[:, :, 0]
        q, g, s = np.nonzero(place < CAP); o = own[q, g, s]; l = CAP * q + place[q, g, s]
        X = np.zeros((N, 8, 4, L), np.int64); T = np.zeros((N, 8, 16, L), np.int64); live = np.zeros((N, 8, L), bool)
        X[o, g, :, l] = x[q, g, :, s]; T[o, g, :, l] = t[q, g, :, s]; live[o, g, l] = True
        i, b, w = cells(X)
        m = np.argmax(np.take_along_axis(C, i.reshape(N, 8, 1, L * 16), 3), axis=2).reshape(N, 8, L, 16)
        v = np.take_along_axis(F, (16 * b + m).reshape(N, 8, 1, L * 16), 3).reshape(N, 8, 16, L, 16)
        y = np.sum(v * w[:, :, None], axis=4) >> 8
        sg = np.sign(T - y)
        k = np.argmax(w, axis=3)[..., None]
        ci, cb, cm = [np.take_along_axis(z, k, 3)[..., 0] for z in (i, b, m)]; fc = 16 * cb + cm
        u = np.take_along_axis(F, (16 * cb[..., None] + np.arange(16)).reshape(N, 8, 1, L * 16), 3).reshape(N, 8, 16, L, 16)
        up = np.sign(np.sum(sg[..., None] * u, axis=2))
        for r in range(N):
            for a in range(8):
                lanes = np.flatnonzero(live[r, a])
                win = firsts(lanes, ci[r, a]); C[r, a][:, ci[r, a, win]] += up[r, a, win].T
                win = firsts(lanes, fc[r, a]); at = fc[r, a, win]; F[r, a][:, at] = np.clip(F[r, a][:, at] + sg[r, a][:, win], 0, 255)
        back = y[o, g, :, l]
        ys[q, g, :, s] += back
        x[q, g, :, s] = (x[q, g, :, s] + np.clip(back[:, :4] - 128, -8, 8)) & 255
    yc = np.sum(C * (np.arange(16) + 1)[:, None], axis=2)
    return {"yc": yc.astype(np.float32), "yf": F.reshape(N, 128, FC).astype(np.float32).astype(BF), "ys": ys.reshape(N, 128, S).astype(np.float32), "yx": x.reshape(N, 32, S).astype(np.float32)}

@@ -1,0 +1,891 @@
+import numpy as np
+from concourse.bass import DstId, RemoteDMATransfer
+from concourse.mybir import AluOpType as A
+from concourse.mybir import ActivationFunctionType as AF
+
+RO, NS, NL, WC = 4, 192, 256, 4096
+TW = 4144
+OFFS = (0, 53, 211, 264)
+CB01 = (0, 97, 133, 230)
+BETA = 0.916
+OPT = dict(
+    f_act=(1, 3, 5, 7),
+    u_act=(0, 1, 2, 3, 4, 5, 6, 7), mn_act=True,
+    m_split=48,
+    inorder=False, hold=0.4, ft_act=2,
+    seed=0, noise=0.0)
+LEVEL = {'f2nd': 32.0, 'v': -60.3, 'g2': 72.3, 'rest': 12.6, 'w': 7.8, 'of': -8.7, 'wab': 8.0, 'f': 30, 't0': 13.0, 't1': 10.6, 'kc': 8.7,
+         'home': 4.8, 'ou': 111.0, 'g0': 7.6, 'g1': 65.9, 'ug0': 66.3, 'ug1': 115.4, 'um0': 306.6, 'um1': -34.4, 'u': 297.7, 'keys': 34.7,
+         'e': 32.8, 'ms': 110.9, 'fn': 37.3, 'fs': 56.9, 'cs': 23.4, 'f2': 34.5, 'end': 181.5, 'cold': 135.7, 'fold': 128.2, 'cn': 18.7,
+         'scan': -100, 'cm': -31.1, 'ft': -35, 'r0': -74.1, 'keysL': -20, 'eL': 10.1, 'foldL': -100, 'kcL': 0, 'um0L': 0, 'um1L': 0,
+         'ug0L': 0, 'ug1L': 0, 'coldL': -29.8, 'uL': 0}
+SHIFT = {'f.1': 200, 'home.9': 5, 'um1.5': 100, 'fs.7': 200, 'r0.11': 200, 'um1.1': -200, 'keys.14': 40, 'r0.7': -100, 'scan.12': 40,
+         'scan.2': -200, 'e.6': 100, 'r0.1': -100, 'w.4': -15, 'e.3': 200, 'cs.4': 100, 'keys.13': 100, 'home.3': 15, 'u.1': 100}
+
+SCRATCH = {}
+PART = {}
+
+
+def _s(dt, cols, *names):
+    for n in names:
+        SCRATCH[n] = ("sbuf", [128, cols], dt)
+
+
+def _p(dt, cols, whole, *names):
+    _s(dt, cols * len(names), whole)
+    for i, n in enumerate(names):
+        PART[n] = (whole, cols * i, cols)
+
+
+_s("bfloat16", TW, "Ct", "Ft", "Ms", "F2")
+_s("float32", 4096, "K")
+_s("int32", 144, "DI", "C4")
+_s("int32", 128, "C16", "C8")
+_s("int32", 16, "ic", "J")
+_s("int32", 32, "L0", "dmi")
+_s("float32", 144, "DG", "Bt32")
+_s("float32", 64, "col")
+_s("float32", 16, "OH", "LT", "OH2", "OH4", "OHs")
+_p("bfloat16", 144, "wide", "Big", "Big4", "Bd", "Bt", "BJ", "BP", "BY", "H1", "H2", "H3", "H4", "H5", "H6", "HD", "W1", "W2", "W3", "W4")
+_p("bfloat16", 128, "tiles", "I", "BO", "BO45", "BO128", "NS4", "ST", "TT", "YW", "I256", "N256", "t1", "t2", "t3", "t4", "t5", "t6")
+_s("float16", 128, "I16")
+_s("float16", 256, "CBt")
+_s("float32", 128, "I32")
+_s("bfloat16", 2048, "TR", "Sel")
+_s("float32", 512, "Sel32", "krow")
+_s("bfloat16", 512, "D0", "V", "Mt")
+_s("bfloat16", 256, "CA", "CL", "CO", "cy", "c128", "fa", "fb", "Wp", "gs", "MsG", "MsM", "Cold", "Fold", "Cnew", "Fnew", "us", "wexp",
+   "oh", "Mnew", "mt", "cb", "hb")
+_s("bfloat16", NS, "CAP", "tb", "X0b", "Hh", "cum", "P")
+_s("bfloat16", 4 * NS, "Yg", "Sg", "Yb")
+_s("int32", NS, "X0", "Sa", "Si")
+_s("float32", NS, "Tf", "Sf", "yso", "yxo")
+_s("float32", 16 * NS, "Zs")
+_s("float32", 4 * NL, "Zr", "SW")
+_s("bfloat16", 4 * NL, "Ys", "G", "Wcd", "Wab", "g4", "E")
+_s("uint16", 64, "dst", "om", "EL")
+_s("uint16", 256, "of", "ou")
+_s("uint16", 32, "kc16", "so")
+_s("float32", 256, "PA", "pr", "yco")
+_s("int32", 256, "vi", "hm", "ki", "mi")
+_s("float32", 64, "ks")
+_s("bfloat16", 64, "kb")
+_s("float32", 40, "kc")
+_s("float32", 32, "dum", "x1", "x2")
+_s("bfloat16", 4096, "Vg", "Ug", "Up")
+_s("float16", 4096, "Vp")
+for _i in range(8):
+    if _i == 3:
+        SCRATCH["pw"] = ("psum", [128, 1024], "float32")
+    elif _i != 4:
+        SCRATCH["ps%d" % _i] = ("psum", [128, 512], "float32")
+
+NDMA = 24
+SEMAPHORES = ["dve", "act", "pe", "pool", "sent"] + ["fw%d" % r for r in range(RO)] + ["bk%d" % r for r in range(RO)] + [
+    "d%d" % i for i in range(NDMA)]
+TWO = {"bfloat16", "float16", "uint16"}
+GUESS = dict(cyc=1.0, fv=45, fa=90, gat=1.6, sca=3.9, pe=0.6, hop=130, same=70, rem=3600, dma=1.0, tt2=1.0)
+
+
+def build(g, T, topo, core):
+    me = T.rank_of(core)
+    N = len(T.cores)
+    ops = []
+    ndma = [0]
+    level = [None]
+    seen = {}
+    FA, UA, MS = OPT["f_act"], OPT["u_act"], OPT["m_split"]
+
+    def R(name, c0=0, c1=None, st=1, key=None):
+        buf, o, w = PART.get(name) or (name, 0, SCRATCH[name][1][1])
+        if c1 is None:
+            c1 = w
+        ap = T[buf][:, o + c0:o + c1:st] if st > 1 else T[buf][:, o + c0:o + c1]
+        return dict(ap=ap, key=key or name, c0=c0, c1=c1, n=len(range(c0, c1, st)), dt=SCRATCH[buf][2], ps=SCRATCH[buf][0] == "psum")
+
+    def X(key):
+        return dict(key=key, c0=0, c1=1, ps=False)
+
+    def IND(win, off):
+        return dict(ap=win["ap"].indirect(off["ap"]), n=16 * off["n"], ind=(win, off), dt=win["dt"], ps=False)
+
+    def parts(v):
+        if not isinstance(v, dict):
+            return []
+        if "ind" in v:
+            return list(v["ind"])
+        if v["key"] == "pw":
+            return [dict(v, key="pw%d" % b) for b in range(v["c0"] // 512, (v["c1"] - 1) // 512 + 1)]
+        return [v]
+
+    def ap(v):
+        return v["ap"] if isinstance(v, dict) else v
+
+    def add(eng, fn, out, ins, size, more=(), sem=None, lat=None):
+        rd = []
+        for v in ins:
+            rd += parts(v)
+        wr = []
+        for o in out:
+            if "ind" in o:
+                wr.append(o["ind"][0])
+                rd.append(o["ind"][1])
+            else:
+                wr += parts(o)
+        seen[level[0]] = seen.get(level[0], 0) + 1
+        tag = level[0] and "%s.%d" % (level[0][1], seen[level[0]])
+        ops.append(dict(eng=eng, fn=fn, rd=rd + list(more), wr=wr, size=size, sem=sem, lat=lat, after=[], lv=level[0], tag=tag))
+        return ops[-1]
+
+    def lv(r, name):
+        level[0] = (r, name)
+
+    def vsize(out, ins, two=False):
+        if "ind" in out:
+            return ("sca", out["n"])
+        if any("ind" in v for v in ins):
+            return ("gat", out["n"])
+        half = all(v["dt"] in TWO for v in [out] + ins)
+        if two and not any(v["ps"] for v in ins):
+            return ("tt2", out["n"]) if half else ("el", 2 * out["n"])
+        return ("el", out["n"] // 2 if half else out["n"])
+
+    def ts(out, a, s1, o1, s2=None, o2=None, more=()):
+        if o2 is None:
+            fn = lambda: g.vector.tensor_scalar(out["ap"], a["ap"], ap(s1), None, o1)
+        else:
+            fn = lambda: g.vector.tensor_scalar(out["ap"], a["ap"], ap(s1), ap(s2), o1, o2)
+        add("dve", fn, [out], [a, s1, s2], vsize(out, [a]), more)
+
+    def tt(out, a, b, op, more=()):
+        add("dve", lambda: g.vector.tensor_tensor(out["ap"], a["ap"], b["ap"], op), [out], [a, b], vsize(out, [a, b], True), more)
+
+    def cp(out, a, more=()):
+        add("dve", lambda: g.vector.tensor_copy(out["ap"], a["ap"]), [out], [a], vsize(out, [a]), more)
+
+    def ms(out, v):
+        add("dve", lambda: g.vector.memset(out["ap"], v), [out], [], vsize(out, []))
+
+    def scan(out, d0, d1, init, o0, o1):
+        add("dve", lambda: g.vector.tensor_tensor_scan(out["ap"], d0["ap"], d1["ap"], ap(init), o0, o1), [out], [d0, d1, init],
+            vsize(out, [d0, d1]))
+
+    def act(out, a, f, bias=None, scale=None, more=()):
+        kw = {}
+        if bias is not None:
+            kw["bias"] = ap(bias)
+        if scale is not None:
+            kw["scale"] = ap(scale)
+        add("act", lambda: g.scalar.activation(out["ap"], a["ap"], f, **kw), [out], [a, bias, scale],
+            ("gat" if "ind" in a else "el", out["n"]), more)
+
+    def af(out, a, scale=None, bias=None):
+        act(out, a, AF.Identity, bias=bias, scale=scale)
+
+    def mm(items, start=True, stop=True, more=(), each=False):
+        def fn():
+            ins = None
+            for i, (o, l, r) in enumerate(items):
+                ins = g.tensor.matmul(o["ap"], l["ap"], r["ap"], each or (start and i == 0), each or (stop and i == len(items) - 1))
+            return ins
+        c = sum(max(64, r["n"]) * (4 if r["dt"] == "float32" else 1) for o, l, r in items)
+        rd = []
+        for o, l, r in items:
+            rd += [l, r]
+        add("pe", fn, [o for o, l, r in items], rd, ("mm", c), more)
+
+    def iota(out, pat, base, cm):
+        if out["dt"] == "int32":
+            fn = lambda: g.iota(out["ap"], pat, base, cm)
+        else:
+            fn = lambda: g.iota(out["ap"], pat, base, cm, allow_small_or_imprecise_dtypes=True)
+        return add("pool", fn, [out], [], ("iota", out["n"]))
+
+    def fill(out, v):
+        return iota(out, [[0, out["n"]]], v, 0)
+
+    def dma(q, pairs, wr, rd, lat, acc=False):
+        sem = "d%d" % ndma[0]
+        ndma[0] += 1
+
+        def fn():
+            for o, i in pairs:
+                if acc:
+                    g.dma_start(o, i, accum_op=A.add).then_inc(T.sem[sem], 16)
+                else:
+                    (g.sync if q == "sp" else g.scalar).dma_start(o, i).then_inc(T.sem[sem], 16)
+        return add(q, fn, wr, rd, ("fix", (800 if acc else 60) * len(pairs)), sem=(sem, 16 * len(pairs)), lat=("dma", lat))
+
+    def exchange(sem, src, dst, key, rd, peers):
+        eng = topo.engines(core, T.cores[peers[0]])
+        half = len(eng) // 2
+        m0 = sum(1 << e for e in eng[:half])
+        m1 = sum(1 << e for e in eng[half:])
+        far = [o for o in peers if o // 2 != me // 2]
+        near = [o for o in peers if o // 2 == me // 2]
+
+        def fn():
+            tr = []
+            for o, m in zip(far, (m0, m1)):
+                rid, pid, _e = topo.addr(T.cores[o])
+                tr.append(RemoteDMATransfer(dst_ids=[DstId(rid=rid, pnc=pid)], dma_engine_mask=m, remote_sem=T.sem[sem],
+                                            src=src(o), dst=dst))
+            if tr:
+                g.remote_dma_fused(tr, local_sem=T.sem["sent"])
+            for o in near:
+                rid, pid, _e = topo.addr(T.cores[o])
+                g.remote_dma(dst, src(o), T.sem[sem], T.sem["sent"], pid, rid, m0 | m1)
+        calls = len(far) // 2 + len(near)
+        op = add("pool", fn, [X(key)], rd, ("fix", 200 * calls), sem=(sem, 2 * len(eng)), lat=("rem", 0.55 + 0.15 * len(peers)))
+        op["sent"] = calls * len(eng)
+        return op
+
+    def C(i):
+        return R("col", i, i + 1)
+
+    def O(i, name="OH"):
+        return R(name, i, i + 1)
+
+    def ic(i):
+        return R("ic", i, i + 1)
+
+    def win(name, s):
+        return R(name, s, s + 128)
+
+    def EX(rho, name="Big"):
+        return win(name, 15 - rho)
+
+    def ps(b, c0, c1, st=1):
+        if b in (3, 4):
+            return R("pw", 512 * (b - 3) + c0, 512 * (b - 3) + c1, st)
+        return R("ps%d" % b, c0, c1, st)
+
+    def SEL(i):
+        return R("Sel", 128 * i, 128 * i + 128)
+
+    I = R("I")
+    add("dve", lambda: g.vector.memset(T.X0[:], 0), [X("X0z")], [], ("el", NS))
+    prev = None
+    for k in range(4):
+        op = dma("sp", [(T.Ct[:, 1024 * k:1024 * k + 1024], T.cf[:, 1024 * k:1024 * k + 1024])], [R("Ct", 1024 * k, 1024 * k + 1024)], [],
+                 2600 + 1100 * k)
+        op["after"] = [prev] if prev else []
+        prev = op
+    dma("act", [(T.tb[:], T.tg[:])], [R("tb")], [], 2200)
+    dma("act", [(T.X0[e::16, :], T.x0[e::4, :]) for e in range(4)], [R("X0")], [X("X0z")], 2200)
+    for k in range(2):
+        op = dma("sp", [(T.Ft[:, 2048 * k:2048 * k + 2048], T.ft[:, 2048 * k:2048 * k + 2048])], [R("Ft", 2048 * k, 2048 * k + 2048)], [],
+                 8000 + 2200 * k)
+        op["after"] = [prev]
+        prev = op
+    iota(ic(0), [[0, 1]], 0, 1)
+    iota(R("J"), [[1, 16]], 0, 0)
+    iota(R("DI"), [[1, 144]], 0, -1)
+    iota(R("C8"), [[1, 16], [0, 8]], 0, 0)
+    iota(R("C4"), [[1, 36], [0, 4]], 0, 0)
+    iota(R("C16"), [[1, 8], [0, 16]], 0, 0)
+    iota(R("L0"), [[0, 4], [16, 2], [4, 4]], 0, 0)
+    iota(R("dmi"), [[0, 16], [16, 2]], 4112, 0)
+    ts(ic(1), ic(0), 15, A.bitwise_and)
+    cp(C(0), ic(1))
+    ts(R("OH"), R("J"), C(0), A.is_equal)
+    ts(R("LT"), R("J"), C(0), A.is_gt)
+    ts(R("DG"), R("DI"), C(0), A.add)
+    ts(ic(2), ic(0), 4, A.arith_shift_right)
+    cp(C(1), ic(2))
+    af(C(2), C(1), 2.0, 1.0)
+    af(C(3), C(1), 4.0, 3.0)
+    ts(ic(3), ic(0), 3, A.bitwise_and)
+    cp(C(4), ic(3))
+    LT4, LT8, LT12 = O(4, "LT"), O(8, "LT"), O(12, "LT")
+    af(C(5), LT4, -1.0, LT8)
+    af(C(6), LT8, -1.0, LT12)
+    af(C(7), LT8, -16385.0, 16384.0)
+    af(C(8), LT12, -192.0, 192.0)
+    af(C(9), C(8), C(4))
+    af(C(10), C(6), -1.0, C(9))
+    af(C(11), C(6), 1024.0, C(9))
+    af(C(12), LT8, 16384.0, -16384.0)
+    af(C(13), C(12), C(4))
+    af(C(14), C(5), 129024.0, 2048.0)
+    af(C(15), C(14), -1.0)
+    af(C(16), O(8), 32768.0)
+    af(C(17), LT4, 64.0)
+    DI = R("DI", 0, 128)
+    ts(I, DI, 0.0, A.is_equal)
+    ts(R("Big"), R("DG"), 15.0, A.is_equal)
+    ts(R("t1"), DI, 0.0, A.is_equal, LT4, A.mult)
+    ts(R("t2"), DI, 4.0, A.is_equal, C(17), A.mult)
+    ts(R("t3"), R("C8"), C(2), A.is_equal, O(0), A.mult)
+    tt(R("t1"), R("t1"), R("t2"), A.add)
+    tt(R("ST"), R("t1"), R("t3"), A.add)
+    af(R("CAP"), R("tb"), 0.0, C(11))
+    af(R("Tf"), R("tb"), None, C(16))
+    ms(R("D0"), 0.0625)
+    ms(R("D0", 0, 512, 16), -1024.0)
+    fill(R("Yb"), 0)
+    for o in range(N):
+        fill(R("Zs", 192 * o, 192 * o + 64), 0)
+    ms(R("Ms", 0, 1024), 0.0)
+    ms(R("Ms", 1024, 2048), 0.0)
+    fill(R("Ms", 2048, 3072), 0)
+    fill(R("Ms", 3072, TW), 0)
+    ms(R("Ct", WC, TW), 0.0)
+    ms(R("Ft", WC, TW), 0.0)
+    ts(R("Big4"), R("C4"), C(3), A.is_equal)
+    af(C(18), O(3), 844.0)
+    af(C(19), O(2), 212.0, C(18))
+    af(C(20), O(1), 2128.0)
+    af(C(21), O(0), 1552.0, C(20))
+    af(C(22), O(12), 128.0)
+    af(C(23), O(8), -128.0, C(22))
+    af(R("OH2"), R("OH"), 2.0)
+    af(R("OH4"), R("OH"), 4.0)
+    af(R("OHs"), R("OH"), 0.0625)
+    B4 = R("Big4")
+    for name, c in (("H1", O(0)), ("H2", O(1, "OH2")), ("H3", C(19)), ("H4", O(2, "OH4")), ("H5", O(3, "OH2")), ("H6", C(21)),
+                    ("HD", C(23)), ("W1", O(6, "OHs")), ("W2", O(4, "OHs")), ("W3", O(7, "OHs")), ("W4", O(5, "OHs"))):
+        af(R(name), B4, c)
+    ts(ic(4), ic(0), 1, A.bitwise_and)
+    ts(ic(5), ic(0), 1, A.arith_shift_right, 1, A.bitwise_and)
+    ts(C(24), ic(4), 2.0, A.mult, -1.0, A.add)
+    ts(C(26), ic(5), 2.0, A.mult, -1.0, A.add)
+    af(C(25), C(24), -12.0, 2.0)
+    af(C(27), C(26), -12.0, 2.0)
+    af(C(28), C(24), 0.5, -159.5)
+    af(C(29), C(24), 2.0, -638.0)
+    af(C(30), C(26), None, -318.0)
+    z64 = R("Big", 0, 64)
+    fill(R("CA", 64, 128), -160)
+    af(R("CA", 128, 192), z64, 0.0, C(29))
+    fill(R("CA", 192, 256), -640)
+    for h in range(2):
+        ts(R("CBt", 128 * h, 128 * h + 64), z64, 0.0, A.mult, C(30), A.add)
+        ts(R("CBt", 128 * h + 64, 128 * h + 128), z64, 0.0, A.mult, -319.0, A.add)
+    fill(R("CL", 0, 128), -5120)
+    fill(R("CL", 128, 256), 1024)
+    for k in range(4):
+        fill(R("CO", 64 * k, 64 * k + 64), 16 * CB01[k])
+    af(R("cy"), R("CL"), 0.0, -127.5)
+    ts(R("Bd"), R("DI"), 12.0, A.is_equal, LT4, A.mult)
+    af(C(31), C(0), 0.25, 12.0)
+    ts(R("Bt"), R("DG"), C(31), A.is_equal)
+    af(R("Bt32"), R("Bt"))
+    ts(R("BO"), R("C16"), C(1), A.is_equal)
+    BO = R("BO")
+    for r in (0, 1, 2, 3, 4, 5, 6, 7, 8, 12):
+        af(SEL(r), BO, O(r))
+    for l in range(4):
+        af(R("Sel32", 128 * l, 128 * l + 128), BO, O(4 * l))
+    cp(R("I16"), I)
+    af(R("I32"), I)
+    af(R("I256"), I, 1.0 / 256)
+    af(R("N256"), I, -1.0 / 256)
+    af(C(32), C(5), -16.0)
+    af(C(33), O(4), -16.0)
+    ts(R("t4"), DI, -4.0, A.is_equal, C(32), A.mult)
+    ts(R("t5"), R("C8"), C(2), A.is_equal, C(33), A.mult)
+    tt(R("t4"), R("t4"), R("t5"), A.add)
+    af(R("t6"), I, -1024.0)
+    tt(R("TT"), R("t6"), R("t4"), A.add)
+    af(C(34), C(5), -2560.0, 163840.0 + 2560.0 - 128.0)
+    for rho in range(16):
+        ts(R("TR", 128 * rho, 128 * rho + 128), EX(rho), O(rho, "LT"), A.mult)
+    af(R("t2"), BO, 0.45)
+    tt(R("BO45"), R("t2"), I, A.subtract)
+    af(C(41), O(0), 60.0)
+    af(C(42), C(0), -0.5)
+    af(R("BO128"), BO, 128.0)
+    af(R("NS4"), SEL(4), -1.0)
+    af(C(40), C(6), -64.0)
+    af(R("YW"), BO, C(40))
+    af(R("BJ"), R("Big"), C(42))
+    af(R("BP"), R("Big"), O(4))
+    af(C(35), C(0), None, 1.0)
+    af(R("BY"), R("Big"), C(35))
+    af(C(36), C(0), -BETA)
+    ts(ic(6), ic(1), 2, A.arith_shift_right)
+    cp(C(37), ic(6))
+    ts(ic(7), ic(6), 1, A.bitwise_and)
+    cp(C(38), ic(7))
+    af(C(39), C(38), -33.0, 32.0)
+    ts(R("x1"), R("L0"), C(37), A.add)
+    cp(R("EL", 0, 32), R("x1"))
+    ts(R("EL", 32, 64), R("x1"), C(38), A.mult, C(39), A.add)
+    ts(R("dum"), R("dmi"), C(0), A.add, 1.0 / 8192, A.mult)
+    fill(R("kc", 32, 40), -1)
+
+    MSK = [X("Ms%d" % x) for x in range(5)]
+
+    def shift():
+        pairs = [(T.Ms[x::16, 0:WC - OFFS[x]], T.Ms[0::16, OFFS[x]:WC]) for x in (1, 2, 3)]
+        pairs += [(T.Ms[x::16, WC - OFFS[x]:WC], T.Ms[0::16, 0:OFFS[x]]) for x in (1, 2, 3)]
+        dma("sp", pairs, MSK[1:4], [MSK[0], R("Ms")], 2800)
+
+    lv(0, "scan")
+    for b in range(8):
+        bank = 3 + b % 4
+        mm([(ps(bank, 128 * c, 128 * c + 128), R("Ct", 512 * b + 128 * c, 512 * b + 128 * c + 128), I) for c in range(4)], each=True)
+        scan(R("K", 512 * b, 512 * b + 512), R("D0"), ps(bank, 0, 512), 0.0, A.add, A.max)
+    for q in range(8):
+        ts(R("ki", 32 * q, 32 * q + 32), R("K", 16 * q + 15, 4096, 128), 16.0, A.mult)
+    ts(R("mi"), R("ki"), 15, A.bitwise_and)
+    ts(R("mt"), R("mi"), -1.0, A.mult, 15.0, A.add)
+    mm([(ps(3, 128 * h, 128 * h + 128), R("mt", 128 * h, 128 * h + 128), I) for h in range(2)], each=True)
+    act(R("Mt", 0, 256), ps(3, 0, 256), AF.Copy)
+    dma("act", [(T.Ms[64 * h:64 * h + 64:16, 0:WC], T.Mt[:, 128 * h:128 * h + 128]) for h in range(2)], [MSK[0]],
+        [R("Mt", 0, 256), R("Ms")], 2200)
+    shift()
+    lv(0, "cm")
+    ts(R("cb"), R("ki"), 0.0625, A.mult)
+    mm([(ps(4, 128 * h, 128 * h + 128), R("cb", 128 * h, 128 * h + 128), I) for h in range(2)], each=True)
+    act(R("Mt", 256, 512), ps(4, 0, 256), AF.Copy)
+    dma("act", [(T.Ms[64 * h + 4:64 * h + 64:16, 0:WC], T.Mt[:, 256 + 128 * h:384 + 128 * h]) for h in range(2)], [MSK[4]],
+        [R("Mt", 256, 512), R("Ms")], 2200)
+    lv(0, "ft")
+    for k in range(4):
+        o = R("Ft", 1024 * k, 1024 * k + 1024)
+        if k < OPT["ft_act"]:
+            af(o, o, None, -128.0)
+        else:
+            ts(o, o, -128.0, A.add)
+    lv(0, "r0")
+
+    def route(r):
+        ts(R("Si"), R("Sa"), 65280, A.bitwise_and)
+        cp(R("Sf"), R("Si"))
+        if r == RO:
+            return None
+        ts(R("Hh"), R("Si"), C(7), A.is_lt)
+        scan(R("cum"), R("Hh"), R("CAP"), C(10), A.add, A.min)
+        tt(R("P"), R("Hh"), R("cum"), A.mult)
+        mm([(ps(7, 448, 460), EX(rho), R("P", rho, NS, 16)) for rho in range(16)])
+        d = R("dst", 16 * r, 16 * r + 12)
+        cp(d, ps(7, 448, 460))
+        act(R("Sg", NS * r, NS * r + NS), R("P"), AF.Sign, bias=-63.5)
+        w = R("Zs", 768 * r, 768 * r + 768)
+        tt(IND(w, d), R("Tf"), R("Sf"), A.add)
+        b = 768 * r
+        op = exchange("fw%d" % r, lambda o: T.Zs[:, b + 192 * o:b + 192 * o + 64], T.Zr[:, NL * r + 64 * me:NL * r + 64 * me + 64],
+                      "Zin%d" % r, [w] + ([R("Yb")] if r == 0 else []), [o for o in range(N) if o != me])
+        act(R("Zr", NL * r + 64 * me, NL * r + 64 * me + 64), R("Zs", b + 192 * me, b + 192 * me + 64), AF.Copy)
+        return op
+
+    ts(R("X0b"), R("X0"), 256.0, A.mult)
+    mm([(ps(7, 0, NS), R("ST"), R("X0b"))])
+    ts(R("Sa"), ps(7, 0, NS), C(13), A.add)
+    first = route(0)
+    level[0] = None
+    for r in range(1, RO):
+        for o in range(N):
+            fill(R("Zs", 768 * r + 192 * o, 768 * r + 192 * o + 64), 0)["after"] = [first]
+    fill(R("c128"), 128)["after"] = [first]
+    for k in range(4):
+        fill(R("F2", 1036 * k, 1036 * k + 1036), 128)["after"] = [first]
+
+    for r in range(RO):
+        last = r == RO - 1
+        Z = R("Zr", NL * r, NL * r + NL)
+        zin = [X("Zin%d" % r)]
+        Vb = R("V", 0, 256)
+        lv(r, "v")
+        act(Vb, Z, AF.Identity, bias=159.5005, scale=1.0 / 1024, more=zin)
+        act(R("V", 256, 512), Z, AF.Identity, bias=159.7505, scale=1.0 / 1024, more=zin)
+
+        def sel(o, nm, c0, c1):
+            return [(o, win(nm, 12 - 4 * l), R("V", c0 + l, c1, 4)) for l in range(4)]
+        mm(sel(ps(0, 0, 64), "H1", 0, 256))
+        mm([(ps(1, 0, 64), R("I16"), R("CBt", 0, 64))] + sel(ps(1, 0, 64), "H2", 0, 256))
+        mm([(ps(1, 64, 128), I, R("CL", 0, 64))] + sel(ps(1, 64, 128), "H3", 0, 256))
+        ts(R("PA", 0, 64), ps(0, 0, 64), C(28), A.add)
+        tt(R("pr", 0, 64), R("PA", 0, 64), ps(1, 0, 64), A.mult)
+        tt(R("vi", 0, 64), R("pr", 0, 64), ps(1, 64, 128), A.add)
+        ts(R("hm", 0, 64), R("vi", 0, 64), 2, A.arith_shift_right, 4095, A.bitwise_and)
+        cp(R("om"), R("hm", 0, 64))
+        Mw = R("Ms")
+        act(R("G", 0, 16 * MS), IND(Mw, R("om", 0, MS)), AF.Copy, more=MSK)
+        lv(r, "g2")
+        if MS < 64:
+            cp(R("G", 16 * MS, 1024), IND(Mw, R("om", MS, 64)), more=MSK)
+        lv(r, "rest")
+        mm([(ps(2, 64, 256), I, R("CA", 64, 256))] + sel(ps(2, 64, 128), "H1", 256, 512) + sel(ps(2, 128, 256), "H4", 0, 512))
+        act(R("PA", 64, 256), ps(2, 64, 256), AF.Copy)
+        mm([(ps(5, 64, 256), R("I16"), R("CBt", 64, 256))] + sel(ps(5, 64, 128), "H2", 256, 512) + sel(ps(5, 128, 256), "H5", 0, 512))
+        mm([(ps(5, 320, 512), I, R("CL", 64, 256))] + sel(ps(5, 320, 384), "H3", 256, 512) + sel(ps(5, 384, 512), "H6", 0, 512))
+        mm(sel(ps(2, 256, 320), "HD", 0, 256))
+        tt(R("pr", 64, 256), R("PA", 64, 256), ps(5, 64, 256), A.mult)
+        tt(R("vi", 64, 256), R("pr", 64, 256), ps(5, 320, 512), A.add)
+        ts(R("hm", 128, 256), R("vi", 128, 256), 4080, A.bitwise_and)
+        ts(R("hm", 64, 128), R("vi", 64, 128), 2, A.arith_shift_right, 4095, A.bitwise_and)
+        cp(R("hb", 0, 64), R("hm", 128, 192))
+        for k in range(1, 4):
+            ts(R("hb", 64 * k, 64 * k + 64), R("hm", 128, 192), 4096.0 - 16 * CB01[k], A.is_ge, -4096.0, A.mult)
+        tt(R("ks"), R("hm", 64, 128), ps(2, 256, 320), A.add)
+        tt(R("kb"), R("hm", 192, 256), ps(2, 256, 320), A.add)
+        lv(r, "ou")
+        for k in range(4):
+            ts(R("ou", 64 * k, 64 * k + 64), R("hm", 192, 256), C(4), A.add, 4.0 * k, A.add)
+        lv(r, "w")
+        mm([(ps(6, 0, 256), win("W1", 12), Vb), (ps(6, 0, 256), win("W2", 8), Vb)])
+        mm([(ps(6, 256, 512), win("W3", 12), Vb), (ps(6, 256, 512), win("W4", 8), Vb)])
+        af(R("fa"), ps(6, 0, 256), C(24), C(25))
+        af(R("fb"), ps(6, 256, 512), C(26), C(27))
+        tt(R("Wp"), R("fa"), R("fb"), A.mult)
+        pW = R("pw")
+        for h in range(2):
+            mm([(ps(3 + h, x, 512, 4), SEL(x), R("Wp", 128 * h, 128 * h + 128)) for x in range(4)], each=True)
+        for n2, h in enumerate((1 - me // 2, me // 2)):
+            if any(4 * n2 + k not in FA for k in range(4)):
+                act(R("Wcd", 512 * h, 512 * h + 512), ps(3 + h, 0, 512), AF.Copy)
+        lv(r, "wab")
+        for h in range(2):
+            mm([(ps(h, 256 * k, 256 * k + 256), SEL(4 + 2 * h + k), R("Wp")) for k in range(2)], each=True)
+            act(R("Wab", 512 * h, 512 * h + 512), ps(h, 0, 512), AF.Copy)
+        lv(r, "kc")
+        mm([(ps(1, 0, 16), win("Bt32", 12 - 4 * a), R("ks", a, 64, 4)) for a in range(4)])
+        ts(R("kc16", 0, 16), ps(1, 0, 16), 4096.0, A.add)
+        ts(R("kc", 0, 16), ps(1, 0, 16), 4096.0, A.add, 1.0 / 8192, A.mult)
+        lv(r, "of")
+        mm([(ps(2, 0, 256), I, R("CO")), (ps(2, 64, 256), I, R("hb", 64, 256))]
+           + [(ps(2, 64 * k, 64 * k + 64), I, R("hb", 0, 64)) for k in range(4)], stop=False)
+        mm([(ps(2, 64 * k, 64 * k + 64), win("Bd", 12 - 4 * l), R("G", 4 * l + k, 1024, 16)) for k in range(4) for l in range(4)],
+           start=False)
+        cp(R("of"), ps(2, 0, 256))
+        Fw = R("Ft")
+        lv(r, "keys")
+        act(R("MsG"), IND(Mw, R("kc16", 0, 16)), AF.Copy, more=MSK)
+        af(R("MsM"), R("MsG"), O(0))
+        lv(r, "cold")
+        act(R("Cold"), IND(R("Ct"), R("kc16", 0, 16)), AF.Copy)
+        lv(r, "keys")
+        for l in range(4):
+            mm([(ps(0, 128 * l, 128 * l + 64), R("Sel32", 128 * l, 128 * l + 128), R("ks"))])
+            o = ps(0, 128 * l + 64, 128 * l + 128)
+            mm([(o, SEL(4 * l), R("kb")), (o, SEL(0), R("MsG", l, 256, 4))])
+        act(R("krow"), ps(0, 0, 512), AF.Identity, bias=0.5, scale=1.0 / 8192)
+        o = ps(1, 16, 32)
+        mm([(o, win("Bt", 12 - 4 * a), R("kb", a, 64, 4)) for a in range(4)] + [(o, EX(rho), R("MsM", rho, 256, 16)) for rho in range(16)])
+        ts(R("kc16", 16, 32), o, 4096.0, A.add)
+        ts(R("kc", 16, 32), o, 4096.0, A.add, 1.0 / 8192, A.mult)
+        lv(r, "fold")
+        act(R("Fold"), IND(Fw, R("kc16", 16, 32)), AF.Copy)
+        if last:
+            dma("pool", [(T.F2[:, 2048 * h:2048 * h + 2048], T.Ft[:, 2048 * h:2048 * h + 2048]) for h in range(2)], [R("F2")],
+                [R("Ft"), R("of")], 6000, acc=True)
+        lv(r, "e")
+        for h in range(2):
+            tt(R("E", 512 * h, 512 * h + 512), IND(R("kc"), R("EL", 32 * h, 32 * h + 32)), R("krow"), A.is_equal)
+        o = ps(1, 32, 64)
+        it = []
+        for rho in range(16):
+            s = 128 * (rho % 4) + rho // 4
+            it.append((o, R("TR", 128 * rho, 128 * rho + 128), R("E", s, s - rho // 4 + 128, 4)))
+        mm(it, stop=False)
+        it = []
+        for rho in range(16):
+            s = 128 * (rho % 4) + rho // 4
+            it.append((o, EX(rho), R("E", 512 + s, 512 + s - rho // 4 + 128, 4)))
+        mm(it, start=False)
+        tt(R("x1"), o, R("kc", 0, 32), A.add)
+        tt(R("x2"), R("x1"), R("dum"), A.min)
+        ts(R("so"), R("x2"), 8192.0, A.mult)
+        lv(r, "f")
+        yb = NL * r
+        Y = R("Ys", yb, yb + NL)
+        for n2, h in enumerate((1 - me // 2, me // 2)):
+            pY = ps(2, 256 + 128 * h, 384 + 128 * h)
+            lv(r, "f2nd" if n2 else "f")
+            mm([(pY, I, R("cy", 0, 128))], stop=False)
+            for k in range(4):
+                lst = R("of", 64 * k + 32 * h, 64 * k + 32 * h + 32)
+                b = 1024 * k + 512 * h
+                pS = ps(5 + k % 2, 128 * n2, 128 * n2 + 128)
+                if 4 * n2 + k in FA:
+                    act(R("Vg", b, b + 512), IND(Fw, lst), AF.Copy)
+                    tt(R("Vp", b, b + 512), R("Vg", b, b + 512), ps(3 + h, 0, 512), A.mult)
+                else:
+                    tt(R("Vp", b, b + 512), IND(Fw, lst), R("Wcd", 512 * h, 512 * h + 512), A.mult)
+                mm([(pS, R("I16"), R("Vp", b + x, b + 512, 4)) for x in range(4)])
+                c = 256 * k + 128 * h
+                tt(R("SW", c, c + 128), pS, R("Wab", c, c + 128), A.mult)
+                mm([(pY, R("I32"), R("SW", c, c + 128))], start=False, stop=k == 3)
+            Yh = R("Ys", yb + 128 * h, yb + 128 * h + 128)
+            ts(Yh, pY, 3221225472.0, A.add, -3221225472.0, A.add)
+            exchange("bk%d" % r, lambda o, yb=yb: T.Ys[:, yb + 64 * o:yb + 64 * o + 64], T.Yb[:, 192 * me:192 * me + 64],
+                     "Yin%d%d" % (r, n2), [Yh], [o for o in (2 * h, 2 * h + 1) if o != me])
+            c = 128 * h
+            pD = ps(7, c, c + 128)
+            lv(r, "t%d" % n2)
+            mm([(pD, R("I32"), R("Zr", NL * r + c, NL * r + c + 128)), (pD, R("TT"), R("V", c, c + 128))], stop=False, more=zin)
+            lv(r, "g%d" % n2)
+            mm([(pD, R("N256"), Yh)], start=False)
+            act(R("gs", c, c + 128), pD, AF.Sign, bias=C(34))
+            mm([(ps(3 + h, x, 512, 4), I, R("gs", c, c + 128)) for x in range(4)], each=True)
+            if any(4 * n2 + k not in UA for k in range(4)):
+                act(R("g4", 512 * h, 512 * h + 512), ps(3 + h, 0, 512), AF.Copy)
+            pU = ps(0, c, c + 128)
+            lv(r, "um%d" % n2)
+            mm([(pU, R("BO128"), R("gs", c, c + 128))], stop=False)
+            for k in range(4):
+                lst = R("ou", 64 * k + 32 * h, 64 * k + 32 * h + 32)
+                b = 1024 * k + 512 * h
+                if 4 * n2 + k in UA:
+                    lv(r, "ug%d" % n2)
+                    act(R("Ug", b, b + 512), IND(Fw, lst), AF.Copy)
+                    lv(r, "um%d" % n2)
+                    tt(R("Up", b, b + 512), R("Ug", b, b + 512), ps(3 + h, 0, 512), A.mult)
+                else:
+                    tt(R("Up", b, b + 512), IND(Fw, lst), R("g4", 512 * h, 512 * h + 512), A.mult)
+                mm([(pU, EX(4 * k + x), R("Up", b + x, b + 512, 4)) for x in range(4)], start=False, stop=k == 3)
+        lv(r, "g1")
+        act(R("Yb", 192 * me, 192 * me + 64), R("Ys", yb + 64 * me, yb + 64 * me + 64), AF.Copy)
+
+        def scatter(name, src, c0, more=()):
+            for t in range(7, -1, -1):
+                cp(IND(R(name), R("so", c0 + 2 * t, c0 + 2 * t + 2)), R(src, 32 * t, 32 * t + 32), more)
+        lv(r, "f2" if last else "fn")
+        o = ps(6, 256, 512)
+        mm([(o, I, R("Fold"))] + ([(o, I, R("c128"))] if last else []) + [(o, I, R("gs"))])
+        if last:
+            ts(R("Fnew"), o, 0.0, A.max, 255.0, A.min)
+            scatter("F2", "Fnew", 16)
+            dma("sp", [(T.yf[:, 2048 * h:2048 * h + 2048], T.F2[:, 2048 * h:2048 * h + 2048]) for h in range(2)], [], [R("F2")], 6000)
+        else:
+            ts(R("Fnew"), o, -128.0, A.max, 127.0, A.min)
+        lv(r, "u")
+        act(R("us"), ps(0, 0, 256), AF.Sign)
+        if not last:
+            o = ps(5, 0, 256)
+            mm([(o, I, R("Cold")), (o, R("NS4"), R("MsG"))], stop=False)
+            mm([(o, I, R("us"))], start=False)
+            act(R("wexp"), o, AF.Exp, bias=C(36), scale=16 * BETA)
+            o = ps(1, 256, 512)
+            mm([(o, R("BO45"), R("wexp"))])
+            act(R("oh"), o, AF.Sign)
+            o = ps(5, 256, 512)
+            mm([(o, EX(4, "BP"), R("MsG")), (o, EX(0, "BJ"), R("oh"))])
+            if OPT["mn_act"]:
+                af(R("Mnew"), o, None, C(41))
+            else:
+                ts(R("Mnew"), o, C(41), A.add)
+            lv(r, "ms")
+            scatter("Ms", "Mnew", 0, MSK)
+            shift()
+            lv(r, "fs")
+            scatter("Ft", "Fnew", 16)
+        lv(r, "cn")
+        o = ps(6, 0, 256)
+        mm([(o, I, R("Cold")), (o, I, R("us"))])
+        act(R("Cnew"), o, AF.Copy)
+        lv(r, "cn" if last else "cs")
+        scatter("Ct", "Cnew", 0)
+        lv(r, "end" if last else "home")
+        yg = R("Yg", NS * r, NS * r + NS)
+        cp(yg, IND(R("Yb"), R("dst", 16 * r, 16 * r + 12)), more=[X("Yin%d0" % r), X("Yin%d1" % r)])
+        mm([(ps(7, 0, NS), R("ST"), yg)])
+        ts(ps(7, 256, 256 + NS), ps(7, 0, NS), C(15), A.max, C(14), A.min)
+        tt(R("Sa"), ps(7, 256, 256 + NS), R("Sf"), A.add)
+        route(r + 1)
+
+    act(R("yxo"), R("Sf"), AF.Copy, scale=1.0 / 256)
+    dma("sp", [(T.yx[e::4, :], T.yxo[e::16, :]) for e in range(4)], [], [R("yxo")], 2200)
+    o = ps(7, 0, NS)
+    mm([(o, R("YW"), R("Sg", NS * r, NS * r + NS)) for r in range(RO)] + [(o, R("I256"), R("Yg", NS * r, NS * r + NS)) for r in range(RO)])
+    af(R("yso"), o, None, -512.0)
+    dma("sp", [(T.ys[:], T.yso[:])], [], [R("yso")], 2200)
+    lv(RO - 1, "cn")
+    o = ps(5, 0, 256)
+    mm([(o, EX(h, "BY"), R("Ct", 256 * h, 256 * h + 256)) for h in range(16)])
+    act(R("yco"), o, AF.Copy)
+    dma("act", [(T.yc[:], T.yco[:])], [], [R("yco")], 2200)
+    return ops
+
+
+def depend(ops):
+    hist = {}
+    bank = {}
+    for i, op in enumerate(ops):
+        op["i"] = i
+        dep = set(a["i"] for a in op["after"])
+        wait = set()
+        e = op["eng"]
+        acc = [(v, False) for v in op["rd"]] + [(v, True) for v in op["wr"]]
+        for v, w in acc:
+            h = hist.setdefault(v["key"], [])
+            if v["ps"]:
+                b = bank.setdefault(v["key"], [e, [], []])
+                if b[0] != e:
+                    b[:] = [e, [], b[1]]
+                wait.update(b[2])
+                if e == "pe":
+                    dep.update(b[1][-2:])
+                b[1].append(i)
+            for j, c0, c1, jw in h:
+                if (w or jw) and c0 < v["c1"] and v["c0"] < c1:
+                    same = ops[j]["eng"] == e and ops[j]["sem"] is None and op["sem"] is None
+                    if same and (e == "pe" or (OPT["inorder"] and w)):
+                        dep.add(j)
+                    else:
+                        wait.add(j)
+        for v, w in acc:
+            h = hist[v["key"]]
+            if w:
+                h[:] = [x for x in h if not (v["c0"] <= x[1] and x[2] <= v["c1"])]
+            h.append((i, v["c0"], v["c1"], w))
+        wait.discard(i)
+        dep.discard(i)
+        op["wait"] = wait
+        op["dep"] = sorted(dep | wait)
+
+
+def price(ops, p):
+    for op in ops:
+        k, n = op["size"]
+        f = p["fa"] if op["eng"] == "act" else p["fv"]
+        if k == "el":
+            c = f + max(n, 32 if op["eng"] == "act" else 64) * p["cyc"]
+        elif k in ("gat", "sca", "tt2"):
+            c = f + max(64, n * p[k]) * p["cyc"]
+        elif k == "mm":
+            c = n * p["pe"]
+        elif k == "iota":
+            c = (130 + 2 * n) * p["cyc"]
+        else:
+            c = n
+        op["cost"] = c
+        op["l"] = 0 if op["lat"] is None else p[op["lat"][0]] * op["lat"][1]
+
+
+def gap(ops, j, i, p):
+    if j not in ops[i]["wait"]:
+        return -ops[j]["l"]
+    return p["same"] if ops[j]["eng"] == ops[i]["eng"] and ops[j]["lat"] is None else p["hop"]
+
+
+def schedule(ops, p, seed, noise):
+    n = len(ops)
+    price(ops, p)
+    succ = [[] for _ in range(n)]
+    for i, op in enumerate(ops):
+        for j in op["dep"]:
+            succ[j].append(i)
+    tail = [0.0] * n
+    lev = [0.0] * n
+    rnd = np.random.RandomState(seed).standard_normal(n)
+    for i in range(n - 1, -1, -1):
+        op = ops[i]
+        tail[i] = op["cost"] + op["l"] + max([gap(ops, i, k, p) + tail[k] for k in succ[i]] + [0])
+        if op["lv"] is None:
+            lev[i] = min([lev[k] for k in succ[i]] + [1e4])
+        else:
+            lev[i] = 100 * op["lv"][0] + LEVEL[op["lv"][1]] + SHIFT.get(op["tag"], 0)
+            if op["lv"][0] == RO - 1:
+                lev[i] += LEVEL.get(op["lv"][1] + "L", 0)
+
+    def ranked(key):
+        left = [len(op["dep"]) for op in ops]
+        ready = [i for i in range(n) if not left[i]]
+        seq = []
+        while ready:
+            i = min(ready, key=lambda k: key[k])
+            ready.remove(i)
+            seq.append(i)
+            for k in succ[i]:
+                left[k] -= 1
+                if not left[k]:
+                    ready.append(k)
+        return seq
+    if OPT["hold"] >= 0:
+        key = [(lev[i], noise * float(rnd[i]) - tail[i], i) for i in range(n)]
+        left = [len(op["dep"]) for op in ops]
+        ready = {}
+        est = [0.0] * n
+        for i in range(n):
+            ready.setdefault(ops[i]["eng"], [])
+            if not left[i]:
+                ready[ops[i]["eng"]].append(i)
+        free = {e: 0.0 for e in ready}
+        for _ in range(n):
+            t, e = min((max(free[e], min(est[i] for i in lst)), e) for e, lst in ready.items() if lst)
+            i = min((k for k in ready[e] if est[k] <= t + 20), key=lambda k: key[k])
+            soon = [k for k in ready[e] if est[k] < t + OPT["hold"] * ops[i]["cost"] and key[k] < key[i]]
+            if soon:
+                i = min(soon, key=lambda k: key[k])
+            op = ops[i]
+            ready[e].remove(i)
+            op["t0"] = max(t, est[i])
+            free[e] = op["t0"] + op["cost"]
+            op["t1"] = free[e] + op["l"]
+            for k in succ[i]:
+                est[k] = max(est[k], op["t1"] + gap(ops, i, k, p))
+                left[k] -= 1
+                if not left[k]:
+                    ready[ops[k]["eng"]].append(k)
+        return ranked([(ops[i]["t0"], i) for i in range(n)])
+    busy = {}
+    for i in ranked([(lev[i], noise * float(rnd[i]) - tail[i], i) for i in range(n)]):
+        op = ops[i]
+        c = op["cost"]
+        t = max([ops[j]["t1"] + gap(ops, j, i, p) for j in op["dep"]] + [0.0])
+        b = busy.setdefault(op["eng"], [])
+        k = len(b)
+        while k > 0 and b[k - 1][1] > t:
+            k -= 1
+        while k < len(b) and b[k][0] < t + c:
+            t = max(t, b[k][1])
+            k += 1
+        b.insert(k, (t, t + c))
+        op["t0"] = t
+        op["t1"] = t + c + op["l"]
+    return ranked([(ops[i]["t0"], i) for i in range(n)])
+
+
+def emit(g, T, ops, order):
+    queue = {"dve": g.vector, "act": g.scalar, "pe": g.tensor, "pool": g, "sp": g.sync}
+    count = {}
+    known = {e: {} for e in queue}
+    total = {}
+    needed = set()
+    for op in ops:
+        needed.update(op["wait"])
+    for i in order:
+        op = ops[i]
+        e = op["eng"]
+        kn = known[e]
+        want = {}
+        for j in op["wait"]:
+            s, v = ops[j]["sig"]
+            if v > want.get(s, (0, 0))[0]:
+                want[s] = (v, j)
+        for s in sorted(want, key=lambda k: -ops[want[k][1]]["t1"]):
+            v, j = want[s]
+            if kn.get(s, 0) < v:
+                queue[e].wait_ge(T.sem[s], v)
+                kn[s] = v
+                for s2, v2 in ops[j]["clock"].items():
+                    if kn.get(s2, 0) < v2:
+                        kn[s2] = v2
+        ins = op["fn"]()
+        if op["sem"] is not None:
+            op["sig"] = op["sem"]
+            total[op["sem"][0]] = op["sem"][1]
+            if "sent" in op:
+                total["sent"] = total.get("sent", 0) + op["sent"]
+            op["clock"] = {} if "sent" in op else dict(kn)
+        else:
+            if i in needed:
+                count[e] = count.get(e, 0) + 1
+                ins.then_inc(T.sem[e], 1)
+                total[e] = count[e]
+            op["sig"] = (e, count.get(e, 0))
+            op["clock"] = dict(kn)
+    for s in sorted(total):
+        g.wait_ge(T.sem[s], total[s])
+
+
+def rank_program(g, core, T, topo):
+    if T.rank_of(core) is None:
+        return
+    ops = build(g, T, topo, core)
+    depend(ops)
+    emit(g, T, ops, schedule(ops, GUESS, OPT["seed"], OPT["noise"]))

@@ -1,3 +1,4 @@
+import math
 import numpy as np
 from concourse.bass import DstId, RemoteDMATransfer
 from concourse.mybir import AluOpType as A
@@ -5,22 +6,20 @@ from concourse.mybir import ActivationFunctionType as AF
 
 RO, NS, NL, WC = 4, 192, 256, 4096
 TW = 4144
+MB = 272
 OFFS = (0, 53, 211, 264)
 CB01 = (0, 97, 133, 230)
 BETA = 0.916
+R16, R256, R8192 = 1.5 * 2 ** 27, 1.5 * 2 ** 31, 1.5 * 2 ** 36
 OPT = dict(
-    f_act=(1, 3, 5, 7),
-    u_act=(0, 1, 2, 3, 4, 5, 6, 7), mn_act=True,
-    m_split=48,
-    inorder=False, hold=0.4, ft_act=2,
-    seed=0, noise=0.0)
-LEVEL = {'f2nd': 32.0, 'v': -60.3, 'g2': 72.3, 'rest': 12.6, 'w': 7.8, 'of': -8.7, 'wab': 8.0, 'f': 30, 't0': 13.0, 't1': 10.6, 'kc': 8.7,
-         'home': 4.8, 'ou': 111.0, 'g0': 7.6, 'g1': 65.9, 'ug0': 66.3, 'ug1': 115.4, 'um0': 306.6, 'um1': -34.4, 'u': 297.7, 'keys': 34.7,
-         'e': 32.8, 'ms': 110.9, 'fn': 37.3, 'fs': 56.9, 'cs': 23.4, 'f2': 34.5, 'end': 181.5, 'cold': 135.7, 'fold': 128.2, 'cn': 18.7,
-         'scan': -100, 'cm': -31.1, 'ft': -35, 'r0': -74.1, 'keysL': -20, 'eL': 10.1, 'foldL': -100, 'kcL': 0, 'um0L': 0, 'um1L': 0,
-         'ug0L': 0, 'ug1L': 0, 'coldL': -29.8, 'uL': 0}
-SHIFT = {'f.1': 200, 'home.9': 5, 'um1.5': 100, 'fs.7': 200, 'r0.11': 200, 'um1.1': -200, 'keys.14': 40, 'r0.7': -100, 'scan.12': 40,
-         'scan.2': -200, 'e.6': 100, 'r0.1': -100, 'w.4': -15, 'e.3': 200, 'cs.4': 100, 'keys.13': 100, 'home.3': 15, 'u.1': 100}
+    dm=False, merge=False, key_pe=False, u_act=(2, 3), u_act_last=(2, 3),
+    m_split=36,
+    sw=(((0, 3), (3, 4)), ((0, 3), (3, 4)), ((0, 3), (3, 4))),
+    pf_early=False, pf_banks=(3, 4, 3, 4), pf_dve=((), ()), f_dve=(1,), wab_dve=(0,), hb_act=False, cm_act=True, pa_act=False,
+    hold=0.4, moves=100000, heat=40.0, drift=0.5, seed=0, sel_act=8, ms_dve=2, x_act=False)
+LEVEL = {'v': -2, 'g2': 69, 'of': -386, 'rest': -44, 'w': 11, 'w0': 98, 'wab0': -130, 'kc': 11, 'keys': 129, 'f0': -192, 't0': -41, 'g0': -170, 'w1': -308, 'wab1': 113, 'f1': -13, 't1': -23, 'g1': -560, 'home': -80, 'x1': -447, 'ms': -123, 'e': 160, 'fold': 495, 'fn1': -27, 'fn0': -8, 'u0': 109, 'x0': 18, 'cold': 180, 'fs': 131, 'late': 61, 'yc': 143, 'pf': -1, 'r0': -446, 'scan': -100, 'cm': -280, 'pf@0': 105, 'fn0@0': 148, 'fn1@3': 80, 'wab1@0': 16, 'v@3': 11, 'late@0': 70, 'w0@3': 166, 'u0@0': -32, 'f1@0': -58, 'kc@0': -46, 'fs@3': -77, 't0@0': 69, 'v@0': -107, 'w@3': -65, 'fn0@3': -138, 'wab1@3': 253, 'fold@3': 171, 'u1@3': 212, 'fold@0': -37, 'e@0': 46, 'pf@3': -393, 'home@3': 23, 'u1@0': -262, 'cold@3': 427, 't1@0': 76, 'x0@3': -278, 'rest@3': 45, 'cold@0': 493, 'g2@0': 104, 'g0@3': 284, 'g1@3': 4, 'x1@0': -630, 'keys@0': -129, 'rest@0': 68, 'of@0': 181, 'ms@0': 538, 'w1@0': 169, 'w1@3': -313, 'x1@3': -64, 'g2@3': -344, 'kc@3': 88, 'home@0': 18, 'wab0@3': 101, 'e@3': -176, 'g0@0': -531, 't1@3': -238, 'f1@3': -34, 'fs@0': 72, 't0@3': -130, 'w0@0': 189, 'of@3': -254, 'fn1@0': 79, 'wab0@0': 5, 'keys@3': -62, 'ms@3': -128, 'g1@0': -151, 'f0@3': -53, 'f0@0': 68, 'r0@0': -189, 'scan@0': -26, 'u0@3': 6, 'x0@0': 32, 'w@0': -185, 'cm@0': 61}
+LEVEL = {'v': -32, 'rest': -17, 'w': 19, 'g2': 53, 'of': -322, 'w0': -64, 'kc': 3, 'wab0': 29, 'keys': -1, 'f0': 14, 'w1': -41, 'wab1': 41, 'f1': 43, 't0': 15, 'g0': 24, 'f2': 50, 't1': 275, 'ug1': 62, 'g1': -42, 'e': 123, 'fold': 148, 'cold': 151, 'home': 61, 'x1': 96, 'u1': 137, 'us1': 162, 'u0': 259, 'x0': 169, 'us0': -37, 'fn0': 19, 'fn1': -39, 'ms': -43, 'late': 126, 'fs': 381, 'pf0': 202, 'pf1': 5, 'yc': 138, 'r0': -243, 'scan': -105, 'ug0': 53, 'pf0@0': -126, 'pf1@0': 247, 'cold@3': 32, 'f0@0': 31, 'x1@0': 57, 'pf0@3': 114, 'cold@0': 63, 'fs@3': 81, 'u1@0': -50, 't0@0': 42, 'f2@0': 18, 'ms@3': -89, 'late@0': 9, 'w1@3': -12, 'g0@3': -41, 'fn0@0': 208, 'w0@3': 29, 'of@3': -197, 'f1@0': 53, 'r0@0': 38, 'of@0': -198, 'x0@0': -17, 'fold@3': -85, 'fn0@3': 31, 'kc@3': -191, 'u1@3': -51, 'fs@0': -11, 'f2@3': -7, 't0@3': 7, 'fold@0': -35, 'keys@0': 43, 'x1@3': 96, 'v@3': -67, 'ms@0': -123, 'w0@0': -8, 'us1@0': 7, 'fn1@3': 269, 'rest@3': -85, 'fn1@0': 113, 'g2@0': 77, 'u0@0': 41, 'home@0': 33, 'w@3': -171, 'x0@3': 135, 'keys@3': 37, 'rest@0': -57, 'pf1@3': -9, 'g1@3': -15, 't1@0': -24, 'v@0': -7, 'f0@3': -22, 'us0@0': 77, 'w@0': -33, 'wab0@0': -37, 'home@3': -143, 'e@0': 57, 'g0@0': -156, 'scan@0': -1, 'kc@0': 44, 'wab1@3': 3, 'g2@3': 28, 'wab0@3': 169, 'u0@3': 97, 't1@3': -234, 'w1@0': 10, 'g1@0': 55, 'wab1@0': 19, 'ug1@3': 25, 'ug1@0': -13}
+LEVEL = {'v': -19, 'rest': -63, 'w': 22, 'g2': -50, 'of': -581, 'w0': -120, 'kc': 39, 'wab0': 409, 'keys': -82, 'f0': 1, 'w1': 7, 'wab1': -126, 'f1': 24, 't0': 199, 'g0': -155, 'f2': 58, 't1': 287, 'ug1': 60, 'g1': 33, 'e': 183, 'fold': 369, 'cold': 515, 'home': -181, 'x1': 161, 'u1': 230, 'us1': 388, 'u0': 368, 'x0': 257, 'us0': 223, 'fn0': -46, 'fn1': -304, 'ms': 163, 'late': 117, 'fs': 582, 'pf0': 372, 'pf1': 54, 'yc': -413, 'r0': -551, 'scan': -77, 'ug0': 53, 'pf0@0': -131, 'pf1@0': 301, 'cold@3': 56, 'f0@0': -36, 'x1@0': 108, 'pf0@3': 33, 'cold@0': 190, 'fs@3': 127, 'u1@0': 8, 't0@0': 244, 'f2@0': -85, 'ms@3': -156, 'late@0': 4, 'w1@3': -78, 'g0@3': -421, 'fn0@0': 650, 'w0@3': 139, 'of@3': -131, 'f1@0': 231, 'r0@0': -124, 'of@0': -284, 'x0@0': 30, 'fold@3': -167, 'fn0@3': -104, 'kc@3': -284, 'u1@3': -139, 'fs@0': -73, 'f2@3': 9, 't0@3': -57, 'fold@0': -369, 'keys@0': -21, 'x1@3': 69, 'v@3': -43, 'ms@0': -314, 'w0@0': 45, 'us1@0': -57, 'fn1@3': 535, 'rest@3': -141, 'fn1@0': 225, 'g2@0': 23, 'u0@0': 58, 'home@0': -89, 'w@3': -326, 'x0@3': 182, 'keys@3': 137, 'rest@0': -349, 'pf1@3': -111, 'g1@3': 155, 't1@0': -178, 'v@0': 49, 'f0@3': -77, 'us0@0': 219, 'w@0': -476, 'wab0@0': -159, 'home@3': -281, 'e@0': 80, 'g0@0': -164, 'scan@0': -201, 'kc@0': 2, 'wab1@3': 79, 'g2@3': -200, 'wab0@3': 391, 'u0@3': -83, 't1@3': -237, 'w1@0': 98, 'g1@0': 3, 'wab1@0': 162, 'ug1@3': 91, 'ug1@0': 23, 'yc@0': -298, 'e@3': 46, 'f1@3': -40}
 
 SCRATCH = {}
 PART = {}
@@ -37,54 +36,54 @@ def _p(dt, cols, whole, *names):
         PART[n] = (whole, cols * i, cols)
 
 
-_s("bfloat16", TW, "Ct", "Ft", "Ms", "F2")
-_s("float32", 4096, "K")
-_s("int32", 144, "DI", "C4")
-_s("int32", 128, "C16", "C8")
-_s("int32", 16, "ic", "J")
-_s("int32", 32, "L0", "dmi")
-_s("float32", 144, "DG", "Bt32")
-_s("float32", 64, "col")
-_s("float32", 16, "OH", "LT", "OH2", "OH4", "OHs")
-_p("bfloat16", 144, "wide", "Big", "Big4", "Bd", "Bt", "BJ", "BP", "BY", "H1", "H2", "H3", "H4", "H5", "H6", "HD", "W1", "W2", "W3", "W4")
-_p("bfloat16", 128, "tiles", "I", "BO", "BO45", "BO128", "NS4", "ST", "TT", "YW", "I256", "N256", "t1", "t2", "t3", "t4", "t5", "t6")
-_s("float16", 128, "I16")
-_s("float16", 256, "CBt")
-_s("float32", 128, "I32")
-_s("bfloat16", 2048, "TR", "Sel")
-_s("float32", 512, "Sel32", "krow")
-_s("bfloat16", 512, "D0", "V", "Mt")
-_s("bfloat16", 256, "CA", "CL", "CO", "cy", "c128", "fa", "fb", "Wp", "gs", "MsG", "MsM", "Cold", "Fold", "Cnew", "Fnew", "us", "wexp",
-   "oh", "Mnew", "mt", "cb", "hb")
-_s("bfloat16", NS, "CAP", "tb", "X0b", "Hh", "cum", "P")
+_s("bfloat16", TW, "Ct", "Ft")
+_s("bfloat16", MB + TW, "Ms")
+_s("float32", TW, "K")
+_s("float32", 2048, "PF0", "PF1", "Up", "Ug")
+_s("int32", 16, "ic")
+_s("float32", 128, "col")
+_p("float32", 16, "sixteen", "OH", "LT", "L4", "L8", "icf")
+_p("bfloat16", 144, "wide", "DI", "DG", "C4", "Big", "B4", "Bd", "Bt", "Bt1", "Bt1s", "EX0", "BY", "Y2", "H1", "H2", "H3", "H4", "H5", "H6",
+   "HD", "HA", "HB", "HL")
+_p("bfloat16", 128, "tiles", "CE", "CEb", "CEm", "C16", "I", "NI", "I64", "I8192", "I256", "N256", "N2048", "BO", "C8", "GB", "BO45", "ST", "STA",
+   "WR", "HM", "TT", "WA", "WB", "DC", "BJ", "KP", "PK", "U1", "U2", "YW", "t1", "t2", "t3", "t4", "t5", "t6", "t7", "t8")
+_p("bfloat16", 64, "narrow", "J", "kb", "hb0", "fl")
+_s("float16", NS, "CB")
+_s("float16", 64, "ks")
+_s("float16", 32, "Kh")
+_s("float32", 128, "I32", "R32")
+_s("float32", 24 if OPT["merge"] else 16, "BB")
+_s("bfloat16", 2048, "Sel", "DM")
+_s("bfloat16", 512, "D0", "Mt", "RS0", "J512")
+_s("bfloat16", 272, "RS1")
+_s("float32", 512, "Z0")
+_s("float32", 272, "Z1")
+_s("bfloat16", 256, "V", "CO", "c128", "fa", "Wp", "gs", "CMg", "Hd", "Cold", "Fold", "CMn", "Fnew", "us", "Xs", "ut", "key", "Mx", "mt")
+_s("bfloat16", NS, "CL", "CAP", "tb", "Sb", "ycl", "sg", "cum", "P", "hbs")
+_s("bfloat16", 128, "cy")
 _s("bfloat16", 4 * NS, "Yg", "Sg", "Yb")
-_s("int32", NS, "X0", "Sa", "Si")
-_s("float32", NS, "Tf", "Sf", "yso", "yxo")
+_s("int32", NS, "X0", "vi", "hm", "hn")
+_s("float32", NS, "Tf", "Sf", "yso", "yxo", "PA", "pr")
+_s("float32", 64, "em", "tab")
 _s("float32", 16 * NS, "Zs")
 _s("float32", 4 * NL, "Zr", "SW")
-_s("bfloat16", 4 * NL, "Ys", "G", "Wcd", "Wab", "g4", "E")
-_s("uint16", 64, "dst", "om", "EL")
-_s("uint16", 256, "of", "ou")
-_s("uint16", 32, "kc16", "so")
-_s("float32", 256, "PA", "pr", "yco")
-_s("int32", 256, "vi", "hm", "ki", "mi")
-_s("float32", 64, "ks")
-_s("bfloat16", 64, "kb")
-_s("float32", 40, "kc")
-_s("float32", 32, "dum", "x1", "x2")
-_s("bfloat16", 4096, "Vg", "Ug", "Up")
+_s("bfloat16", 4 * NL, "Ys", "G", "Wab")
+_s("uint16", 64, "dst", "om", "kl")
+_s("uint16", 256, "of")
+_s("uint16", 32, "so")
+_s("float32", 256, "yc0", "yco", "ycg", "d3", "Km")
+_s("int32", 256, "ki", "mi")
+_s("bfloat16", 4096, "Vg")
 _s("float16", 4096, "Vp")
 for _i in range(8):
-    if _i == 3:
-        SCRATCH["pw"] = ("psum", [128, 1024], "float32")
-    elif _i != 4:
-        SCRATCH["ps%d" % _i] = ("psum", [128, 512], "float32")
+    SCRATCH["ps%d" % _i] = ("psum", [128, 512], "float32")
 
-NDMA = 24
+NDMA = 28
 SEMAPHORES = ["dve", "act", "pe", "pool", "sent"] + ["fw%d" % r for r in range(RO)] + ["bk%d" % r for r in range(RO)] + [
     "d%d" % i for i in range(NDMA)]
 TWO = {"bfloat16", "float16", "uint16"}
-GUESS = dict(cyc=1.0, fv=45, fa=90, gat=1.6, sca=3.9, pe=0.6, hop=130, same=70, rem=3600, dma=1.0, tt2=1.0)
+GUESS = dict(cyc=0.87, fv=48, fa=95, gat=1.3, sca=3.0, pe=0.52, hop=130, same=70, rem=2900, dma=0.85, tt2=1.0)
+OTHERS = (dict(cyc=1.1, pe=0.62, gat=1.7, sca=4.5, tt2=2.0), dict(hop=200, same=100, rem=4200, dma=1.1, pe=0.45))
 
 
 def build(g, T, topo, core):
@@ -93,8 +92,8 @@ def build(g, T, topo, core):
     ops = []
     ndma = [0]
     level = [None]
-    seen = {}
-    FA, UA, MS = OPT["f_act"], OPT["u_act"], OPT["m_split"]
+    cols = {}
+    MS = OPT["m_split"]
 
     def R(name, c0=0, c1=None, st=1, key=None):
         buf, o, w = PART.get(name) or (name, 0, SCRATCH[name][1][1])
@@ -112,11 +111,7 @@ def build(g, T, topo, core):
     def parts(v):
         if not isinstance(v, dict):
             return []
-        if "ind" in v:
-            return list(v["ind"])
-        if v["key"] == "pw":
-            return [dict(v, key="pw%d" % b) for b in range(v["c0"] // 512, (v["c1"] - 1) // 512 + 1)]
-        return [v]
+        return list(v["ind"]) if "ind" in v else [v]
 
     def ap(v):
         return v["ap"] if isinstance(v, dict) else v
@@ -131,10 +126,8 @@ def build(g, T, topo, core):
                 wr.append(o["ind"][0])
                 rd.append(o["ind"][1])
             else:
-                wr += parts(o)
-        seen[level[0]] = seen.get(level[0], 0) + 1
-        tag = level[0] and "%s.%d" % (level[0][1], seen[level[0]])
-        ops.append(dict(eng=eng, fn=fn, rd=rd + list(more), wr=wr, size=size, sem=sem, lat=lat, after=[], lv=level[0], tag=tag))
+                wr.append(o)
+        ops.append(dict(eng=eng, fn=fn, rd=rd + list(more), wr=wr, size=size, sem=sem, lat=lat, after=[], lv=level[0]))
         return ops[-1]
 
     def lv(r, name):
@@ -155,16 +148,16 @@ def build(g, T, topo, core):
             fn = lambda: g.vector.tensor_scalar(out["ap"], a["ap"], ap(s1), None, o1)
         else:
             fn = lambda: g.vector.tensor_scalar(out["ap"], a["ap"], ap(s1), ap(s2), o1, o2)
-        add("dve", fn, [out], [a, s1, s2], vsize(out, [a]), more)
+        return add("dve", fn, [out], [a, s1, s2], vsize(out, [a]), more)
 
     def tt(out, a, b, op, more=()):
-        add("dve", lambda: g.vector.tensor_tensor(out["ap"], a["ap"], b["ap"], op), [out], [a, b], vsize(out, [a, b], True), more)
+        return add("dve", lambda: g.vector.tensor_tensor(out["ap"], a["ap"], b["ap"], op), [out], [a, b], vsize(out, [a, b], True), more)
 
     def cp(out, a, more=()):
-        add("dve", lambda: g.vector.tensor_copy(out["ap"], a["ap"]), [out], [a], vsize(out, [a]), more)
+        return add("dve", lambda: g.vector.tensor_copy(out["ap"], a["ap"]), [out], [a], vsize(out, [a]), more)
 
     def ms(out, v):
-        add("dve", lambda: g.vector.memset(out["ap"], v), [out], [], vsize(out, []))
+        return add("dve", lambda: g.vector.memset(out["ap"], v), [out], [], vsize(out, []))
 
     def scan(out, d0, d1, init, o0, o1):
         add("dve", lambda: g.vector.tensor_tensor_scan(out["ap"], d0["ap"], d1["ap"], ap(init), o0, o1), [out], [d0, d1, init],
@@ -176,11 +169,11 @@ def build(g, T, topo, core):
             kw["bias"] = ap(bias)
         if scale is not None:
             kw["scale"] = ap(scale)
-        add("act", lambda: g.scalar.activation(out["ap"], a["ap"], f, **kw), [out], [a, bias, scale],
-            ("gat" if "ind" in a else "el", out["n"]), more)
+        return add("act", lambda: g.scalar.activation(out["ap"], a["ap"], f, **kw), [out], [a, bias, scale],
+                   ("gat" if "ind" in a else "el", out["n"]), more)
 
     def af(out, a, scale=None, bias=None):
-        act(out, a, AF.Identity, bias=bias, scale=scale)
+        return act(out, a, AF.Identity, bias=bias, scale=scale)
 
     def mm(items, start=True, stop=True, more=(), each=False):
         def fn():
@@ -192,7 +185,7 @@ def build(g, T, topo, core):
         rd = []
         for o, l, r in items:
             rd += [l, r]
-        add("pe", fn, [o for o, l, r in items], rd, ("mm", c), more)
+        return add("pe", fn, [o for o, l, r in items], rd, ("mm", c), more)
 
     def iota(out, pat, base, cm):
         if out["dt"] == "int32":
@@ -229,22 +222,33 @@ def build(g, T, topo, core):
             for o, m in zip(far, (m0, m1)):
                 rid, pid, _e = topo.addr(T.cores[o])
                 tr.append(RemoteDMATransfer(dst_ids=[DstId(rid=rid, pnc=pid)], dma_engine_mask=m, remote_sem=T.sem[sem],
-                                            src=src(o), dst=dst))
+                                            src=src(o), dst=dst(o)))
             if tr:
                 g.remote_dma_fused(tr, local_sem=T.sem["sent"])
             for o in near:
                 rid, pid, _e = topo.addr(T.cores[o])
-                g.remote_dma(dst, src(o), T.sem[sem], T.sem["sent"], pid, rid, m0 | m1)
+                g.remote_dma(dst(o), src(o), T.sem[sem], T.sem["sent"], pid, rid, m0 | m1)
         calls = len(far) // 2 + len(near)
         op = add("pool", fn, [X(key)], rd, ("fix", 200 * calls), sem=(sem, 2 * len(eng)), lat=("rem", 0.55 + 0.15 * len(peers)))
         op["sent"] = calls * len(eng)
         return op
 
-    def C(i):
+    def place(q, o):
+        return 3 if q == o else 2 if q // 2 == o // 2 else q % 2
+
+    def C(name):
+        i = cols.setdefault(name, len(cols))
         return R("col", i, i + 1)
 
-    def O(i, name="OH"):
-        return R(name, i, i + 1)
+    def lin(name, a, scale=None, bias=None):
+        af(C(name), a, scale, bias)
+        return C(name)
+
+    def OH(i):
+        return R("OH", i, i + 1)
+
+    def LT(i):
+        return R("LT", i, i + 1)
 
     def ic(i):
         return R("ic", i, i + 1)
@@ -256,12 +260,21 @@ def build(g, T, topo, core):
         return win(name, 15 - rho)
 
     def ps(b, c0, c1, st=1):
-        if b in (3, 4):
-            return R("pw", 512 * (b - 3) + c0, 512 * (b - 3) + c1, st)
         return R("ps%d" % b, c0, c1, st)
 
     def SEL(i):
         return R("Sel", 128 * i, 128 * i + 128)
+
+    def pick(out, index, target, coef=None):
+        if coef is None:
+            ts(out, index, target, A.is_equal)
+        else:
+            ts(out, index, target, A.is_equal, coef, A.mult)
+
+    def two(out, index, a, b, t):
+        pick(R(t[0]), index, *a)
+        pick(R(t[1]), index, *b)
+        tt(out, R(t[0]), R(t[1]), A.add)
 
     I = R("I")
     add("dve", lambda: g.vector.memset(T.X0[:], 0), [X("X0z")], [], ("el", NS))
@@ -271,156 +284,186 @@ def build(g, T, topo, core):
                  2600 + 1100 * k)
         op["after"] = [prev] if prev else []
         prev = op
-    dma("act", [(T.tb[:], T.tg[:])], [R("tb")], [], 2200)
     dma("act", [(T.X0[e::16, :], T.x0[e::4, :]) for e in range(4)], [R("X0")], [X("X0z")], 2200)
+    dma("act", [(T.tb[:], T.tg[:])], [R("tb")], [], 2200)
+    ms(R("Ms", 0, 1104), 0.0)
+    op = dma("sp", [(T.Ms[:, 1104 * k:1104 * k + 1104], T.Ms[:, 0:1104]) for k in range(1, 4)], [R("Ms", 1104, MB + TW)],
+             [R("Ms", 0, 1104)], 8600)
+    op["after"] = [prev]
+    prev = op
     for k in range(2):
         op = dma("sp", [(T.Ft[:, 2048 * k:2048 * k + 2048], T.ft[:, 2048 * k:2048 * k + 2048])], [R("Ft", 2048 * k, 2048 * k + 2048)], [],
-                 8000 + 2200 * k)
+                 10800 + 2200 * k)
         op["after"] = [prev]
         prev = op
-    iota(ic(0), [[0, 1]], 0, 1)
-    iota(R("J"), [[1, 16]], 0, 0)
+    iota(R("ic", 0, 2), [[3, 2]], 0, 1)
+    iota(R("J", 0, 16), [[1, 16]], 0, 0)
     iota(R("DI"), [[1, 144]], 0, -1)
-    iota(R("C8"), [[1, 16], [0, 8]], 0, 0)
+    iota(R("CE"), [[16, 8], [0, 4], [1, 4]], 0, 0)
+    iota(R("CEb"), [[16, 8], [-8, 2], [0, 8]], 8, 0)
     iota(R("C4"), [[1, 36], [0, 4]], 0, 0)
     iota(R("C16"), [[1, 8], [0, 16]], 0, 0)
-    iota(R("L0"), [[0, 4], [16, 2], [4, 4]], 0, 0)
-    iota(R("dmi"), [[0, 16], [16, 2]], 4112, 0)
-    ts(ic(1), ic(0), 15, A.bitwise_and)
-    cp(C(0), ic(1))
-    ts(R("OH"), R("J"), C(0), A.is_equal)
-    ts(R("LT"), R("J"), C(0), A.is_gt)
-    ts(R("DG"), R("DI"), C(0), A.add)
-    ts(ic(2), ic(0), 4, A.arith_shift_right)
-    cp(C(1), ic(2))
-    af(C(2), C(1), 2.0, 1.0)
-    af(C(3), C(1), 4.0, 3.0)
-    ts(ic(3), ic(0), 3, A.bitwise_and)
-    cp(C(4), ic(3))
-    LT4, LT8, LT12 = O(4, "LT"), O(8, "LT"), O(12, "LT")
-    af(C(5), LT4, -1.0, LT8)
-    af(C(6), LT8, -1.0, LT12)
-    af(C(7), LT8, -16385.0, 16384.0)
-    af(C(8), LT12, -192.0, 192.0)
-    af(C(9), C(8), C(4))
-    af(C(10), C(6), -1.0, C(9))
-    af(C(11), C(6), 1024.0, C(9))
-    af(C(12), LT8, 16384.0, -16384.0)
-    af(C(13), C(12), C(4))
-    af(C(14), C(5), 129024.0, 2048.0)
-    af(C(15), C(14), -1.0)
-    af(C(16), O(8), 32768.0)
-    af(C(17), LT4, 64.0)
-    DI = R("DI", 0, 128)
-    ts(I, DI, 0.0, A.is_equal)
-    ts(R("Big"), R("DG"), 15.0, A.is_equal)
-    ts(R("t1"), DI, 0.0, A.is_equal, LT4, A.mult)
-    ts(R("t2"), DI, 4.0, A.is_equal, C(17), A.mult)
-    ts(R("t3"), R("C8"), C(2), A.is_equal, O(0), A.mult)
-    tt(R("t1"), R("t1"), R("t2"), A.add)
-    tt(R("ST"), R("t1"), R("t3"), A.add)
-    af(R("CAP"), R("tb"), 0.0, C(11))
-    af(R("Tf"), R("tb"), None, C(16))
+    iota(R("C8"), [[1, 16], [0, 8]], -8, 0)
+    iota(R("J512"), [[0, 32], [-1, 16]], 15, 0)
+    sh, an = A.arith_shift_right, A.bitwise_and
+    ts(ic(2), ic(0), 15, an)
+    ts(ic(3), ic(0), 3, an)
+    ts(ic(4), ic(1), 3, an)
+    ts(ic(5), ic(0), 112, an)
+    cp(R("icf", 0, 6), R("ic", 0, 6))
+    ts(ic(6), ic(0), 4, sh)
+    ts(ic(7), ic(0), 2, sh, 3, an)
+    ts(ic(8), ic(0), 1, an)
+    ts(ic(9), ic(0), 1, sh, 1, an)
+    ts(ic(10), ic(0), 1, sh, 7, an)
+    cp(R("icf", 6, 11), R("ic", 6, 11))
+    p_, _x, r_, e_, e1_, g16, gr, s_, b0, b1, w_ = [R("icf", i, i + 1) for i in range(11)]
+    J16 = R("J", 0, 16)
+    ts(R("OH"), J16, r_, A.is_equal)
+    ts(R("LT"), J16, r_, A.is_gt)
+    ts(R("DG"), R("DI"), r_, A.add)
+    DI, DG, DG1 = R("DI", 0, 128), R("DG"), R("DG", 0, 128)
+    pick(I, DI, 0.0)
+    pick(R("Big"), DG, 15.0)
+    pick(R("ST"), R("CE"), p_)
+    tt(R("CEm"), R("CE"), R("CEb"), A.min)
+    pick(R("STA"), R("CEm"), p_)
+    tE = lin("tE", g16, None, e_)
+    tE1 = lin("tE1", g16, None, e1_)
+    pick(R("WR"), R("CE"), tE, lin("cWR", LT(8), -32768.0))
+    ts(R("L4"), R("LT"), LT(4), A.subtract)
+    ts(R("L8"), R("LT"), LT(8), A.subtract)
+    r45, r47, r411, r414 = [R("L4", j, j + 1) for j in (6, 8, 12, 15)]
+    r811, r812, r813 = [R("L8", j, j + 1) for j in (12, 13, 14)]
+    cP = lin("cP", OH(15), -0.5, lin("cP0", r812, 0.5))
+    two(R("HM"), R("CE"), (tE, cP), (tE1, lin("cM", r813, -0.5)), ("t1", "t2"))
+    act(C("r8"), r_, AF.Relu, bias=-8.0)
+    bsg = lin("bsg", C("r8"), -16384.0, lin("bsg0", r47, -65536.0, 128.0))
+    o192 = lin("o192", lin("h192", LT(12), -192.0, 192.0), e_)
+    init = lin("init", r811, -1.0, o192)
+    cap = lin("cap", r811, 1024.0, o192)
+    rows = {"b0": ((1, -160), (-480, -160), (4, -640), (6144, -5120), (15, 1), (-1, 14), (2, -1)),
+            "b1": ((2, -319), (2, -1), (1, -1)), "r": ((1, 4112), (1, 4128), (1, 1), (2, -8), (2, -7))}
+    at, made = 0, []
+    for x, name in ((b0, "b0"), (b1, "b1"), (r_, "r")):
+        n = len(rows[name])
+        for i, (a, b) in enumerate(rows[name]):
+            iota(R("tab", at + i, at + i + 17, 16), [[b - a, 2]], a, 0)
+            made.append(R("tab", 32 + at + i, 33 + at + i))
+        af(R("tab", 48 + at, 48 + at + n), R("tab", at, at + n), x)
+        tt(R("tab", 32 + at, 32 + at + n), R("tab", 48 + at, 48 + at + n), R("tab", 16 + at, 16 + at + n), A.add)
+        at += n
+    aCol, aBest, aBlk, lBest, cPK, tPY, sa, bVar, sb, dc, spE, spO, r1, tU, tU1 = made
+    bT = lin("bT", s_, 256.0, lin("bT0", OH(12), 16384.0))
+    af(R("CAP"), R("tb"), 0.0, cap)
+    af(R("Tf"), R("tb"), None, bT)
     ms(R("D0"), 0.0625)
     ms(R("D0", 0, 512, 16), -1024.0)
     fill(R("Yb"), 0)
     for o in range(N):
         fill(R("Zs", 192 * o, 192 * o + 64), 0)
-    ms(R("Ms", 0, 1024), 0.0)
-    ms(R("Ms", 1024, 2048), 0.0)
-    fill(R("Ms", 2048, 3072), 0)
-    fill(R("Ms", 3072, TW), 0)
     ms(R("Ct", WC, TW), 0.0)
     ms(R("Ft", WC, TW), 0.0)
-    ts(R("Big4"), R("C4"), C(3), A.is_equal)
-    af(C(18), O(3), 844.0)
-    af(C(19), O(2), 212.0, C(18))
-    af(C(20), O(1), 2128.0)
-    af(C(21), O(0), 1552.0, C(20))
-    af(C(22), O(12), 128.0)
-    af(C(23), O(8), -128.0, C(22))
-    af(R("OH2"), R("OH"), 2.0)
-    af(R("OH4"), R("OH"), 4.0)
-    af(R("OHs"), R("OH"), 0.0625)
-    B4 = R("Big4")
-    for name, c in (("H1", O(0)), ("H2", O(1, "OH2")), ("H3", C(19)), ("H4", O(2, "OH4")), ("H5", O(3, "OH2")), ("H6", C(21)),
-                    ("HD", C(23)), ("W1", O(6, "OHs")), ("W2", O(4, "OHs")), ("W3", O(7, "OHs")), ("W4", O(5, "OHs"))):
-        af(R(name), B4, c)
-    ts(ic(4), ic(0), 1, A.bitwise_and)
-    ts(ic(5), ic(0), 1, A.arith_shift_right, 1, A.bitwise_and)
-    ts(C(24), ic(4), 2.0, A.mult, -1.0, A.add)
-    ts(C(26), ic(5), 2.0, A.mult, -1.0, A.add)
-    af(C(25), C(24), -12.0, 2.0)
-    af(C(27), C(26), -12.0, 2.0)
-    af(C(28), C(24), 0.5, -159.5)
-    af(C(29), C(24), 2.0, -638.0)
-    af(C(30), C(26), None, -318.0)
+    ms(R("K", WC, TW), 0.0)
+    pick(R("B4"), R("C4"), lin("g43", gr, 4.0, 3.0))
+    B4 = R("B4")
+    af(R("H1"), B4, OH(0))
+    ts(R("H2"), B4, OH(1), A.mult, 2.0, A.mult)
+    q4 = lin("q4", b0, lin("q4a", b1, 56.0, 576.0), lin("q4b", b1, -1340.0, 1552.0))
+    h6 = lin("h6", q4, LT(2))
+    af(R("H3"), B4, lin("h3", h6, -1.0, lin("h3a", q4, LT(4))))
+    ts(R("H4"), B4, OH(2), A.mult, 4.0, A.mult)
+    ts(R("H5"), B4, OH(3), A.mult, 2.0, A.mult)
+    af(R("H6"), B4, h6)
+    ts(R("HD"), B4, lin("hd", OH(12), -1.0, OH(8)), A.mult, 512.0, A.mult)
+    tL = lin("tL", r45, None, 12.0)
+    tA = lin("tA", r45, -1.0, 13.0)
+    pick(R("HA"), DG, tA, lin("ha", OH(6), 4.0, OH(4)))
+    pick(R("HB"), DG, tA, lin("hb", b0, lin("hba", r47, 2.0)))
+    pick(R("HL"), DG, tL, lin("hl", q4, r47))
     z64 = R("Big", 0, 64)
-    fill(R("CA", 64, 128), -160)
-    af(R("CA", 128, 192), z64, 0.0, C(29))
-    fill(R("CA", 192, 256), -640)
-    for h in range(2):
-        ts(R("CBt", 128 * h, 128 * h + 64), z64, 0.0, A.mult, C(30), A.add)
-        ts(R("CBt", 128 * h + 64, 128 * h + 128), z64, 0.0, A.mult, -319.0, A.add)
-    fill(R("CL", 0, 128), -5120)
-    fill(R("CL", 128, 256), 1024)
+    ts(R("CB", 0, 64), z64, 0.0, A.mult, bVar, A.add)
+    ts(R("CB", 64, 128), z64, 0.0, A.mult, -319.0, A.add)
+    ts(R("CB", 128, 192), z64, 0.0, A.mult, bVar, A.add)
+    fill(R("CL", 0, 64), -5120)
+    af(R("CL", 64, 128), z64, 0.0, lBest)
+    fill(R("CL", 128, 192), 1024)
     for k in range(4):
-        fill(R("CO", 64 * k, 64 * k + 64), 16 * CB01[k])
-    af(R("cy"), R("CL"), 0.0, -127.5)
-    ts(R("Bd"), R("DI"), 12.0, A.is_equal, LT4, A.mult)
-    af(C(31), C(0), 0.25, 12.0)
-    ts(R("Bt"), R("DG"), C(31), A.is_equal)
-    af(R("Bt32"), R("Bt"))
-    ts(R("BO"), R("C16"), C(1), A.is_equal)
+        fill(R("CO", 64 * k, 64 * k + 64), 16 * CB01[k] - (2048 if k and OPT["hb_act"] else 0))
+    fill(R("c128"), 4)
+    af(R("cy"), R("c128", 0, 128), 0.0, -127.5)
+    pick(R("Bd"), R("DI"), 12.0, LT(4))
+    if OPT["hb_act"]:
+        af(R("N2048"), I, -2048.0)
+    pick(R("Bt"), DG, lin("tBt", r_, 0.25, 12.0))
+    pick(R("Bt1"), DG, lin("tBt1", r_, 0.25, 11.75))
+    af(R("Bt1s"), R("Bt1"), 0.0625)
+    af(R("EX0"), R("Big"), OH(0))
+    cs = lin("cs", LT(4), -4.0, 1.0)
+    tW = lin("tW", b1, -1.0, lin("g41", gr, 4.0, 1.0))
+    csB = lin("csB", cs, b0)
+    csA = lin("csA", csB, -1.0, cs)
+    pick(R("WA"), R("C4", 0, 128), tW, csA)
+    pick(R("WB"), R("C4", 0, 128), tW, csB)
+    fs = lin("fs", sa, sb)
+    m16 = lin("m16", lin("m16a", r47, -16.0), sa)
+    fb = lin("fb", lin("fb0", b0, -4.0, lin("fb1", m16, None, 4.0)), sb)
+    af(R("DC"), I, dc)
+    pick(R("BO"), R("C16"), gr)
     BO = R("BO")
-    for r in (0, 1, 2, 3, 4, 5, 6, 7, 8, 12):
-        af(SEL(r), BO, O(r))
-    for l in range(4):
-        af(R("Sel32", 128 * l, 128 * l + 128), BO, O(4 * l))
-    cp(R("I16"), I)
-    af(R("I32"), I)
-    af(R("I256"), I, 1.0 / 256)
-    af(R("N256"), I, -1.0 / 256)
-    af(C(32), C(5), -16.0)
-    af(C(33), O(4), -16.0)
-    ts(R("t4"), DI, -4.0, A.is_equal, C(32), A.mult)
-    ts(R("t5"), R("C8"), C(2), A.is_equal, C(33), A.mult)
-    tt(R("t4"), R("t4"), R("t5"), A.add)
-    af(R("t6"), I, -1024.0)
-    tt(R("TT"), R("t6"), R("t4"), A.add)
-    af(C(34), C(5), -2560.0, 163840.0 + 2560.0 - 128.0)
-    for rho in range(16):
-        ts(R("TR", 128 * rho, 128 * rho + 128), EX(rho), O(rho, "LT"), A.mult)
-    af(R("t2"), BO, 0.45)
-    tt(R("BO45"), R("t2"), I, A.subtract)
-    af(C(41), O(0), 60.0)
-    af(C(42), C(0), -0.5)
-    af(R("BO128"), BO, 128.0)
-    af(R("NS4"), SEL(4), -1.0)
-    af(C(40), C(6), -64.0)
-    af(R("YW"), BO, C(40))
-    af(R("BJ"), R("Big"), C(42))
-    af(R("BP"), R("Big"), O(4))
-    af(C(35), C(0), None, 1.0)
-    af(R("BY"), R("Big"), C(35))
-    af(C(36), C(0), -BETA)
-    ts(ic(6), ic(1), 2, A.arith_shift_right)
-    cp(C(37), ic(6))
-    ts(ic(7), ic(6), 1, A.bitwise_and)
-    cp(C(38), ic(7))
-    af(C(39), C(38), -33.0, 32.0)
-    ts(R("x1"), R("L0"), C(37), A.add)
-    cp(R("EL", 0, 32), R("x1"))
-    ts(R("EL", 32, 64), R("x1"), C(38), A.mult, C(39), A.add)
-    ts(R("dum"), R("dmi"), C(0), A.add, 1.0 / 8192, A.mult)
-    fill(R("kc", 32, 40), -1)
+    for q in range(4):
+        o = R("Sel", 512 * q, 512 * q + 512)
+        iota(R("DM", 512 * q, 512 * q + 512), [[1, 4], [16, 8], [0, 16]], 4 * q, 0)
+        pick(o, R("DM", 512 * q, 512 * q + 512), p_)
+    fill(R("t8"), 0)
+    for name, v in (("I32", 1.0), ("I256", 1.0 / 256), ("N256", -1.0 / 256), ("NI", -1.0), ("I64", 64.0), ("I8192", 8192.0)):
+        add("pool", lambda name=name, v=v: g.affine_select(R(name)["ap"], R("t8")["ap"], [[-1, 128]], A.not_equal, v, 0, 1),
+            [R(name)], [R("t8")], ("iota", 150))
+    pick(R("TT"), R("CE"), tE, -256.0)
+    act(C("e0"), e_, AF.Relu, bias=1.0, scale=-1.0)
+    bG = lin("bG", bT, -1.0, lin("bG0", C("e0"), 4096.0, 163840.0 - 128.0))
+    pick(R("RS0"), R("J512"), r_)
+    if OPT["dm"]:
+        for r in range(16):
+            tt(R("DM", 128 * r, 128 * r + 128), SEL(r), I, A.subtract)
+    fill(R("RS1"), 0)
+    fill(R("RS1", 0, 272, 17), 1)
+    if OPT["merge"]:
+        iota(R("J", 32, 64), [[0, 2], [1, 16]], 0, 0)
+        pick(R("BB"), R("J", 32, 56), gr)
+    else:
+        iota(R("J", 32, 48), [[0, 2], [1, 8]], 0, 0)
+        pick(R("BB"), R("J", 32, 48), gr)
+    pick(R("GB"), R("C8"), gr, 2.0 ** 20)
+    af(R("KP"), I, r414)
+    two(R("PK"), DG1, (lin("tPK", w_, None, 4.0), cPK), (tPY, r1), ("t5", "t6"))
+    pick(R("U1"), DG1, tU, r411)
+    pick(R("t7"), DG1, tU1, lin("cU", r411, 0.0625))
+    tt(R("U2"), R("t7"), R("U1"), A.subtract)
+    fill(R("Mx"), 0)
+    af(R("BY"), R("Big"), r1)
+    af(R("YW"), BO, lin("yw", r811, -64.0))
 
-    MSK = [X("Ms%d" % x) for x in range(5)]
+    MSK = [X("Ms%d" % x) for x in range(4)]
+    Mw = R("Ms", MB, MB + TW)
 
     def shift():
-        pairs = [(T.Ms[x::16, 0:WC - OFFS[x]], T.Ms[0::16, OFFS[x]:WC]) for x in (1, 2, 3)]
-        pairs += [(T.Ms[x::16, WC - OFFS[x]:WC], T.Ms[0::16, 0:OFFS[x]]) for x in (1, 2, 3)]
+        pairs = [(T.Ms[x::16, MB - OFFS[x]:MB - OFFS[x] + WC], T.Ms[0::16, MB:MB + WC]) for x in (1, 2, 3)]
+        pairs += [(T.Ms[x::16, MB + WC - OFFS[x]:MB + WC], T.Ms[0::16, MB:MB + OFFS[x]]) for x in (1, 2, 3)]
         dma("sp", pairs, MSK[1:4], [MSK[0], R("Ms")], 2800)
+
+    def pairs_of(r, banks):
+        for c in range(4):
+            lv(r, "pf%d" % (c // 2))
+            for jj in (2 * c, 2 * c + 1):
+                o = ps(banks[c], 256 * (jj % 2), 256 * (jj % 2) + 256)
+                mm([(o, I, R("Ft", 2 * jj, WC, 16)), (o, R("I8192"), R("Ft", 2 * jj + 1, WC, 16))])
+            o = R("PF%d" % (r % 2), 512 * c, 512 * c + 512)
+            if c in OPT["pf_dve"][min(r, 1)]:
+                ts(o, ps(banks[c], 0, 512), -2.0 ** 20, A.add)
+            else:
+                af(o, ps(banks[c], 0, 512), None, -2.0 ** 20)
+
 
     lv(0, "scan")
     for b in range(8):
@@ -431,273 +474,393 @@ def build(g, T, topo, core):
         ts(R("ki", 32 * q, 32 * q + 32), R("K", 16 * q + 15, 4096, 128), 16.0, A.mult)
     ts(R("mi"), R("ki"), 15, A.bitwise_and)
     ts(R("mt"), R("mi"), -1.0, A.mult, 15.0, A.add)
-    mm([(ps(3, 128 * h, 128 * h + 128), R("mt", 128 * h, 128 * h + 128), I) for h in range(2)], each=True)
+    mm([(ps(3, 128 * h, 128 * h + 128), R("mt", h, 256, 2), I) for h in range(2)], each=True)
     act(R("Mt", 0, 256), ps(3, 0, 256), AF.Copy)
-    dma("act", [(T.Ms[64 * h:64 * h + 64:16, 0:WC], T.Mt[:, 128 * h:128 * h + 128]) for h in range(2)], [MSK[0]],
-        [R("Mt", 0, 256), R("Ms")], 2200)
-    shift()
-    lv(0, "cm")
-    ts(R("cb"), R("ki"), 0.0625, A.mult)
-    mm([(ps(4, 128 * h, 128 * h + 128), R("cb", 128 * h, 128 * h + 128), I) for h in range(2)], each=True)
-    act(R("Mt", 256, 512), ps(4, 0, 256), AF.Copy)
-    dma("act", [(T.Ms[64 * h + 4:64 * h + 64:16, 0:WC], T.Mt[:, 256 + 128 * h:384 + 128 * h]) for h in range(2)], [MSK[4]],
-        [R("Mt", 256, 512), R("Ms")], 2200)
-    lv(0, "ft")
-    for k in range(4):
-        o = R("Ft", 1024 * k, 1024 * k + 1024)
-        if k < OPT["ft_act"]:
-            af(o, o, None, -128.0)
-        else:
-            ts(o, o, -128.0, A.add)
-    lv(0, "r0")
+
+    def first(x):
+        b = MB - OFFS[x]
+        pr = [(T.Ms[x::16, b:b + WC], T.Mt[:, 0:256])]
+        n = min(OFFS[x], 256)
+        if n:
+            pr.append((T.Ms[x::16, b + WC:b + WC + n], T.Mt[0::16, 0:n]))
+        if OFFS[x] > n:
+            pr.append((T.Ms[x::16, b + WC + n:MB + WC], T.Mt[1::16, 0:OFFS[x] - n]))
+        return pr
+    dma("sp", first(0) + first(3), [MSK[0], MSK[3]], [R("Mt", 0, 256), R("Ms")], 2400)
+    dma("act", first(1) + first(2), MSK[1:3], [R("Mt", 0, 256), R("Ms")], 2400)
+
+    lv(0, "yc")
+    for q in range(8):
+        mm([(ps(0, 0, 256), EX(h, "BY"), R("Ct", 256 * h, 256 * h + 256)) for h in (2 * q, 2 * q + 1)], start=q == 0, stop=q == 7)
+    act(R("yco"), ps(0, 0, 256), AF.Copy)
+    dma("sp", [(T.K[0::16, 0:WC], T.yco[:])], [R("K")], [R("yco")], 2400)
 
     def route(r):
-        ts(R("Si"), R("Sa"), 65280, A.bitwise_and)
-        cp(R("Sf"), R("Si"))
+        src = [R("Sb")] + ([R("ycl")] if r else [])
+        for i, v in enumerate(src):
+            mm([(ps(7, 0, NS), R("STA"), v)], start=i == 0, stop=i == len(src) - 1)
+        act(R("sg"), ps(7, 0, NS), AF.Sign, bias=bsg)
+        if r < RO:
+            mm([(ps(7, NS, 2 * NS), R("HM"), R("sg"))])
+        pX = ps(2, 0, NS)
+        mm([(pX, R("ST"), v) for v in src] + [(pX, R("WR"), R("sg"))])
         if r == RO:
+            act(R("yxo"), pX, AF.Copy, scale=1.0 / 256)
             return None
-        ts(R("Hh"), R("Si"), C(7), A.is_lt)
-        scan(R("cum"), R("Hh"), R("CAP"), C(10), A.add, A.min)
-        tt(R("P"), R("Hh"), R("cum"), A.mult)
+        act(R("Sf"), pX, AF.Copy)
+        scan(R("cum"), ps(7, NS, 2 * NS), R("CAP"), init, A.add, A.min)
+        tt(R("P"), ps(7, NS, 2 * NS), R("cum"), A.mult)
         mm([(ps(7, 448, 460), EX(rho), R("P", rho, NS, 16)) for rho in range(16)])
         d = R("dst", 16 * r, 16 * r + 12)
         cp(d, ps(7, 448, 460))
-        act(R("Sg", NS * r, NS * r + NS), R("P"), AF.Sign, bias=-63.5)
         w = R("Zs", 768 * r, 768 * r + 768)
         tt(IND(w, d), R("Tf"), R("Sf"), A.add)
         b = 768 * r
-        op = exchange("fw%d" % r, lambda o: T.Zs[:, b + 192 * o:b + 192 * o + 64], T.Zr[:, NL * r + 64 * me:NL * r + 64 * me + 64],
-                      "Zin%d" % r, [w] + ([R("Yb")] if r == 0 else []), [o for o in range(N) if o != me])
-        act(R("Zr", NL * r + 64 * me, NL * r + 64 * me + 64), R("Zs", b + 192 * me, b + 192 * me + 64), AF.Copy)
+        op = exchange("fw%d" % r, lambda o: T.Zs[:, b + 192 * o:b + 192 * o + 64],
+                      lambda o: T.Zr[:, NL * r + 64 * place(me, o):NL * r + 64 * place(me, o) + 64],
+                      "Zin%d" % r, [w, R("Yb") if r == 0 else R("Yg", NS * (r - 1), NS * r)], [o for o in range(N) if o != me])
+        act(R("Zr", NL * r + 192, NL * r + 256), R("Zs", b + 192 * me, b + 192 * me + 64), AF.Copy)
+        lv(max(r - 1, 0), "late")
+        act(R("Sb"), pX, AF.Copy)
+        act(R("Sg", NS * r, NS * r + NS), R("P"), AF.Sign, bias=-63.5)
         return op
 
-    ts(R("X0b"), R("X0"), 256.0, A.mult)
-    mm([(ps(7, 0, NS), R("ST"), R("X0b"))])
-    ts(R("Sa"), ps(7, 0, NS), C(13), A.add)
-    first = route(0)
+    lv(0, "r0")
+    ts(R("Sb"), R("X0"), 256.0, A.mult)
+    sent0 = route(0)
     level[0] = None
     for r in range(1, RO):
         for o in range(N):
-            fill(R("Zs", 768 * r + 192 * o, 768 * r + 192 * o + 64), 0)["after"] = [first]
-    fill(R("c128"), 128)["after"] = [first]
-    for k in range(4):
-        fill(R("F2", 1036 * k, 1036 * k + 1036), 128)["after"] = [first]
+            fill(R("Zs", 768 * r + 192 * o, 768 * r + 192 * o + 64), 0)["after"] = [sent0]
 
+    if OPT["pf_early"]:
+        pairs_of(0, OPT["pf_banks"])
     for r in range(RO):
         last = r == RO - 1
+        UA = OPT["u_act_last" if last else "u_act"]
         Z = R("Zr", NL * r, NL * r + NL)
         zin = [X("Zin%d" % r)]
-        Vb = R("V", 0, 256)
+        V = R("V")
         lv(r, "v")
-        act(Vb, Z, AF.Identity, bias=159.5005, scale=1.0 / 1024, more=zin)
-        act(R("V", 256, 512), Z, AF.Identity, bias=159.7505, scale=1.0 / 1024, more=zin)
+        act(V, Z, AF.Identity, bias=159.5005, scale=1.0 / 1024, more=zin)
 
-        def sel(o, nm, c0, c1):
-            return [(o, win(nm, 12 - 4 * l), R("V", c0 + l, c1, 4)) for l in range(4)]
-        mm(sel(ps(0, 0, 64), "H1", 0, 256))
-        mm([(ps(1, 0, 64), R("I16"), R("CBt", 0, 64))] + sel(ps(1, 0, 64), "H2", 0, 256))
-        mm([(ps(1, 64, 128), I, R("CL", 0, 64))] + sel(ps(1, 64, 128), "H3", 0, 256))
-        ts(R("PA", 0, 64), ps(0, 0, 64), C(28), A.add)
+        def sel(o, nm):
+            return [(o, win(nm, 12 - 4 * l), R("V", l, 256, 4)) for l in range(4)]
+        mm(sel(ps(0, 0, 64), "H1"))
+        mm([(ps(1, 0, 64), I, R("CB", 0, 64))] + sel(ps(1, 0, 64), "H2"))
+        mm([(ps(1, 64, 128), I, R("CL", 0, 64))] + sel(ps(1, 64, 128), "H3"))
+        if OPT["pa_act"]:
+            af(R("PA", 0, 64), ps(0, 0, 64), None, aCol)
+        else:
+            ts(R("PA", 0, 64), ps(0, 0, 64), aCol, A.add)
         tt(R("pr", 0, 64), R("PA", 0, 64), ps(1, 0, 64), A.mult)
         tt(R("vi", 0, 64), R("pr", 0, 64), ps(1, 64, 128), A.add)
-        ts(R("hm", 0, 64), R("vi", 0, 64), 2, A.arith_shift_right, 4095, A.bitwise_and)
+        ts(R("hm", 0, 64), R("vi", 0, 64), 2, sh, 4095, an)
         cp(R("om"), R("hm", 0, 64))
-        Mw = R("Ms")
         act(R("G", 0, 16 * MS), IND(Mw, R("om", 0, MS)), AF.Copy, more=MSK)
         lv(r, "g2")
         if MS < 64:
             cp(R("G", 16 * MS, 1024), IND(Mw, R("om", MS, 64)), more=MSK)
         lv(r, "rest")
-        mm([(ps(2, 64, 256), I, R("CA", 64, 256))] + sel(ps(2, 64, 128), "H1", 256, 512) + sel(ps(2, 128, 256), "H4", 0, 512))
-        act(R("PA", 64, 256), ps(2, 64, 256), AF.Copy)
-        mm([(ps(5, 64, 256), R("I16"), R("CBt", 64, 256))] + sel(ps(5, 64, 128), "H2", 256, 512) + sel(ps(5, 128, 256), "H5", 0, 512))
-        mm([(ps(5, 320, 512), I, R("CL", 64, 256))] + sel(ps(5, 320, 384), "H3", 256, 512) + sel(ps(5, 384, 512), "H6", 0, 512))
-        mm(sel(ps(2, 256, 320), "HD", 0, 256))
-        tt(R("pr", 64, 256), R("PA", 64, 256), ps(5, 64, 256), A.mult)
-        tt(R("vi", 64, 256), R("pr", 64, 256), ps(5, 320, 512), A.add)
-        ts(R("hm", 128, 256), R("vi", 128, 256), 4080, A.bitwise_and)
-        ts(R("hm", 64, 128), R("vi", 64, 128), 2, A.arith_shift_right, 4095, A.bitwise_and)
-        cp(R("hb", 0, 64), R("hm", 128, 192))
+        mm(sel(ps(2, 0, 64), "HA") + sel(ps(2, 64, 128), "H4"))
+        af(R("PA", 128, 192), ps(2, 64, 128), None, aBlk)
+        af(R("PA", 64, 128), ps(2, 0, 64), None, aBest)
+        mm([(ps(5, 0, 128), I, R("CB", 64, 192))] + sel(ps(5, 0, 64), "HB") + sel(ps(5, 64, 128), "H5"))
+        mm([(ps(5, 128, 256), I, R("CL", 64, 192))] + sel(ps(5, 128, 192), "HL") + sel(ps(5, 192, 256), "H6"))
+        mm(sel(ps(5, 256, 320), "HD"))
+        tt(R("pr", 64, 192), R("PA", 64, 192), ps(5, 0, 128), A.mult)
+        tt(R("vi", 64, 192), R("pr", 64, 192), ps(5, 128, 256), A.add)
+        ts(R("hn", 64, 192), R("vi", 64, 192), 4080, an)
+        cp(R("hb0"), R("hn", 128, 192))
         for k in range(1, 4):
-            ts(R("hb", 64 * k, 64 * k + 64), R("hm", 128, 192), 4096.0 - 16 * CB01[k], A.is_ge, -4096.0, A.mult)
-        tt(R("ks"), R("hm", 64, 128), ps(2, 256, 320), A.add)
-        tt(R("kb"), R("hm", 192, 256), ps(2, 256, 320), A.add)
-        lv(r, "ou")
-        for k in range(4):
-            ts(R("ou", 64 * k, 64 * k + 64), R("hm", 192, 256), C(4), A.add, 4.0 * k, A.add)
-        lv(r, "w")
-        mm([(ps(6, 0, 256), win("W1", 12), Vb), (ps(6, 0, 256), win("W2", 8), Vb)])
-        mm([(ps(6, 256, 512), win("W3", 12), Vb), (ps(6, 256, 512), win("W4", 8), Vb)])
-        af(R("fa"), ps(6, 0, 256), C(24), C(25))
-        af(R("fb"), ps(6, 256, 512), C(26), C(27))
-        tt(R("Wp"), R("fa"), R("fb"), A.mult)
-        pW = R("pw")
-        for h in range(2):
-            mm([(ps(3 + h, x, 512, 4), SEL(x), R("Wp", 128 * h, 128 * h + 128)) for x in range(4)], each=True)
-        for n2, h in enumerate((1 - me // 2, me // 2)):
-            if any(4 * n2 + k not in FA for k in range(4)):
-                act(R("Wcd", 512 * h, 512 * h + 512), ps(3 + h, 0, 512), AF.Copy)
-        lv(r, "wab")
-        for h in range(2):
-            mm([(ps(h, 256 * k, 256 * k + 256), SEL(4 + 2 * h + k), R("Wp")) for k in range(2)], each=True)
-            act(R("Wab", 512 * h, 512 * h + 512), ps(h, 0, 512), AF.Copy)
+            if OPT["hb_act"]:
+                act(R("hbs", 64 * k - 64, 64 * k), R("hb0"), AF.Sign, bias=16.0 * CB01[k] - 4088.0)
+            else:
+                ts(R("hbs", 64 * k - 64, 64 * k), R("hn", 128, 192), 4096.0 - 16 * CB01[k], A.is_ge, -4096.0, A.mult)
         lv(r, "kc")
-        mm([(ps(1, 0, 16), win("Bt32", 12 - 4 * a), R("ks", a, 64, 4)) for a in range(4)])
-        ts(R("kc16", 0, 16), ps(1, 0, 16), 4096.0, A.add)
-        ts(R("kc", 0, 16), ps(1, 0, 16), 4096.0, A.add, 1.0 / 8192, A.mult)
+        ts(R("em"), ps(5, 256, 320), 2048.0, A.add, -2048.0, A.max)
+        ts(R("hm", 64, 128), R("vi", 64, 128), 2, sh, 4095, an)
+        tt(R("ks"), R("hm", 64, 128), R("em"), A.add)
+        tt(R("kb"), R("hn", 64, 128), R("em"), A.add)
+        lv(r, "w")
+        mm([(ps(6, 0, 256), R("WA"), V)])
+        mm([(ps(6, 256, 512), R("DC"), R("c128")), (ps(6, 256, 512), R("WB"), V)])
+        af(R("fa"), ps(6, 0, 256), fs, fb)
+        tt(R("Wp"), R("fa"), ps(6, 256, 512), A.mult)
+        for h in range(2):
+            lv(r, "w%d" % h)
+            mm([(ps(3 + h, x, 512, 4), SEL(x), R("Wp", 128 * h, 128 * h + 128)) for x in range(4)], each=True)
+            lv(r, "wab%d" % h)
+            if h:
+                mm([(ps(7, 256 * q + 64 * k, 256 * q + 64 * k + 64), SEL(4 + k), R("Wp", 128 + 64 * q, 192 + 64 * q))
+                    for q in range(2) for k in range(4)], each=True)
+            else:
+                mm([(ps(0, 128 * k, 128 * k + 128), SEL(4 + k), R("Wp", 0, 128)) for k in range(4)], each=True)
+            if h in OPT["wab_dve"]:
+                cp(R("Wab", 512 * h, 512 * h + 512), ps(7 * h, 0, 512))
+            else:
+                act(R("Wab", 512 * h, 512 * h + 512), ps(7 * h, 0, 512), AF.Copy)
+        lv(r, "kc")
+        mm([(ps(1, 128, 144), win("Bt1s", 12 - 4 * a), R("kb", a, 64, 4)) for a in range(4)]
+           + [(ps(1, 144, 160), win("Bt", 12 - 4 * a), R("ks", a, 64, 4)) for a in range(4)])
+        kc, bl, kf = R("kl", 0, 16), R("kl", 16, 32), R("kl", 32, 48)
+        ts(kc, ps(1, 144, 160), 2048.0, A.add)
+        ts(bl, ps(1, 128, 144), 128.0, A.add, 255.0, A.min)
         lv(r, "of")
-        mm([(ps(2, 0, 256), I, R("CO")), (ps(2, 64, 256), I, R("hb", 64, 256))]
-           + [(ps(2, 64 * k, 64 * k + 64), I, R("hb", 0, 64)) for k in range(4)], stop=False)
-        mm([(ps(2, 64 * k, 64 * k + 64), win("Bd", 12 - 4 * l), R("G", 4 * l + k, 1024, 16)) for k in range(4) for l in range(4)],
+        mm([(ps(2, 256, 512), I, R("CO")), (ps(2, 320, 512), R("N2048") if OPT["hb_act"] else I, R("hbs"))]
+           + [(ps(2, 256 + 64 * k, 320 + 64 * k), I, R("hb0")) for k in range(4)], stop=False)
+        mm([(ps(2, 256 + 64 * k, 320 + 64 * k), win("Bd", 12 - 4 * l), R("G", 4 * l + k, 1024, 16)) for k in range(4) for l in range(4)],
            start=False)
-        cp(R("of"), ps(2, 0, 256))
+        cp(R("of"), ps(2, 256, 512))
         Fw = R("Ft")
         lv(r, "keys")
-        act(R("MsG"), IND(Mw, R("kc16", 0, 16)), AF.Copy, more=MSK)
-        af(R("MsM"), R("MsG"), O(0))
-        lv(r, "cold")
-        act(R("Cold"), IND(R("Ct"), R("kc16", 0, 16)), AF.Copy)
-        lv(r, "keys")
-        for l in range(4):
-            mm([(ps(0, 128 * l, 128 * l + 64), R("Sel32", 128 * l, 128 * l + 128), R("ks"))])
-            o = ps(0, 128 * l + 64, 128 * l + 128)
-            mm([(o, SEL(4 * l), R("kb")), (o, SEL(0), R("MsG", l, 256, 4))])
-        act(R("krow"), ps(0, 0, 512), AF.Identity, bias=0.5, scale=1.0 / 8192)
-        o = ps(1, 16, 32)
-        mm([(o, win("Bt", 12 - 4 * a), R("kb", a, 64, 4)) for a in range(4)] + [(o, EX(rho), R("MsM", rho, 256, 16)) for rho in range(16)])
-        ts(R("kc16", 16, 32), o, 4096.0, A.add)
-        ts(R("kc", 16, 32), o, 4096.0, A.add, 1.0 / 8192, A.mult)
+        if OPT["cm_act"]:
+            act(R("CMg"), IND(Mw, kc), AF.Copy, more=MSK)
+        else:
+            cp(R("CMg"), IND(Mw, kc), more=MSK)
+        o = ps(1, 160, 176)
+        mm([(o, win("Bt1", 12 - 4 * a), R("kb", a, 64, 4)) for a in range(4)]
+           + [(o, EX(rho, "EX0"), R("CMg", rho, 256, 16)) for rho in range(16)])
+        ts(R("Kh"), ps(1, 144, 176), 1.0 / 64, A.mult)
+        ts(kf, o, 2048.0, A.add)
         lv(r, "fold")
-        act(R("Fold"), IND(Fw, R("kc16", 16, 32)), AF.Copy)
+        act(R("Fold"), IND(Fw, kf), AF.Copy)
+        lv(r, "cold")
         if last:
-            dma("pool", [(T.F2[:, 2048 * h:2048 * h + 2048], T.Ft[:, 2048 * h:2048 * h + 2048]) for h in range(2)], [R("F2")],
-                [R("Ft"), R("of")], 6000, acc=True)
+            act(R("ycg"), IND(R("K"), kc), AF.Copy, more=[X("Ky")])
+        else:
+            act(R("Cold"), IND(R("Ct"), kc), AF.Copy)
+            if r:
+                ts(R("Hd"), R("CMg"), R16, A.add, -R16, A.add)
         lv(r, "e")
-        for h in range(2):
-            tt(R("E", 512 * h, 512 * h + 512), IND(R("kc"), R("EL", 32 * h, 32 * h + 32)), R("krow"), A.is_equal)
-        o = ps(1, 32, 64)
-        it = []
-        for rho in range(16):
-            s = 128 * (rho % 4) + rho // 4
-            it.append((o, R("TR", 128 * rho, 128 * rho + 128), R("E", s, s - rho // 4 + 128, 4)))
-        mm(it, stop=False)
-        it = []
-        for rho in range(16):
-            s = 128 * (rho % 4) + rho // 4
-            it.append((o, EX(rho), R("E", 512 + s, 512 + s - rho // 4 + 128, 4)))
-        mm(it, start=False)
-        tt(R("x1"), o, R("kc", 0, 32), A.add)
-        tt(R("x2"), R("x1"), R("dum"), A.min)
-        ts(R("so"), R("x2"), 8192.0, A.mult)
-        lv(r, "f")
-        yb = NL * r
-        Y = R("Ys", yb, yb + NL)
-        for n2, h in enumerate((1 - me // 2, me // 2)):
-            pY = ps(2, 256 + 128 * h, 384 + 128 * h)
-            lv(r, "f2nd" if n2 else "f")
-            mm([(pY, I, R("cy", 0, 128))], stop=False)
-            for k in range(4):
-                lst = R("of", 64 * k + 32 * h, 64 * k + 32 * h + 32)
-                b = 1024 * k + 512 * h
-                pS = ps(5 + k % 2, 128 * n2, 128 * n2 + 128)
-                if 4 * n2 + k in FA:
-                    act(R("Vg", b, b + 512), IND(Fw, lst), AF.Copy)
-                    tt(R("Vp", b, b + 512), R("Vg", b, b + 512), ps(3 + h, 0, 512), A.mult)
-                else:
-                    tt(R("Vp", b, b + 512), IND(Fw, lst), R("Wcd", 512 * h, 512 * h + 512), A.mult)
-                mm([(pS, R("I16"), R("Vp", b + x, b + 512, 4)) for x in range(4)])
-                c = 256 * k + 128 * h
-                tt(R("SW", c, c + 128), pS, R("Wab", c, c + 128), A.mult)
-                mm([(pY, R("I32"), R("SW", c, c + 128))], start=False, stop=k == 3)
-            Yh = R("Ys", yb + 128 * h, yb + 128 * h + 128)
-            ts(Yh, pY, 3221225472.0, A.add, -3221225472.0, A.add)
-            exchange("bk%d" % r, lambda o, yb=yb: T.Ys[:, yb + 64 * o:yb + 64 * o + 64], T.Yb[:, 192 * me:192 * me + 64],
-                     "Yin%d%d" % (r, n2), [Yh], [o for o in (2 * h, 2 * h + 1) if o != me])
+        for q in range(4):
+            if OPT["dm"]:
+                mm([(ps(2, 15 - x, 512, 16), R("DM", 128 * x, 128 * x + 128), R("Kh")) for x in range(4 * q, 4 * q + 4)], each=True)
+            else:
+                mm([(ps(2, 15 - x, 512, 16), m, R("Kh")) for x in range(4 * q, 4 * q + 4) for m in (SEL(x), R("NI"))],
+                   start=q == 0, stop=q == 3)
+        scan(R("Z0"), ps(2, 0, 512), R("RS0"), 1.0, A.mult, A.add)
+        mm([(ps(1, 176, 448, 17), I, R("RS1", 1, 17))], stop=False)
+        for q in range(4):
+            it = []
+            for x in range(4 * q, 4 * q + 4):
+                o = ps(1, 177 + x, 448, 17)
+                it += [(o, SEL(x), R("Kh", 0, 32, 2)), (o, R("NI"), R("Kh", 1, 32, 2))]
+            mm(it, start=False, stop=q == 3)
+        scan(R("Z1"), ps(1, 176, 448), R("RS1"), 1.0, A.mult, A.add)
+        ts(R("fl", 0, 32), R("Z0", 15, 512, 16), 0.0, A.is_equal, 8192.0, A.mult)
+        ts(R("fl", 32, 48), R("Z1", 16, 272, 17), 0.0, A.is_equal, 8192.0, A.mult)
+        mm([(ps(1, 448, 480), R("I64"), R("Kh")), (ps(1, 448, 480), I, R("fl", 0, 32)), (ps(1, 449, 480, 2), I, R("fl", 32, 48))])
+        ts(R("so", 0, 32, 2, key="soE"), ps(1, 448, 480, 2), 2048.0, A.add, spE, A.min)
+        ts(R("so", 1, 32, 2, key="soO"), ps(1, 449, 480, 2), 2048.0, A.add, spO, A.min)
+        SO = [R("so", key="soE"), R("so", key="soO")]
+        if r == 0 and not OPT["pf_early"]:
+            pairs_of(0, (2, 1, 2, 1))
+
+        def train(n2, h):
             c = 128 * h
+
+            def H(name):
+                return R(name, c, c + 128)
+            lv(r, "fn%d" % n2)
+            o = ps(3 + n2, 0, 128)
+            mm([(o, I, H("Fold")), (o, I, H("gs"))])
+            ts(H("Fnew"), o, 0.0, A.max, 255.0, A.min)
+            lv(r, "u%d" % n2)
+            b = 5 + n2
+            if any(2 * n2 + q in UA for q in range(2)):
+                mm([(ps(3 + n2, 128 * x, 128 * x + 128), I, H("gs")) for x in range(4)], each=True)
+            if not last:
+                o = ps(b, 256, 384)
+                mm([(o, H("Cold"), I)] + ([(o, H("CMg"), R("U1")), (o, H("Hd"), R("U2"))] if r else []))
+            mm([(ps(b, 0, 128), H("gs"), R("GB"))], stop=False)
+            for q in range(2):
+                u0 = 1024 * h + 512 * q
+                for jj in range(4 * q, 4 * q + 4):
+                    w = IND(R("PF%d" % (r % 2), 256 * jj, 256 * jj + 256), R("kl", 16 + 8 * h, 24 + 8 * h))
+                    up = R("Up", 1024 * h + 128 * jj, 1024 * h + 128 * jj + 128)
+                    if 2 * n2 + q in UA:
+                        lv(r, "ug%d" % n2)
+                        act(R("Ug", up["c0"], up["c1"]), w, AF.Copy)
+                    else:
+                        tt(up, w, H("gs"), A.mult)
+                        mm([(ps(b, jj, 128, 8), up, R("BB"))], start=False, stop=jj == 7)
+                lv(r, "u%d" % n2)
+                if 2 * n2 + q in UA:
+                    tt(R("Up", u0, u0 + 512), R("Ug", u0, u0 + 512), ps(3 + n2, 0, 512), A.mult)
+                    mm([(ps(b, 4 * q + x, 128, 8), R("Up", u0 + 128 * x, u0 + 128 * x + 128), R("BB")) for x in range(4)],
+                       start=False, stop=q == 1)
+            lv(r, "x%d" % n2)
+            r32 = R("R32", 64 * h, 64 * h + 64)
+            ts(r32, ps(b, 0, 64), R8192, A.add, -R8192, A.add)
+            tt(R("Xs", c, c + 128, 2, key="XsE"), ps(b, 0, 64), r32, A.subtract)
+            ts(R("Xs", c + 1, c + 128, 2, key="XsO"), ps(b, 64, 128), R8192, A.add, -R8192, A.add)
+            xs, xo = R("Xs", c, c + 128, key="XsE"), [R("Xs", c, c + 128, key="XsO")]
+            if last:
+                mm([(ps(b, 128, 256), xs, I)], more=xo)
+                act(H("us"), ps(b, 128, 256), AF.Sign)
+                mm([(ps(b, 256, 384), EX(0, "BY"), H("us"))])
+                act(H("d3"), ps(b, 256, 384), AF.Copy)
+                return
+            ts(H("ut"), xs, -1.0, A.max, 1.0, A.min, more=xo)
+            tt(H("key"), ps(b, 256, 384), H("ut"), A.add)
+            scan(H("Km"), R("D0", 0, 128), H("key"), 0.0, A.add, A.max)
+            ki, mi = R("ki", 8 * h, 8 * h + 8), R("mi", 8 * h, 8 * h + 8)
+            ts(ki, R("Km", c + 15, c + 128, 16), 16.0, A.mult)
+            ts(mi, ki, 15, an)
+            ts(R("Mx", c, c + 128, 16), mi, -1.0, A.mult, 15.0, A.add)
+            lv(r, "us%d" % n2)
+            mm([(ps(3 + n2, 0, 128), H("ut"), I)])
+            act(H("us"), ps(3 + n2, 0, 128), AF.Copy)
+            o = ps(b, 384, 512)
+            mm([(o, R("KP"), H("CMg")), (o, R("PK"), H("us"))], stop=False)
+            mm([(o, H("Mx"), I)], start=False)
+            act(H("CMn"), o, AF.Copy)
+        def train_all():
+            gs = R("gs")
+            lv(r, "fn0")
+            o = ps(3, 0, 256)
+            mm([(o, I, R("Fold")), (o, I, gs)])
+            ts(R("Fnew"), o, 0.0, A.max, 255.0, A.min)
+            lv(r, "u1")
+            if UA:
+                mm([(ps(4, 256 * x, 256 * x + 256), I, gs) for x in range(2)], each=True)
+            lv(r, "c0")
+            if not last:
+                mm([(ps(6, 128 * h, 128 * h + 128), R(a, 128 * h, 128 * h + 128), m) for h in range(2)
+                    for a, m in [("Cold", I)] + ([("CMg", R("U1")), ("Hd", R("U2"))] if r else [])], stop=not OPT["key_pe"])
+            lv(r, "u1")
+            mm([(ps(5, 64 * h, 64 * h + 64), I, R("GB", 0, 64)) for h in range(2)]
+               + [(ps(5, 128 + 64 * h, 192 + 64 * h), R("gs", 128 * h, 128 * h + 128), R("GB", 64, 128)) for h in range(2)], stop=False)
+            for q in range(4):
+                for jj in (2 * q, 2 * q + 1):
+                    w = IND(R("PF%d" % (r % 2), 256 * jj, 256 * jj + 256), bl)
+                    if q in UA:
+                        lv(r, "ug1")
+                        act(R("Ug", 256 * jj, 256 * jj + 256), w, AF.Copy)
+                    else:
+                        tt(R("Up", 256 * jj, 256 * jj + 256), w, gs, A.mult)
+                lv(r, "u1")
+                if q in UA:
+                    tt(R("Up", 512 * q, 512 * q + 512), R("Ug", 512 * q, 512 * q + 512), ps(4, 0, 512), A.mult)
+                mm([(ps(5, 64 * h + jj, 64 * h + jj + 185, 8), R("Up", 256 * jj + 128 * h, 256 * jj + 128 * h + 128), R("BB"))
+                    for jj in (2 * q, 2 * q + 1) for h in range(2)], start=False, stop=q == 3)
+            lv(r, "x1")
+            ts(R("R32"), ps(5, 0, 128), R8192, A.add, -R8192, A.add)
+            tt(R("Xs", 0, 256, 2, key="XsE"), ps(5, 0, 128), R("R32"), A.subtract)
+            ts(R("Xs", 1, 256, 2, key="XsO"), ps(5, 128, 256), R8192, A.add, -R8192, A.add)
+            xo = [R("Xs", key="XsO")]
+            if last:
+                mm([(ps(3, 128 * h, 128 * h + 128), R("Xs", 128 * h, 128 * h + 128, key="XsE"), I) for h in range(2)], more=xo, each=True)
+                act(R("us"), ps(3, 0, 256), AF.Sign)
+                mm([(ps(6, 0, 256), EX(0, "BY"), R("us"))])
+                act(R("d3"), ps(6, 0, 256), AF.Copy)
+                return
+            ts(R("ut"), R("Xs", key="XsE"), -1.0, A.max, 1.0, A.min, more=xo)
+            if OPT["key_pe"]:
+                mm([(ps(6, 0, 256), I, R("ut"))], start=False)
+                scan(R("Km"), R("D0", 0, 256), ps(6, 0, 256), 0.0, A.add, A.max)
+            else:
+                tt(R("key"), ps(6, 0, 256), R("ut"), A.add)
+                scan(R("Km"), R("D0", 0, 256), R("key"), 0.0, A.add, A.max)
+            ki, mi = R("ki", 0, 16), R("mi", 0, 16)
+            ts(ki, R("Km", 15, 256, 16), 16.0, A.mult)
+            ts(mi, ki, 15, an)
+            ts(R("Mx", 0, 256, 16), mi, -1.0, A.mult, 15.0, A.add)
+            lv(r, "us1")
+            mm([(ps(3, 128 * h, 128 * h + 128), R("ut", 128 * h, 128 * h + 128), I) for h in range(2)], each=True)
+            act(R("us"), ps(3, 0, 256), AF.Copy)
+            o = ps(5, 256, 512)
+            mm([(o, R("KP"), R("CMg")), (o, R("PK"), R("us"))], stop=False)
+            mm([(ps(5, 256 + 128 * h, 384 + 128 * h), R("Mx", 128 * h, 128 * h + 128), I) for h in range(2)], start=False)
+            act(R("CMn"), o, AF.Copy)
+        yb = NL * r
+        Y = {}
+        for n3, (l0, n) in enumerate(((0, 128), (128, 64), (192, 64))):
+            n2, c0 = l0 // 128, l0 % 128
+            pY = ps(0, l0, l0 + n)
+            lv(r, "f%d" % n3)
+            for k0, k1 in OPT["sw"][n3]:
+                for k in range(k0, k1):
+                    lst = R("of", 64 * k + l0 // 4, 64 * k + (l0 + n) // 4)
+                    b = 16 * l0 + 4 * n * k
+                    vg, vp = R("Vg", b, b + 4 * n), R("Vp", b, b + 4 * n)
+                    if 4 * n3 + k in OPT["f_dve"]:
+                        ts(vg, IND(Fw, lst), -128.0, A.add)
+                    else:
+                        af(vg, IND(Fw, lst), None, -128.0)
+                    tt(vp, vg, ps(3 + n2, 4 * c0, 4 * c0 + 4 * n), A.mult)
+                    mm([(ps(5 + n2, 4 * c0 + n * k, 4 * c0 + n * k + n), I, R("Vp", b + x, b + 4 * n, 4)) for x in range(4)])
+                c = 4 * l0
+                tt(R("SW", c + n * k0, c + n * k1), ps(5 + n2, 4 * c0 + n * k0, 4 * c0 + n * k1), R("Wab", c + n * k0, c + n * k1), A.mult)
+                mm(([(pY, I, R("cy", 0, n))] if k0 == 0 else [])
+                   + [(pY, R("I32"), R("SW", c + n * k, c + n * k + n)) for k in range(k0, k1)], start=k0 == 0, stop=k1 == 4)
+            Y[n3] = R("Yb", 192 * me, 192 * me + 64) if n3 == 2 else R("Ys", yb + l0, yb + l0 + n)
+            ts(Y[n3], pY, R256, A.add, -R256, A.add)
+            if n3 < 2:
+                exchange("bk%d" % r, lambda o, yb=yb: T.Ys[:, yb + 64 * place(o, me):yb + 64 * place(o, me) + 64],
+                         lambda o: T.Yb[:, 192 * me:192 * me + 64], "Yin%d%d" % (r, n3), [Y[n3]],
+                         [o for o in range(N) if place(o, me) == 2] if n3 else [o for o in range(N) if place(o, me) < 2])
+            if OPT["merge"] and n3 == 2:
+                pD = ps(7, 0, 256)
+                lv(r, "t1")
+                mm([(pD, R("I32"), Z), (pD, R("TT"), V)], stop=False, more=zin)
+                lv(r, "g1")
+                mm([(ps(7, 0, 128), R("N256"), Y[0]), (ps(7, 128, 192), R("N256"), Y[1])], start=False, stop=False)
+                mm([(ps(7, 192, 256), R("N256"), Y[2])], start=False)
+                act(R("gs"), pD, AF.Sign, bias=bG)
+                train_all()
+            if n3 == 1 or OPT["merge"]:
+                continue
+            c = 128 * n2
             pD = ps(7, c, c + 128)
             lv(r, "t%d" % n2)
             mm([(pD, R("I32"), R("Zr", NL * r + c, NL * r + c + 128)), (pD, R("TT"), R("V", c, c + 128))], stop=False, more=zin)
             lv(r, "g%d" % n2)
-            mm([(pD, R("N256"), Yh)], start=False)
-            act(R("gs", c, c + 128), pD, AF.Sign, bias=C(34))
-            mm([(ps(3 + h, x, 512, 4), I, R("gs", c, c + 128)) for x in range(4)], each=True)
-            if any(4 * n2 + k not in UA for k in range(4)):
-                act(R("g4", 512 * h, 512 * h + 512), ps(3 + h, 0, 512), AF.Copy)
-            pU = ps(0, c, c + 128)
-            lv(r, "um%d" % n2)
-            mm([(pU, R("BO128"), R("gs", c, c + 128))], stop=False)
-            for k in range(4):
-                lst = R("ou", 64 * k + 32 * h, 64 * k + 32 * h + 32)
-                b = 1024 * k + 512 * h
-                if 4 * n2 + k in UA:
-                    lv(r, "ug%d" % n2)
-                    act(R("Ug", b, b + 512), IND(Fw, lst), AF.Copy)
-                    lv(r, "um%d" % n2)
-                    tt(R("Up", b, b + 512), R("Ug", b, b + 512), ps(3 + h, 0, 512), A.mult)
-                else:
-                    tt(R("Up", b, b + 512), IND(Fw, lst), R("g4", 512 * h, 512 * h + 512), A.mult)
-                mm([(pU, EX(4 * k + x), R("Up", b + x, b + 512, 4)) for x in range(4)], start=False, stop=k == 3)
-        lv(r, "g1")
-        act(R("Yb", 192 * me, 192 * me + 64), R("Ys", yb + 64 * me, yb + 64 * me + 64), AF.Copy)
-
-        def scatter(name, src, c0, more=()):
-            for t in range(7, -1, -1):
-                cp(IND(R(name), R("so", c0 + 2 * t, c0 + 2 * t + 2)), R(src, 32 * t, 32 * t + 32), more)
-        lv(r, "f2" if last else "fn")
-        o = ps(6, 256, 512)
-        mm([(o, I, R("Fold"))] + ([(o, I, R("c128"))] if last else []) + [(o, I, R("gs"))])
-        if last:
-            ts(R("Fnew"), o, 0.0, A.max, 255.0, A.min)
-            scatter("F2", "Fnew", 16)
-            dma("sp", [(T.yf[:, 2048 * h:2048 * h + 2048], T.F2[:, 2048 * h:2048 * h + 2048]) for h in range(2)], [], [R("F2")], 6000)
-        else:
-            ts(R("Fnew"), o, -128.0, A.max, 127.0, A.min)
-        lv(r, "u")
-        act(R("us"), ps(0, 0, 256), AF.Sign)
-        if not last:
-            o = ps(5, 0, 256)
-            mm([(o, I, R("Cold")), (o, R("NS4"), R("MsG"))], stop=False)
-            mm([(o, I, R("us"))], start=False)
-            act(R("wexp"), o, AF.Exp, bias=C(36), scale=16 * BETA)
-            o = ps(1, 256, 512)
-            mm([(o, R("BO45"), R("wexp"))])
-            act(R("oh"), o, AF.Sign)
-            o = ps(5, 256, 512)
-            mm([(o, EX(4, "BP"), R("MsG")), (o, EX(0, "BJ"), R("oh"))])
-            if OPT["mn_act"]:
-                af(R("Mnew"), o, None, C(41))
+            if n2:
+                mm([(ps(7, 128, 192), R("N256"), Y[1]), (ps(7, 192, 256), R("N256"), Y[2])], start=False)
             else:
-                ts(R("Mnew"), o, C(41), A.add)
+                mm([(pD, R("N256"), Y[0])], start=False)
+            act(R("gs", c, c + 128), pD, AF.Sign, bias=bG)
+            train(n2, n2)
+
+        def scatter(w, src, c0, more=()):
+            for t in [2 * place(q, me) + x for q in range(N - 1, -1, -1) for x in (1, 0)]:
+                o = IND(w, R("so", c0 + 2 * t, c0 + 2 * t + 2, key="sox"))
+                also = SO + list(more) + [R(src[-1])]
+                if len(src) == 1:
+                    cp(o, R(src[0], 32 * t, 32 * t + 32), also)
+                else:
+                    tt(o, R(src[0], 32 * t, 32 * t + 32), R(src[1], 32 * t, 32 * t + 32), A.add, also)
+        lv(r, "fs")
+        scatter(Fw, ["Fnew"], 16)
+        if last:
+            dma("sp", [(T.yf[:, 2048 * h:2048 * h + 2048], T.Ft[:, 2048 * h:2048 * h + 2048]) for h in range(2)], [], [Fw], 6000)
             lv(r, "ms")
-            scatter("Ms", "Mnew", 0, MSK)
+            scatter(R("K"), ["ycg", "d3"], 0, [X("Ky")])
+            dma("sp", [(T.yc[:], T.K[0::16, 0:WC])], [], [R("K")], 2200)
+        else:
+            lv(r, "ms")
+            scatter(Mw, ["CMn"], 0, MSK)
             shift()
-            lv(r, "fs")
-            scatter("Ft", "Fnew", 16)
-        lv(r, "cn")
-        o = ps(6, 0, 256)
-        mm([(o, I, R("Cold")), (o, I, R("us"))])
-        act(R("Cnew"), o, AF.Copy)
-        lv(r, "cn" if last else "cs")
-        scatter("Ct", "Cnew", 0)
-        lv(r, "end" if last else "home")
-        yg = R("Yg", NS * r, NS * r + NS)
-        cp(yg, IND(R("Yb"), R("dst", 16 * r, 16 * r + 12)), more=[X("Yin%d0" % r), X("Yin%d1" % r)])
-        mm([(ps(7, 0, NS), R("ST"), yg)])
-        ts(ps(7, 256, 256 + NS), ps(7, 0, NS), C(15), A.max, C(14), A.min)
-        tt(R("Sa"), ps(7, 256, 256 + NS), R("Sf"), A.add)
+            pairs_of(r + 1, OPT["pf_banks"])
+            lv(r, "yc")
+            if r == 2:
+                for x in (13, 14):
+                    dma("pool", [(T.K[0::16, 2048 * h:2048 * h + 2048], T.Ms[x::16, MB + 2048 * h:MB + 2048 * h + 2048]) for h in range(2)],
+                        [R("K"), X("Ky")], [R("Ms")], 3500, acc=True)
+        lv(r, "home")
+        yin = [X("Yin%d0" % r), X("Yin%d1" % r)]
+        d = IND(R("Yb"), R("dst", 16 * r, 16 * r + 12))
+        ts(R("ycl"), d, -2048.0, A.max, 2048.0, A.min, more=yin)
+        act(R("Yg", NS * r, NS * r + NS), d, AF.Copy, more=yin)
         route(r + 1)
 
-    act(R("yxo"), R("Sf"), AF.Copy, scale=1.0 / 256)
     dma("sp", [(T.yx[e::4, :], T.yxo[e::16, :]) for e in range(4)], [], [R("yxo")], 2200)
-    o = ps(7, 0, NS)
+    o = ps(7, 256, 256 + NS)
     mm([(o, R("YW"), R("Sg", NS * r, NS * r + NS)) for r in range(RO)] + [(o, R("I256"), R("Yg", NS * r, NS * r + NS)) for r in range(RO)])
     af(R("yso"), o, None, -512.0)
     dma("sp", [(T.ys[:], T.yso[:])], [], [R("yso")], 2200)
-    lv(RO - 1, "cn")
-    o = ps(5, 0, 256)
-    mm([(o, EX(h, "BY"), R("Ct", 256 * h, 256 * h + 256)) for h in range(16)])
-    act(R("yco"), o, AF.Copy)
-    dma("act", [(T.yc[:], T.yco[:])], [], [R("yco")], 2200)
     return ops
 
 
@@ -722,8 +885,7 @@ def depend(ops):
                 b[1].append(i)
             for j, c0, c1, jw in h:
                 if (w or jw) and c0 < v["c1"] and v["c0"] < c1:
-                    same = ops[j]["eng"] == e and ops[j]["sem"] is None and op["sem"] is None
-                    if same and (e == "pe" or (OPT["inorder"] and w)):
+                    if e == "pe" and ops[j]["eng"] == e:
                         dep.add(j)
                     else:
                         wait.add(j)
@@ -744,7 +906,9 @@ def price(ops, p):
         f = p["fa"] if op["eng"] == "act" else p["fv"]
         if k == "el":
             c = f + max(n, 32 if op["eng"] == "act" else 64) * p["cyc"]
-        elif k in ("gat", "sca", "tt2"):
+        elif k in ("gat", "sca"):
+            c = f + n * p[k] * p["cyc"]
+        elif k == "tt2":
             c = f + max(64, n * p[k]) * p["cyc"]
         elif k == "mm":
             c = n * p["pe"]
@@ -762,85 +926,184 @@ def gap(ops, j, i, p):
     return p["same"] if ops[j]["eng"] == ops[i]["eng"] and ops[j]["lat"] is None else p["hop"]
 
 
-def schedule(ops, p, seed, noise):
+def schedule(ops, p, others=()):
     n = len(ops)
     price(ops, p)
+    cost = [op["cost"] for op in ops]
+    eng = [op["eng"] for op in ops]
+    pred = [[(j, ops[j]["l"] + gap(ops, j, i, p)) for j in op["dep"]] for i, op in enumerate(ops)]
     succ = [[] for _ in range(n)]
-    for i, op in enumerate(ops):
-        for j in op["dep"]:
-            succ[j].append(i)
+    for i in range(n):
+        for j, d in pred[i]:
+            succ[j].append((i, d))
     tail = [0.0] * n
     lev = [0.0] * n
-    rnd = np.random.RandomState(seed).standard_normal(n)
     for i in range(n - 1, -1, -1):
-        op = ops[i]
-        tail[i] = op["cost"] + op["l"] + max([gap(ops, i, k, p) + tail[k] for k in succ[i]] + [0])
-        if op["lv"] is None:
-            lev[i] = min([lev[k] for k in succ[i]] + [1e4])
+        tail[i] = cost[i] + max([d + tail[k] for k, d in succ[i]] + [ops[i]["l"]])
+        if ops[i]["lv"] is None:
+            lev[i] = min([lev[k] for k, d in succ[i]] + [1e4])
         else:
-            lev[i] = 100 * op["lv"][0] + LEVEL[op["lv"][1]] + SHIFT.get(op["tag"], 0)
-            if op["lv"][0] == RO - 1:
-                lev[i] += LEVEL.get(op["lv"][1] + "L", 0)
+            r, name = ops[i]["lv"]
+            lev[i] = 100 * r + LEVEL.get(name, 0) + LEVEL.get("%s@%d" % (name, r), 0)
+    key = [(lev[i], -tail[i], i) for i in range(n)]
+    left = [len(q) for q in pred]
+    ready = {e: [i for i in range(n) if eng[i] == e and not left[i]] for e in sorted(set(eng))}
+    est = [0.0] * n
+    free = {e: 0.0 for e in ready}
+    order = []
+    for _ in range(n):
+        t, e = min((max(free[e], min(est[i] for i in lst)), e) for e, lst in ready.items() if lst)
+        i = min((k for k in ready[e] if est[k] <= t + 20), key=lambda k: key[k])
+        i = min([i] + [k for k in ready[e] if est[k] < t + OPT["hold"] * cost[i]], key=lambda k: key[k])
+        ready[e].remove(i)
+        free[e] = max(t, est[i]) + cost[i]
+        order.append(i)
+        for k, d in succ[i]:
+            est[k] = max(est[k], free[e] + d)
+            left[k] -= 1
+            if not left[k]:
+                ready[eng[k]].append(k)
 
-    def ranked(key):
-        left = [len(op["dep"]) for op in ops]
-        ready = [i for i in range(n) if not left[i]]
-        seq = []
-        while ready:
-            i = min(ready, key=lambda k: key[k])
-            ready.remove(i)
-            seq.append(i)
-            for k in succ[i]:
-                left[k] -= 1
-                if not left[k]:
-                    ready.append(k)
-        return seq
-    if OPT["hold"] >= 0:
-        key = [(lev[i], noise * float(rnd[i]) - tail[i], i) for i in range(n)]
-        left = [len(op["dep"]) for op in ops]
-        ready = {}
-        est = [0.0] * n
-        for i in range(n):
-            ready.setdefault(ops[i]["eng"], [])
-            if not left[i]:
-                ready[ops[i]["eng"]].append(i)
-        free = {e: 0.0 for e in ready}
-        for _ in range(n):
-            t, e = min((max(free[e], min(est[i] for i in lst)), e) for e, lst in ready.items() if lst)
-            i = min((k for k in ready[e] if est[k] <= t + 20), key=lambda k: key[k])
-            soon = [k for k in ready[e] if est[k] < t + OPT["hold"] * ops[i]["cost"] and key[k] < key[i]]
-            if soon:
-                i = min(soon, key=lambda k: key[k])
-            op = ops[i]
-            ready[e].remove(i)
-            op["t0"] = max(t, est[i])
-            free[e] = op["t0"] + op["cost"]
-            op["t1"] = free[e] + op["l"]
-            for k in succ[i]:
-                est[k] = max(est[k], op["t1"] + gap(ops, i, k, p))
-                left[k] -= 1
-                if not left[k]:
-                    ready[ops[k]["eng"]].append(k)
-        return ranked([(ops[i]["t0"], i) for i in range(n)])
-    busy = {}
-    for i in ranked([(lev[i], noise * float(rnd[i]) - tail[i], i) for i in range(n)]):
-        op = ops[i]
-        c = op["cost"]
-        t = max([ops[j]["t1"] + gap(ops, j, i, p) for j in op["dep"]] + [0.0])
-        b = busy.setdefault(op["eng"], [])
-        k = len(b)
-        while k > 0 and b[k - 1][1] > t:
-            k -= 1
-        while k < len(b) and b[k][0] < t + c:
-            t = max(t, b[k][1])
-            k += 1
-        b.insert(k, (t, t + c))
-        op["t0"] = t
-        op["t1"] = t + c + op["l"]
-    return ranked([(ops[i]["t0"], i) for i in range(n)])
+    above = [0] * n
+    before = []
+    for i in range(n):
+        m = 0
+        for j, d in pred[i]:
+            m |= above[j]
+        before.append(set(j for j, d in pred[i] if not m >> j & 1))
+        above[i] = m | sum(1 << j for j in before[i])
+    after = [set() for _ in range(n)]
+    for i in range(n):
+        for j in before[i]:
+            after[j].add(i)
+    cases = []
+    for q in [p] + [dict(p, **x) for x in others]:
+        price(ops, q)
+        cases.append(([op["cost"] for op in ops],
+                      [[(j, ops[j]["cost"] + ops[j]["l"] + gap(ops, j, i, q)) for j in sorted(before[i])] for i in range(n)],
+                      [(i, ops[i]["cost"] + ops[i]["l"]) for i in range(n) if not succ[i]],
+                      [[(k, ops[i]["cost"] + ops[i]["l"] + gap(ops, i, k, q)) for k in sorted(after[i])] for i in range(n)],
+                      [op["cost"] + op["l"] for op in ops]))
+
+    def times(case, seq, a=0, old=None):
+        cost, near, sinks, far, lat = case
+        h, by = (list(old[1]), list(old[2])) if a else ([0.0] * n, [-1] * n)
+        last = {eng[k]: k for k in seq[:a]}
+        for i in seq[a:]:
+            b = last.get(eng[i], -1)
+            t = h[b] + cost[b] if b >= 0 else 0.0
+            for j, d in near[i]:
+                x = h[j] + d
+                if x > t:
+                    t, b = x, j
+            h[i], by[i], last[eng[i]] = t, b, i
+        end, at = max((h[i] + c, i) for i, c in sinks)
+        return end, h, by, at
+
+    def tails(case, seq, b, old):
+        cost, near, sinks, far, lat = case
+        q = list(old)
+        nxt = {eng[k]: k for k in seq[:b:-1]}
+        for i in seq[b::-1]:
+            k = nxt.get(eng[i], -1)
+            t = cost[i] + q[k] if k >= 0 else 0.0
+            if lat[i] > t:
+                t = lat[i]
+            for k, d in far[i]:
+                x = q[k] + d
+                if x > t:
+                    t = x
+            q[i], nxt[eng[i]] = t, i
+        return q
+
+    def through(case, now, rest, part, first, final):
+        cost, near, sinks, far, lat = case
+        h, h2, last = now[1], {}, dict(first)
+        for i in part:
+            b = last[eng[i]]
+            t = h2.get(b, h[b]) + cost[b] if b >= 0 else 0.0
+            for j, d in near[i]:
+                x = h2.get(j, h[j]) + d
+                if x > t:
+                    t = x
+            h2[i], last[eng[i]] = t, i
+        top = 0.0
+        for i, t in h2.items():
+            x = lat[i]
+            for k, d in far[i]:
+                if k not in h2 and rest[k] + d > x:
+                    x = rest[k] + d
+            if t + x > top:
+                top = t + x
+        for e, k in final.items():
+            if k >= 0 and h2[last[e]] + cost[last[e]] + rest[k] > top:
+                top = h2[last[e]] + cost[last[e]] + rest[k]
+        return top
+
+    draws = np.random.RandomState(OPT["seed"]).random_sample((OPT["moves"], 5)).tolist()
+    now = [times(c, order) for c in cases]
+    rest = [tails(c, order, n - 1, [0.0] * n) for c in cases]
+    weight = [now[0][0] / x[0] / len(cases) for x in now]
+    order.sort(key=lambda k: now[0][1][k])
+    end = now[0][0]
+    best = (end, order)
+    edges = None
+    for it, (x0, x1, x2, x3, x4) in enumerate(draws):
+        if edges is None:
+            edges = []
+            for _e, h, by, i in now:
+                while by[i] >= 0:
+                    if eng[by[i]] == eng[i] and by[i] not in before[i]:
+                        edges.append((by[i], i))
+                    i = by[i]
+            pos, ahead, behind, last = [0] * n, [-1] * n, [-1] * n, {}
+            for q, k in enumerate(order):
+                pos[k] = q
+                j = ahead[k] = last.get(eng[k], -1)
+                behind[j] = k if j >= 0 else behind[j]
+                last[eng[k]] = k
+        if not edges:
+            break
+        j, i = edges[int(x0 * len(edges))]
+        a, b = pos[j], pos[i]
+        up = x1 < 0.5
+        far = 1 + int(7 * x2) if x3 < 0.5 else 0
+        while far and 0 < a and b < n - 1:
+            a, b = (a - 1, b) if up else (a, b + 1)
+            far -= eng[order[a if up else b]] == eng[i]
+        seg = order[a:b + 1]
+        need = {i if up else j}
+        for k in (seg[::-1] if up else seg):
+            if not need.isdisjoint(after[k] if up else before[k]):
+                need.add(k)
+        if seg[0 if up else -1] in need:
+            continue
+        move, stay = [k for k in seg if k in need], [k for k in seg if k not in need]
+        part = move + stay if up else stay + move
+        room = -math.log(x4 + 1e-12) * OPT["heat"] * (1.02 - it / OPT["moves"])
+        first, final = {eng[k]: ahead[k] for k in seg[::-1]}, {eng[k]: behind[k] for k in seg}
+        more = sum(w * (through(c, x, y, part, first, final) - x[0]) for c, x, y, w in zip(cases, now, rest, weight))
+        if more > room or (more > -1 and x2 * 64 % 1 > OPT["drift"]):
+            continue
+        new = order[:a] + part + order[b + 1:]
+        then = [times(c, new, a, x) for c, x in zip(cases, now)]
+        more = sum(w * (y[0] - x[0]) for x, y, w in zip(now, then, weight))
+        if more <= room:
+            rest = [tails(c, new, b, y) for c, y in zip(cases, rest)]
+            now, end = then, end + more
+            order = sorted(new, key=lambda k: now[0][1][k])
+            edges = None
+            if end < best[0]:
+                best = (end, order)
+    end, h, by, at = times(cases[0], best[1])
+    price(ops, p)
+    return best[1], [h[i] + op["cost"] + op["l"] for i, op in enumerate(ops)]
 
 
-def emit(g, T, ops, order):
+ORDERS = {}
+
+
+def emit(g, T, ops, order, ends):
     queue = {"dve": g.vector, "act": g.scalar, "pe": g.tensor, "pool": g, "sp": g.sync}
     count = {}
     known = {e: {} for e in queue}
@@ -857,7 +1120,7 @@ def emit(g, T, ops, order):
             s, v = ops[j]["sig"]
             if v > want.get(s, (0, 0))[0]:
                 want[s] = (v, j)
-        for s in sorted(want, key=lambda k: -ops[want[k][1]]["t1"]):
+        for s in sorted(want, key=lambda k: -ends[want[k][1]]):
             v, j = want[s]
             if kn.get(s, 0) < v:
                 queue[e].wait_ge(T.sem[s], v)
@@ -888,4 +1151,7 @@ def rank_program(g, core, T, topo):
         return
     ops = build(g, T, topo, core)
     depend(ops)
-    emit(g, T, ops, schedule(ops, GUESS, OPT["seed"], OPT["noise"]))
+    shape = tuple((op["eng"], op["size"], tuple(op["dep"])) for op in ops)
+    if shape not in ORDERS:
+        ORDERS[shape] = schedule(ops, GUESS, OTHERS)
+    emit(g, T, ops, *ORDERS[shape])

@@ -8,18 +8,21 @@ RO, NS, NL, WC = 4, 192, 256, 4096
 TW = 4144
 MB = 272
 OFFS = (0, 53, 211, 264)
-CB01 = (0, 97, 133, 230)
-BETA = 0.916
-R16, R256, R8192 = 1.5 * 2 ** 27, 1.5 * 2 ** 31, 1.5 * 2 ** 36
+R1, R16, R256, R4096, R8192 = 1.5 * 2 ** 23, 1.5 * 2 ** 27, 1.5 * 2 ** 31, 1.5 * 2 ** 35, 1.5 * 2 ** 36
 OPT = dict(
-    dm=False, merge=False, key_pe=False, u_act=(2, 3), u_act_last=(2, 3),
-    m_split=36,
-    sw=(((0, 3), (3, 4)), ((0, 3), (3, 4)), ((0, 3), (3, 4))),
-    pf_early=False, pf_banks=(3, 4, 3, 4), pf_dve=((), ()), f_dve=(1,), wab_dve=(0,), hb_act=False, cm_act=True, pa_act=False,
-    hold=0.4, moves=100000, heat=40.0, drift=0.5, seed=0, sel_act=8, ms_dve=2, x_act=False)
-LEVEL = {'v': -2, 'g2': 69, 'of': -386, 'rest': -44, 'w': 11, 'w0': 98, 'wab0': -130, 'kc': 11, 'keys': 129, 'f0': -192, 't0': -41, 'g0': -170, 'w1': -308, 'wab1': 113, 'f1': -13, 't1': -23, 'g1': -560, 'home': -80, 'x1': -447, 'ms': -123, 'e': 160, 'fold': 495, 'fn1': -27, 'fn0': -8, 'u0': 109, 'x0': 18, 'cold': 180, 'fs': 131, 'late': 61, 'yc': 143, 'pf': -1, 'r0': -446, 'scan': -100, 'cm': -280, 'pf@0': 105, 'fn0@0': 148, 'fn1@3': 80, 'wab1@0': 16, 'v@3': 11, 'late@0': 70, 'w0@3': 166, 'u0@0': -32, 'f1@0': -58, 'kc@0': -46, 'fs@3': -77, 't0@0': 69, 'v@0': -107, 'w@3': -65, 'fn0@3': -138, 'wab1@3': 253, 'fold@3': 171, 'u1@3': 212, 'fold@0': -37, 'e@0': 46, 'pf@3': -393, 'home@3': 23, 'u1@0': -262, 'cold@3': 427, 't1@0': 76, 'x0@3': -278, 'rest@3': 45, 'cold@0': 493, 'g2@0': 104, 'g0@3': 284, 'g1@3': 4, 'x1@0': -630, 'keys@0': -129, 'rest@0': 68, 'of@0': 181, 'ms@0': 538, 'w1@0': 169, 'w1@3': -313, 'x1@3': -64, 'g2@3': -344, 'kc@3': 88, 'home@0': 18, 'wab0@3': 101, 'e@3': -176, 'g0@0': -531, 't1@3': -238, 'f1@3': -34, 'fs@0': 72, 't0@3': -130, 'w0@0': 189, 'of@3': -254, 'fn1@0': 79, 'wab0@0': 5, 'keys@3': -62, 'ms@3': -128, 'g1@0': -151, 'f0@3': -53, 'f0@0': 68, 'r0@0': -189, 'scan@0': -26, 'u0@3': 6, 'x0@0': 32, 'w@0': -185, 'cm@0': 61}
-LEVEL = {'v': -32, 'rest': -17, 'w': 19, 'g2': 53, 'of': -322, 'w0': -64, 'kc': 3, 'wab0': 29, 'keys': -1, 'f0': 14, 'w1': -41, 'wab1': 41, 'f1': 43, 't0': 15, 'g0': 24, 'f2': 50, 't1': 275, 'ug1': 62, 'g1': -42, 'e': 123, 'fold': 148, 'cold': 151, 'home': 61, 'x1': 96, 'u1': 137, 'us1': 162, 'u0': 259, 'x0': 169, 'us0': -37, 'fn0': 19, 'fn1': -39, 'ms': -43, 'late': 126, 'fs': 381, 'pf0': 202, 'pf1': 5, 'yc': 138, 'r0': -243, 'scan': -105, 'ug0': 53, 'pf0@0': -126, 'pf1@0': 247, 'cold@3': 32, 'f0@0': 31, 'x1@0': 57, 'pf0@3': 114, 'cold@0': 63, 'fs@3': 81, 'u1@0': -50, 't0@0': 42, 'f2@0': 18, 'ms@3': -89, 'late@0': 9, 'w1@3': -12, 'g0@3': -41, 'fn0@0': 208, 'w0@3': 29, 'of@3': -197, 'f1@0': 53, 'r0@0': 38, 'of@0': -198, 'x0@0': -17, 'fold@3': -85, 'fn0@3': 31, 'kc@3': -191, 'u1@3': -51, 'fs@0': -11, 'f2@3': -7, 't0@3': 7, 'fold@0': -35, 'keys@0': 43, 'x1@3': 96, 'v@3': -67, 'ms@0': -123, 'w0@0': -8, 'us1@0': 7, 'fn1@3': 269, 'rest@3': -85, 'fn1@0': 113, 'g2@0': 77, 'u0@0': 41, 'home@0': 33, 'w@3': -171, 'x0@3': 135, 'keys@3': 37, 'rest@0': -57, 'pf1@3': -9, 'g1@3': -15, 't1@0': -24, 'v@0': -7, 'f0@3': -22, 'us0@0': 77, 'w@0': -33, 'wab0@0': -37, 'home@3': -143, 'e@0': 57, 'g0@0': -156, 'scan@0': -1, 'kc@0': 44, 'wab1@3': 3, 'g2@3': 28, 'wab0@3': 169, 'u0@3': 97, 't1@3': -234, 'w1@0': 10, 'g1@0': 55, 'wab1@0': 19, 'ug1@3': 25, 'ug1@0': -13}
-LEVEL = {'v': -19, 'rest': -63, 'w': 22, 'g2': -50, 'of': -581, 'w0': -120, 'kc': 39, 'wab0': 409, 'keys': -82, 'f0': 1, 'w1': 7, 'wab1': -126, 'f1': 24, 't0': 199, 'g0': -155, 'f2': 58, 't1': 287, 'ug1': 60, 'g1': 33, 'e': 183, 'fold': 369, 'cold': 515, 'home': -181, 'x1': 161, 'u1': 230, 'us1': 388, 'u0': 368, 'x0': 257, 'us0': 223, 'fn0': -46, 'fn1': -304, 'ms': 163, 'late': 117, 'fs': 582, 'pf0': 372, 'pf1': 54, 'yc': -413, 'r0': -551, 'scan': -77, 'ug0': 53, 'pf0@0': -131, 'pf1@0': 301, 'cold@3': 56, 'f0@0': -36, 'x1@0': 108, 'pf0@3': 33, 'cold@0': 190, 'fs@3': 127, 'u1@0': 8, 't0@0': 244, 'f2@0': -85, 'ms@3': -156, 'late@0': 4, 'w1@3': -78, 'g0@3': -421, 'fn0@0': 650, 'w0@3': 139, 'of@3': -131, 'f1@0': 231, 'r0@0': -124, 'of@0': -284, 'x0@0': 30, 'fold@3': -167, 'fn0@3': -104, 'kc@3': -284, 'u1@3': -139, 'fs@0': -73, 'f2@3': 9, 't0@3': -57, 'fold@0': -369, 'keys@0': -21, 'x1@3': 69, 'v@3': -43, 'ms@0': -314, 'w0@0': 45, 'us1@0': -57, 'fn1@3': 535, 'rest@3': -141, 'fn1@0': 225, 'g2@0': 23, 'u0@0': 58, 'home@0': -89, 'w@3': -326, 'x0@3': 182, 'keys@3': 137, 'rest@0': -349, 'pf1@3': -111, 'g1@3': 155, 't1@0': -178, 'v@0': 49, 'f0@3': -77, 'us0@0': 219, 'w@0': -476, 'wab0@0': -159, 'home@3': -281, 'e@0': 80, 'g0@0': -164, 'scan@0': -201, 'kc@0': 2, 'wab1@3': 79, 'g2@3': -200, 'wab0@3': 391, 'u0@3': -83, 't1@3': -237, 'w1@0': 98, 'g1@0': 3, 'wab1@0': 162, 'ug1@3': 91, 'ug1@0': 23, 'yc@0': -298, 'e@3': 46, 'f1@3': -40}
+    merge=True, merge_g=False, f_bank=2, key_pe=False,
+    gp=((0, 16, "act"), (16, 32, "dve"), (32, 48, "act"), (48, 64, "dve")),
+    o_banks=(2, 6), pf0=(3, 4, 3, 4),
+    sets=((0, 64), (64, 64), (128, 64), (192, 64)),
+    fp=((0, 32, "dve"), (32, 64, "act"), (64, 96, "dve"), (96, 128, "act"), (128, 192, "act"), (192, 256, "act")),
+    sw=((0, 4),),
+    ug=((0, 128, "act"), (128, 256, "act")),
+    pf_banks=(3, 4, 3, 4), pf_dve=((), ()), rt_eng="pool", late_eng="pool", e_banks=(2, 1), wr_act=True, of_split=(0, 256), x_eng="act",
+    y_banks=(0, 6, 6), eq_pool=True,
+    turns=1500, noise=150.0, share=0.05, shove=5000.0, warm=0.0015, hold=0.4, moves=90000, heat=40.0, drift=0.5, seed=0)
+LEVEL = dict(c1=-95, cold=105, e=117, f0=18, f1=28, f2=125, fn0=65, fn1=8, fold=-57, fs=30, g0=25, g1=145, g2=-10, home=10, kc=-7, keys=6,
+             late=50, ms=-80, of=2, pf0=10, pf1=-90, r0=-330, rest=-30, rt=-7, scan=-325, t0=225, t1=265, u0=93, u1=108, ug=57, us1=48,
+             v=-25, w=-5, x1=-33, yc=100)
 
 SCRATCH = {}
 PART = {}
@@ -42,39 +45,41 @@ _s("float32", TW, "K")
 _s("float32", 2048, "PF0", "PF1", "Up", "Ug")
 _s("int32", 16, "ic")
 _s("float32", 128, "col")
-_p("float32", 16, "sixteen", "OH", "LT", "L4", "L8", "icf")
-_p("bfloat16", 144, "wide", "DI", "DG", "C4", "Big", "B4", "Bd", "Bt", "Bt1", "Bt1s", "EX0", "BY", "Y2", "H1", "H2", "H3", "H4", "H5", "H6",
-   "HD", "HA", "HB", "HL")
-_p("bfloat16", 128, "tiles", "CE", "CEb", "CEm", "C16", "I", "NI", "I64", "I8192", "I256", "N256", "N2048", "BO", "C8", "GB", "BO45", "ST", "STA",
-   "WR", "HM", "TT", "WA", "WB", "DC", "BJ", "KP", "PK", "U1", "U2", "YW", "t1", "t2", "t3", "t4", "t5", "t6", "t7", "t8")
-_p("bfloat16", 64, "narrow", "J", "kb", "hb0", "fl")
-_s("float16", NS, "CB")
+_p("float32", 16, "sixteen", "OH", "LT", "L4", "L8", "icf", "cv")
+_p("bfloat16", 144, "wide", "DI", "DG", "C4", "Big", "B4", "Bd", "Bt", "Bt1", "Bt2", "EX0", "BY", "HS", "HK", "HE", "HX", "H90", "H3", "H4",
+   "H5", "HD", "HA", "HB", "HL", "w1", "w2")
+_p("bfloat16", 128, "tiles", "CE", "CEb", "CEm", "CK", "C16", "I", "NI", "I64", "I8192", "I256", "N256", "BO", "C8", "GB", "ST", "STA",
+   "WR", "HM", "TT", "RA", "RB", "B1", "KP", "PK", "U1", "U2", "YW", "WT", "t1", "t2", "t3", "t4", "t5", "t6", "t7", "t8",
+   "EQ1", "EQ2", "EQ3", "EL0", "EL1", "EL2", "EL3", "hb", "HK2", "N4096")
+_p("bfloat16", 64, "narrow", "J", "kb", "fl")
+_s("float16", 128, "CB")
 _s("float16", 64, "ks")
 _s("float16", 32, "Kh")
-_s("float32", 128, "I32", "R32")
+_s("float32", 128, "I32", "R32", "PA")
 _s("float32", 24 if OPT["merge"] else 16, "BB")
 _s("bfloat16", 2048, "Sel", "DM")
 _s("bfloat16", 512, "D0", "Mt", "RS0", "J512")
 _s("bfloat16", 272, "RS1")
 _s("float32", 512, "Z0")
 _s("float32", 272, "Z1")
-_s("bfloat16", 256, "V", "CO", "c128", "fa", "Wp", "gs", "CMg", "Hd", "Cold", "Fold", "CMn", "Fnew", "us", "Xs", "ut", "key", "Mx", "mt")
-_s("bfloat16", NS, "CL", "CAP", "tb", "Sb", "ycl", "sg", "cum", "P", "hbs")
-_s("bfloat16", 128, "cy")
+_s("bfloat16", 256, "V", "wr", "Wp", "gs", "CMg", "Hd", "Cold", "Fold", "CMn", "Fnew", "us", "Xs", "ut", "key", "Mx", "mt")
+_s("bfloat16", NS, "CAP", "tb", "Sb", "ycl", "sg", "cum", "P", "DA")
+_s("bfloat16", 128, "cy", "CL")
 _s("bfloat16", 4 * NS, "Yg", "Sg", "Yb")
 _s("int32", NS, "X0", "vi", "hm", "hn")
-_s("float32", NS, "Tf", "Sf", "yso", "yxo", "PA", "pr")
-_s("float32", 64, "em", "tab")
+_s("float32", NS, "Tf", "Sf", "yso", "yxo", "sc")
+_s("float32", 64, "em", "tab", "pu")
+_s("float32", 16, "kr")
 _s("float32", 16 * NS, "Zs")
 _s("float32", 4 * NL, "Zr", "SW")
-_s("bfloat16", 4 * NL, "Ys", "G", "Wab")
-_s("uint16", 64, "dst", "om", "kl")
+_s("bfloat16", 4 * NL, "Ys", "G", "Rt")
+_s("uint16", 64, "dst", "om", "kl", "bl")
 _s("uint16", 256, "of")
 _s("uint16", 32, "so")
-_s("float32", 256, "yc0", "yco", "ycg", "d3", "Km")
+_s("float32", 256, "yco", "ycg", "d3", "Km")
 _s("int32", 256, "ki", "mi")
 _s("bfloat16", 4096, "Vg")
-_s("float16", 4096, "Vp")
+_s("float16", 4096, "Hs")
 for _i in range(8):
     SCRATCH["ps%d" % _i] = ("psum", [128, 512], "float32")
 
@@ -82,8 +87,8 @@ NDMA = 28
 SEMAPHORES = ["dve", "act", "pe", "pool", "sent"] + ["fw%d" % r for r in range(RO)] + ["bk%d" % r for r in range(RO)] + [
     "d%d" % i for i in range(NDMA)]
 TWO = {"bfloat16", "float16", "uint16"}
-GUESS = dict(cyc=0.87, fv=48, fa=95, gat=1.3, sca=3.0, pe=0.52, hop=130, same=70, rem=2900, dma=0.85, tt2=1.0)
-OTHERS = (dict(cyc=1.1, pe=0.62, gat=1.7, sca=4.5, tt2=2.0), dict(hop=200, same=100, rem=4200, dma=1.1, pe=0.45))
+GUESS = dict(cyc=0.87, fv=48, fa=95, gat=1.56, sca=3.8, pe=0.52, hop=130, same=70, rem=2900, dma=0.85, tt2=1.0)
+OTHERS = (dict(cyc=1.1, pe=0.62, gat=1.9, sca=5.0, tt2=2.0), dict(hop=200, same=100, rem=4200, dma=1.1, pe=0.45, gat=1.2, sca=2.5))
 
 
 def build(g, T, topo, core):
@@ -93,17 +98,16 @@ def build(g, T, topo, core):
     ndma = [0]
     level = [None]
     cols = {}
-    MS = OPT["m_split"]
 
     def R(name, c0=0, c1=None, st=1, key=None):
         buf, o, w = PART.get(name) or (name, 0, SCRATCH[name][1][1])
         if c1 is None:
             c1 = w
         ap = T[buf][:, o + c0:o + c1:st] if st > 1 else T[buf][:, o + c0:o + c1]
-        return dict(ap=ap, key=key or name, c0=c0, c1=c1, n=len(range(c0, c1, st)), dt=SCRATCH[buf][2], ps=SCRATCH[buf][0] == "psum")
+        return dict(ap=ap, key=key or name, c0=c0, c1=c1, st=st, n=len(range(c0, c1, st)), dt=SCRATCH[buf][2], ps=SCRATCH[buf][0] == "psum")
 
     def X(key):
-        return dict(key=key, c0=0, c1=1, ps=False)
+        return dict(key=key, c0=0, c1=1, st=1, ps=False)
 
     def IND(win, off):
         return dict(ap=win["ap"].indirect(off["ap"]), n=16 * off["n"], ind=(win, off), dt=win["dt"], ps=False)
@@ -174,6 +178,12 @@ def build(g, T, topo, core):
 
     def af(out, a, scale=None, bias=None):
         return act(out, a, AF.Identity, bias=bias, scale=scale)
+
+    def plus(eng, out, a, c, more=()):
+        if eng == "pool":
+            return add("pool", lambda: g.affine_select(out["ap"], a["ap"], [[0, out["n"]]], A.is_ge, 0.0, 0, 0), [out], [a],
+                       ("iota", out["n"] + 20), more)
+        return act(out, a, AF.Identity, bias=c, more=more) if eng == "act" else ts(out, a, c, A.add, more=more)
 
     def mm(items, start=True, stop=True, more=(), each=False):
         def fn():
@@ -296,7 +306,11 @@ def build(g, T, topo, core):
                  10800 + 2200 * k)
         op["after"] = [prev]
         prev = op
-    iota(R("ic", 0, 2), [[3, 2]], 0, 1)
+    iota(R("ic", 0, 2), [[-48, 2]], 48, 16)
+    iota(R("ic", 2, 3), [[0, 1]], 0, 4)
+    iota(R("ic", 3, 4), [[0, 1]], 0, 8)
+    iota(R("ic", 4, 5), [[0, 1]], 0, 1)
+    iota(R("icf", 0, 1), [[0, 1]], 0, 1)
     iota(R("J", 0, 16), [[1, 16]], 0, 0)
     iota(R("DI"), [[1, 144]], 0, -1)
     iota(R("CE"), [[16, 8], [0, 4], [1, 4]], 0, 0)
@@ -306,18 +320,21 @@ def build(g, T, topo, core):
     iota(R("C8"), [[1, 16], [0, 8]], -8, 0)
     iota(R("J512"), [[0, 32], [-1, 16]], 15, 0)
     sh, an = A.arith_shift_right, A.bitwise_and
-    ts(ic(2), ic(0), 15, an)
-    ts(ic(3), ic(0), 3, an)
-    ts(ic(4), ic(1), 3, an)
-    ts(ic(5), ic(0), 112, an)
-    cp(R("icf", 0, 6), R("ic", 0, 6))
-    ts(ic(6), ic(0), 4, sh)
-    ts(ic(7), ic(0), 2, sh, 3, an)
-    ts(ic(8), ic(0), 1, an)
-    ts(ic(9), ic(0), 1, sh, 1, an)
-    ts(ic(10), ic(0), 1, sh, 7, an)
-    cp(R("icf", 6, 11), R("ic", 6, 11))
-    p_, _x, r_, e_, e1_, g16, gr, s_, b0, b1, w_ = [R("icf", i, i + 1) for i in range(11)]
+    ts(R("ic", 5, 8), R("ic", 0, 3), 4, sh, 3, an)
+    ts(R("ic", 8, 11), R("ic", 1, 4), 4, sh, 1, an)
+    ts(ic(11), ic(4), 4, sh)
+    cp(R("icf", 5, 12), R("ic", 5, 12))
+    p_, e1_, e_, s_, b0, b2, b1, gr = [R("icf", i, i + 1) for i in (0, 5, 6, 7, 8, 9, 10, 11)]
+    r_ = C("r")
+    ts(r_, gr, -16.0, A.mult, p_, A.add)
+    g16 = lin("g16", gr, 16.0)
+    w_ = lin("w", s_, 2.0, b1)
+
+    def diag(out, pat, base, v):
+        n = out["n"]
+        add("pool", lambda: g.affine_select(out["ap"], R("DM", 0, n)["ap"], pat, A.not_equal, v, base, -1), [out], [R("DM", 0, n)],
+            ("iota", n + 20))
+    ms(R("DM", 0, 512), 0.0)
     J16 = R("J", 0, 16)
     ts(R("OH"), J16, r_, A.is_equal)
     ts(R("LT"), J16, r_, A.is_gt)
@@ -342,8 +359,9 @@ def build(g, T, topo, core):
     o192 = lin("o192", lin("h192", LT(12), -192.0, 192.0), e_)
     init = lin("init", r811, -1.0, o192)
     cap = lin("cap", r811, 1024.0, o192)
-    rows = {"b0": ((1, -160), (-480, -160), (4, -640), (6144, -5120), (15, 1), (-1, 14), (2, -1)),
-            "b1": ((2, -319), (2, -1), (1, -1)), "r": ((1, 4112), (1, 4128), (1, 1), (2, -8), (2, -7))}
+    rows = {"b0": ((-464, -176), (4, -640), (5888, -5120), (15, 1), (-1, 14), (3, 1), (2, -1), (-6, -2)),
+            "b1": ((2, -319), (-1, 1), (-60, 64)),
+            "r": ((1, 4112), (1, 4128), (1, 1), (2, -8), (2, -7))}
     at, made = 0, []
     for x, name in ((b0, "b0"), (b1, "b1"), (r_, "r")):
         n = len(rows[name])
@@ -353,79 +371,94 @@ def build(g, T, topo, core):
         af(R("tab", 48 + at, 48 + at + n), R("tab", at, at + n), x)
         tt(R("tab", 32 + at, 32 + at + n), R("tab", 48 + at, 48 + at + n), R("tab", 16 + at, 16 + at + n), A.add)
         at += n
-    aCol, aBest, aBlk, lBest, cPK, tPY, sa, bVar, sb, dc, spE, spO, r1, tU, tU1 = made
-    bT = lin("bT", s_, 256.0, lin("bT0", OH(12), 16384.0))
+    aBest0, aBlk, lBest0, cPK, tPY, qa, sa, cRB, bVar, nb1, qb, spE, spO, r1, tU, tU1 = made
+    act(C("e0"), e_, AF.Relu, bias=1.0, scale=-1.0)
+    bT = lin("bT", s_, 256.0, lin("bT0", C("e0"), 16384.0))
     af(R("CAP"), R("tb"), 0.0, cap)
     af(R("Tf"), R("tb"), None, bT)
-    ms(R("D0"), 0.0625)
+    ms(R("D0"), 1.0 / 64)
     ms(R("D0", 0, 512, 16), -1024.0)
-    fill(R("Yb"), 0)
     for o in range(N):
         fill(R("Zs", 192 * o, 192 * o + 64), 0)
-    ms(R("Ct", WC, TW), 0.0)
-    ms(R("Ft", WC, TW), 0.0)
-    ms(R("K", WC, TW), 0.0)
+        fill(R("Yb", 192 * o + 64, 192 * o + 192), 0)
+    dma("sp", [(T[n][:, WC:TW], T.DM[:, 0:TW - WC]) for n in ("Ct", "Ft")] + [(R("HE")["ap"], T.DM[:, 0:144])],
+        [R("Ct", WC, TW), R("Ft", WC, TW), R("HE")], [R("DM", 0, 144)], 2400)
+    fill(R("K", WC, TW), 0)
     pick(R("B4"), R("C4"), lin("g43", gr, 4.0, 3.0))
     B4 = R("B4")
-    af(R("H1"), B4, OH(0))
-    ts(R("H2"), B4, OH(1), A.mult, 2.0, A.mult)
+    tt(R("cv", 0, 4), R("OH", 0, 4), R("OH", 12, 16), A.add)
+    tt(R("cv", 4, 6), R("cv", 0, 2), R("OH", 4, 6), A.subtract)
+    tt(R("cv", 6, 7), R("cv", 0, 1), OH(8), A.subtract)
+    tt(R("cv", 7, 8), OH(5), R("cv", 5, 6), A.subtract)
+    smA, smB, a2, dB = [R("cv", j, j + 1) for j in (4, 5, 6, 7)]
+    sgn = lin("sgn", b2, 2.0, -1.0)
+    af(R("HS"), B4, lin("nod", lin("nod0", sgn, -1.0), C("e0")))
+    for k, c in enumerate((OH(4), OH(8), a2, smA)):
+        af(R("HK", k, 144, 4), R("B4", k, 144, 4), c)
+    ts(R("HE", 1, 144, 4), R("B4", 1, 144, 4), dB, A.mult, 2.0, A.mult)
+    ts(R("HE", 2, 144, 4), R("B4", 2, 144, 4), dB, A.mult, -2.0, A.mult)
+    ts(R("HX", 0, 144, 2), R("B4", 0, 144, 2), OH(5), A.mult, 2.0, A.mult)
+    ts(R("HX", 1, 144, 2), R("B4", 1, 144, 2), smB, A.mult, 2.0, A.mult)
     q4 = lin("q4", b0, lin("q4a", b1, 56.0, 576.0), lin("q4b", b1, -1340.0, 1552.0))
-    h6 = lin("h6", q4, LT(2))
-    af(R("H3"), B4, lin("h3", h6, -1.0, lin("h3a", q4, LT(4))))
+    af(R("H3"), B4, lin("h3", lin("h3a", q4, LT(4)), b1))
     ts(R("H4"), B4, OH(2), A.mult, 4.0, A.mult)
     ts(R("H5"), B4, OH(3), A.mult, 2.0, A.mult)
-    af(R("H6"), B4, h6)
-    ts(R("HD"), B4, lin("hd", OH(12), -1.0, OH(8)), A.mult, 512.0, A.mult)
+    ts(R("HD"), B4, OH(0), A.mult, -256.0, A.mult)
     tL = lin("tL", r45, None, 12.0)
     tA = lin("tA", r45, -1.0, 13.0)
     pick(R("HA"), DG, tA, lin("ha", OH(6), 4.0, OH(4)))
     pick(R("HB"), DG, tA, lin("hb", b0, lin("hba", r47, 2.0)))
-    pick(R("HL"), DG, tL, lin("hl", q4, r47))
+    cs = lin("cs", LT(4), -4.0, 1.0)
+    cI = lin("cI", lin("cI2", lin("cI1", lin("cI0", sgn, -1.0, cs), b1, sgn), qa), qb)
+    two(R("HL"), DG, (tL, lin("hl", q4, r47)), (14.0, cI), ("w1", "w2"))
+    aBest, lBest = lin("aBest", aBest0, nb1), lin("lBest", lBest0, nb1)
     z64 = R("Big", 0, 64)
-    ts(R("CB", 0, 64), z64, 0.0, A.mult, bVar, A.add)
-    ts(R("CB", 64, 128), z64, 0.0, A.mult, -319.0, A.add)
-    ts(R("CB", 128, 192), z64, 0.0, A.mult, bVar, A.add)
+    ts(R("CB", 0, 64), z64, 0.0, A.mult, -319.0, A.add)
+    ts(R("CB", 64, 128), z64, 0.0, A.mult, bVar, A.add)
     fill(R("CL", 0, 64), -5120)
     af(R("CL", 64, 128), z64, 0.0, lBest)
-    fill(R("CL", 128, 192), 1024)
-    for k in range(4):
-        fill(R("CO", 64 * k, 64 * k + 64), 16 * CB01[k] - (2048 if k and OPT["hb_act"] else 0))
-    fill(R("c128"), 4)
-    af(R("cy"), R("c128", 0, 128), 0.0, -127.5)
+    fill(R("DA", 0, NS, 3), 0)
+    fill(R("Rt", 0, 1024, 4), 0)
+    af(R("cy"), R("Big", 0, 128), 0.0, -127.5)
     pick(R("Bd"), R("DI"), 12.0, LT(4))
-    if OPT["hb_act"]:
-        af(R("N2048"), I, -2048.0)
     pick(R("Bt"), DG, lin("tBt", r_, 0.25, 12.0))
     pick(R("Bt1"), DG, lin("tBt1", r_, 0.25, 11.75))
-    af(R("Bt1s"), R("Bt1"), 0.0625)
+    pick(R("Bt2"), DG, lin("tBt2", r_, 0.25, 11.5))
+    pick(R("B1"), R("C4", 0, 128), lin("tB1", p_, 0.25, -0.25), 0.0625)
+    cB1 = lin("cB1", e_, 256.0, 128.0)
     af(R("EX0"), R("Big"), OH(0))
-    cs = lin("cs", LT(4), -4.0, 1.0)
-    tW = lin("tW", b1, -1.0, lin("g41", gr, 4.0, 1.0))
-    csB = lin("csB", cs, b0)
-    csA = lin("csA", csB, -1.0, cs)
-    pick(R("WA"), R("C4", 0, 128), tW, csA)
-    pick(R("WB"), R("C4", 0, 128), tW, csB)
-    fs = lin("fs", sa, sb)
-    m16 = lin("m16", lin("m16a", r47, -16.0), sa)
-    fb = lin("fb", lin("fb0", b0, -4.0, lin("fb1", m16, None, 4.0)), sb)
-    af(R("DC"), I, dc)
+    for l in range(4):
+        if l and OPT["eq_pool"]:
+            diag(R("EQ%d" % l), [[16, 8], [0, 4], [1, 4]], 4 * l, 1.0)
+        elif l:
+            ts(R("EQ%d" % l), R("CE"), 4.0 * l, A.add, p_, A.is_equal)
+        diag(R("EL%d" % l), [[16, 8], [1, 4], [0, 4]], 4 * l, 1064.0)
+    mm([(ps(7, 256, 384), win("HK", 12), I)])
+    af(R("t8"), ps(7, 256, 384), 97.0)
+    diag(R("CK"), [[16, 8], [1, 4], [0, 4]], 0, 16.0)
+    mm([(ps(7, 384, 512), R("t8"), R("CK"))])
+    act(R("HK2"), ps(7, 384, 512), AF.Copy)
     pick(R("BO"), R("C16"), gr)
     BO = R("BO")
+    od = lin("od", sgn, nb1)
+    ts(R("RA"), BO, od, A.mult, -2.0, A.mult)
+    ts(R("RB"), BO, od, A.mult, lin("cRB", cRB, None, 4.0), A.mult)
+    iota(R("t3"), [[0, 32], [1, 4]], -2, 0)
+    iota(R("t4"), [[0, 8], [1, 4], [0, 4]], -2, 0)
+    iota(R("t5"), [[0, 2], [-1, 4], [0, 16]], 2, 0)
+    iota(R("t6"), [[-1, 2], [0, 64]], 2, 0)
+    af(R("t3"), R("t3"), sa, 2.0)
+    af(R("t4"), R("t4"), lin("sb", nb1, -2.0, 1.0), 2.0)
+    tt(R("t5"), R("t5"), R("t6"), A.mult)
+    tt(R("t3"), R("t3"), R("t4"), A.mult)
+    tt(R("WT"), R("t3"), R("t5"), A.mult)
     for q in range(4):
-        o = R("Sel", 512 * q, 512 * q + 512)
-        iota(R("DM", 512 * q, 512 * q + 512), [[1, 4], [16, 8], [0, 16]], 4 * q, 0)
-        pick(o, R("DM", 512 * q, 512 * q + 512), p_)
-    fill(R("t8"), 0)
-    for name, v in (("I32", 1.0), ("I256", 1.0 / 256), ("N256", -1.0 / 256), ("NI", -1.0), ("I64", 64.0), ("I8192", 8192.0)):
-        add("pool", lambda name=name, v=v: g.affine_select(R(name)["ap"], R("t8")["ap"], [[-1, 128]], A.not_equal, v, 0, 1),
-            [R(name)], [R("t8")], ("iota", 150))
+        diag(R("Sel", 512 * q, 512 * q + 512), [[1, 4], [16, 8], [0, 16]], 4 * q, 1.0)
+    for name, v in (("I32", 1.0), ("I256", 1.0 / 256), ("N256", -1.0 / 256), ("NI", -1.0), ("I64", 64.0), ("I8192", 8192.0), ("N4096", -4096.0)):
+        diag(R(name), [[1, 128]], 0, v)
     pick(R("TT"), R("CE"), tE, -256.0)
-    act(C("e0"), e_, AF.Relu, bias=1.0, scale=-1.0)
-    bG = lin("bG", bT, -1.0, lin("bG0", C("e0"), 4096.0, 163840.0 - 128.0))
+    bG = lin("bG", s_, -256.0, 163840.0 - 128.0)
     pick(R("RS0"), R("J512"), r_)
-    if OPT["dm"]:
-        for r in range(16):
-            tt(R("DM", 128 * r, 128 * r + 128), SEL(r), I, A.subtract)
     fill(R("RS1"), 0)
     fill(R("RS1", 0, 272, 17), 1)
     if OPT["merge"]:
@@ -436,11 +469,12 @@ def build(g, T, topo, core):
         pick(R("BB"), R("J", 32, 48), gr)
     pick(R("GB"), R("C8"), gr, 2.0 ** 20)
     af(R("KP"), I, r414)
-    two(R("PK"), DG1, (lin("tPK", w_, None, 4.0), cPK), (tPY, r1), ("t5", "t6"))
+    two(R("PK"), DG1, (lin("tPK", w_, None, 4.0), cPK), (tPY, r1), ("t1", "t2"))
     pick(R("U1"), DG1, tU, r411)
     pick(R("t7"), DG1, tU1, lin("cU", r411, 0.0625))
     tt(R("U2"), R("t7"), R("U1"), A.subtract)
     fill(R("Mx"), 0)
+    b15 = lin("b15", OH(0), 15.0)
     af(R("BY"), R("Big"), r1)
     af(R("YW"), BO, lin("yw", r811, -64.0))
 
@@ -458,12 +492,7 @@ def build(g, T, topo, core):
             for jj in (2 * c, 2 * c + 1):
                 o = ps(banks[c], 256 * (jj % 2), 256 * (jj % 2) + 256)
                 mm([(o, I, R("Ft", 2 * jj, WC, 16)), (o, R("I8192"), R("Ft", 2 * jj + 1, WC, 16))])
-            o = R("PF%d" % (r % 2), 512 * c, 512 * c + 512)
-            if c in OPT["pf_dve"][min(r, 1)]:
-                ts(o, ps(banks[c], 0, 512), -2.0 ** 20, A.add)
-            else:
-                af(o, ps(banks[c], 0, 512), None, -2.0 ** 20)
-
+            plus("dve" if c in OPT["pf_dve"][min(r, 1)] else "act", R("PF%d" % (r % 2), 512 * c, 512 * c + 512), ps(banks[c], 0, 512), -2.0 ** 20)
 
     lv(0, "scan")
     for b in range(8):
@@ -471,7 +500,7 @@ def build(g, T, topo, core):
         mm([(ps(bank, 128 * c, 128 * c + 128), R("Ct", 512 * b + 128 * c, 512 * b + 128 * c + 128), I) for c in range(4)], each=True)
         scan(R("K", 512 * b, 512 * b + 512), R("D0"), ps(bank, 0, 512), 0.0, A.add, A.max)
     for q in range(8):
-        ts(R("ki", 32 * q, 32 * q + 32), R("K", 16 * q + 15, 4096, 128), 16.0, A.mult)
+        ts(R("ki", 32 * q, 32 * q + 32), R("K", 16 * q + 15, 4096, 128), 64.0, A.mult)
     ts(R("mi"), R("ki"), 15, A.bitwise_and)
     ts(R("mt"), R("mi"), -1.0, A.mult, 15.0, A.add)
     mm([(ps(3, 128 * h, 128 * h + 128), R("mt", h, 256, 2), I) for h in range(2)], each=True)
@@ -518,10 +547,10 @@ def build(g, T, topo, core):
         b = 768 * r
         op = exchange("fw%d" % r, lambda o: T.Zs[:, b + 192 * o:b + 192 * o + 64],
                       lambda o: T.Zr[:, NL * r + 64 * place(me, o):NL * r + 64 * place(me, o) + 64],
-                      "Zin%d" % r, [w, R("Yb") if r == 0 else R("Yg", NS * (r - 1), NS * r)], [o for o in range(N) if o != me])
-        act(R("Zr", NL * r + 192, NL * r + 256), R("Zs", b + 192 * me, b + 192 * me + 64), AF.Copy)
+                      "Zin%d" % r, [w] + ([R("Yg", NS * (r - 1), NS * r)] if r else []), [o for o in range(N) if o != me])
+        plus(OPT["late_eng"], R("Zr", NL * r + 192, NL * r + 256), R("Zs", b + 192 * me, b + 192 * me + 64), 0.0)["after"] = [op]
         lv(max(r - 1, 0), "late")
-        act(R("Sb"), pX, AF.Copy)
+        plus(OPT["late_eng"], R("Sb"), R("Sf"), 0.0)["after"] = [op]
         act(R("Sg", NS * r, NS * r + NS), R("P"), AF.Sign, bias=-63.5)
         return op
 
@@ -533,11 +562,11 @@ def build(g, T, topo, core):
         for o in range(N):
             fill(R("Zs", 768 * r + 192 * o, 768 * r + 192 * o + 64), 0)["after"] = [sent0]
 
-    if OPT["pf_early"]:
-        pairs_of(0, OPT["pf_banks"])
+    if OPT["pf0"]:
+        pairs_of(0, OPT["pf0"])
     for r in range(RO):
         last = r == RO - 1
-        UA = OPT["u_act_last" if last else "u_act"]
+        PF = "PF%d" % (r % 2)
         Z = R("Zr", NL * r, NL * r + NL)
         zin = [X("Zin%d" % r)]
         V = R("V")
@@ -546,83 +575,82 @@ def build(g, T, topo, core):
 
         def sel(o, nm):
             return [(o, win(nm, 12 - 4 * l), R("V", l, 256, 4)) for l in range(4)]
-        mm(sel(ps(0, 0, 64), "H1"))
-        mm([(ps(1, 0, 64), I, R("CB", 0, 64))] + sel(ps(1, 0, 64), "H2"))
-        mm([(ps(1, 64, 128), I, R("CL", 0, 64))] + sel(ps(1, 64, 128), "H3"))
-        if OPT["pa_act"]:
-            af(R("PA", 0, 64), ps(0, 0, 64), None, aCol)
-        else:
-            ts(R("PA", 0, 64), ps(0, 0, 64), aCol, A.add)
-        tt(R("pr", 0, 64), R("PA", 0, 64), ps(1, 0, 64), A.mult)
-        tt(R("vi", 0, 64), R("pr", 0, 64), ps(1, 64, 128), A.add)
-        ts(R("hm", 0, 64), R("vi", 0, 64), 2, sh, 4095, an)
+        mm(sel(ps(0, 0, 64), "HK"))
+        mm(sel(ps(7, 0, 64), "HS"))
+        mm([(ps(1, 1, NS, 3), I, R("CB", 0, 64)), (ps(1, 2, NS, 3), I, R("CL", 0, 64))], stop=False)
+        mm(sel(ps(1, 0, NS, 3), "HE") + sel(ps(1, 1, NS, 3), "HX") + sel(ps(1, 2, NS, 3), "H3"), start=False)
+        ts(R("DA", 2, NS, 3), ps(0, 0, 64), -176.0, A.add)
+        af(R("DA", 1, NS, 3), ps(7, 0, 64), None, 1.0)
+        mm(sel(ps(7, 64, 128), "H4"))
+        mm(sel(ps(7, 128, 192), "HA"))
+        scan(R("sc"), R("DA"), ps(1, 0, NS), 0.0, A.mult, A.add)
+        cp(R("ki", 64, 128), R("sc", 2, NS, 3))
+        ts(R("hm", 0, 64), R("ki", 64, 128), 2, sh, 4095, an)
         cp(R("om"), R("hm", 0, 64))
-        act(R("G", 0, 16 * MS), IND(Mw, R("om", 0, MS)), AF.Copy, more=MSK)
-        lv(r, "g2")
-        if MS < 64:
-            cp(R("G", 16 * MS, 1024), IND(Mw, R("om", MS, 64)), more=MSK)
+        for a, b, eng in OPT["gp"]:
+            lv(r, "g2" if a else "v")
+            plus(eng, R("G", 16 * a, 16 * b), IND(Mw, R("om", a, b)), 0.0, more=MSK)
+        lv(r, "rt")
+        mm([(ps(6, 0, 256), R("RA"), V), (ps(6, 256, 512), R("RB"), V)], each=True)
+        act(R("Rt", 1, 1024, 4), ps(6, 0, 256), AF.Abs, bias=1.0)
+        act(R("Rt", 2, 1024, 4), ps(6, 256, 512), AF.Abs, bias=1.0)
+        plus(OPT["rt_eng"], R("Rt", 3, 1024, 4), R("Rt", 1, 1024, 4), 0.0)
         lv(r, "rest")
-        mm(sel(ps(2, 0, 64), "HA") + sel(ps(2, 64, 128), "H4"))
-        af(R("PA", 128, 192), ps(2, 64, 128), None, aBlk)
-        af(R("PA", 64, 128), ps(2, 0, 64), None, aBest)
-        mm([(ps(5, 0, 128), I, R("CB", 64, 192))] + sel(ps(5, 0, 64), "HB") + sel(ps(5, 64, 128), "H5"))
-        mm([(ps(5, 128, 256), I, R("CL", 64, 192))] + sel(ps(5, 128, 192), "HL") + sel(ps(5, 192, 256), "H6"))
-        mm(sel(ps(5, 256, 320), "HD"))
-        tt(R("pr", 64, 192), R("PA", 64, 192), ps(5, 0, 128), A.mult)
-        tt(R("vi", 64, 192), R("pr", 64, 192), ps(5, 128, 256), A.add)
-        ts(R("hn", 64, 192), R("vi", 64, 192), 4080, an)
-        cp(R("hb0"), R("hn", 128, 192))
-        for k in range(1, 4):
-            if OPT["hb_act"]:
-                act(R("hbs", 64 * k - 64, 64 * k), R("hb0"), AF.Sign, bias=16.0 * CB01[k] - 4088.0)
-            else:
-                ts(R("hbs", 64 * k - 64, 64 * k), R("hn", 128, 192), 4096.0 - 16 * CB01[k], A.is_ge, -4096.0, A.mult)
+        af(R("PA", 64, 128), ps(7, 64, 128), None, aBlk)
+        mm([(ps(5, 0, 64), I, R("CB", 64, 128))] + sel(ps(5, 0, 64), "H5"))
+        tt(R("vi", 64, 128), R("PA", 64, 128), ps(5, 0, 64), A.mult)
+        ts(R("hn", 64, 128), R("vi", 64, 128), 4080, an)
+        ts(R("hb", 0, 64), R("hn", 64, 128), -1824.0, A.add)
+        plus(OPT["x_eng"], R("hb", 64, 128), R("sc", 1, NS, 3), 0.0)
+        mm([(ps(5, 256, 512), R("HK2"), V)], stop=False)
+        mm([(ps(5, 256 + l, 512, 4), R("EL%d" % l), R("hb", 64, 128)) for l in range(4)], start=False, stop=False)
+        mm([(ps(5, 256 + l, 512, 4), R("EQ%d" % l if l else "ST"), R("hb", 0, 64)) for l in range(4)], start=False)
+        if OPT["wr_act"]:
+            af(R("wr"), ps(5, 256, 512), 1.0 / 4096, 100.0)
+        else:
+            ts(R("wr"), ps(5, 256, 512), R4096, A.add, -R4096, A.add)
+        for h, b in enumerate(OPT["o_banks"]):
+            c = 256 + 128 * h
+            mm([(ps(b, c, c + 128), R("HK2"), R("V", 128 * h, 128 * h + 128))]
+               + [(ps(b, c + l, c + 128, 4), R(m), R("hb", a + 32 * h, a + 32 * h + 32)) for l in range(4)
+                  for m, a in (("EL%d" % l, 64), ("EQ%d" % l if l else "ST", 0))], stop=False)
         lv(r, "kc")
-        ts(R("em"), ps(5, 256, 320), 2048.0, A.add, -2048.0, A.max)
-        ts(R("hm", 64, 128), R("vi", 64, 128), 2, sh, 4095, an)
+        af(R("PA", 0, 64), ps(7, 128, 192), None, aBest)
+        mm([(ps(0, 64, 128), I, R("CB", 0, 64))] + sel(ps(0, 64, 128), "HB"))
+        mm([(ps(0, 128, 192), I, R("CL", 64, 128))] + sel(ps(0, 128, 192), "HL"))
+        mm(sel(ps(0, 192, 256), "HD"))
+        tt(R("pu"), R("PA", 0, 64), ps(0, 64, 128), A.mult)
+        tt(R("vi", 0, 64), R("pu"), ps(0, 128, 192), A.add)
+        ts(R("hn", 0, 64), R("vi", 0, 64), 4080, an)
+        ts(R("em"), ps(0, 192, 256), 43008.0, A.add, -2048.0, A.max)
+        ts(R("hm", 64, 128), R("vi", 0, 64), 2, sh, 4095, an)
         tt(R("ks"), R("hm", 64, 128), R("em"), A.add)
-        tt(R("kb"), R("hn", 64, 128), R("em"), A.add)
+        tt(R("kb"), R("hn", 0, 64), R("em"), A.add)
+        mm([(ps(1, 192, 208), win("Bt2", 12 - 4 * a), R("ks", a, 64, 4)) for a in range(4)]
+           + [(ps(1, 208, 224), win("Bt", 12 - 4 * a), R("ks", a, 64, 4)) for a in range(4)] + [(ps(1, 256, 320), R("B1"), R("kb"))])
+        kc, kw, kf = R("kl", 0, 16), R("kl", 16, 32), R("kl", 32, 48)
+        ts(kw, ps(1, 192, 208), 2048.0, A.add, 127.0, A.min)
+        ts(kc, ps(1, 208, 224), 2048.0, A.add, 4096.0, A.min)
+        ts(R("bl"), ps(1, 256, 320), cB1, A.add, 1023.0, A.min)
         lv(r, "w")
-        mm([(ps(6, 0, 256), R("WA"), V)])
-        mm([(ps(6, 256, 512), R("DC"), R("c128")), (ps(6, 256, 512), R("WB"), V)])
-        af(R("fa"), ps(6, 0, 256), fs, fb)
-        tt(R("Wp"), R("fa"), ps(6, 256, 512), A.mult)
-        for h in range(2):
-            lv(r, "w%d" % h)
-            mm([(ps(3 + h, x, 512, 4), SEL(x), R("Wp", 128 * h, 128 * h + 128)) for x in range(4)], each=True)
-            lv(r, "wab%d" % h)
-            if h:
-                mm([(ps(7, 256 * q + 64 * k, 256 * q + 64 * k + 64), SEL(4 + k), R("Wp", 128 + 64 * q, 192 + 64 * q))
-                    for q in range(2) for k in range(4)], each=True)
-            else:
-                mm([(ps(0, 128 * k, 128 * k + 128), SEL(4 + k), R("Wp", 0, 128)) for k in range(4)], each=True)
-            if h in OPT["wab_dve"]:
-                cp(R("Wab", 512 * h, 512 * h + 512), ps(7 * h, 0, 512))
-            else:
-                act(R("Wab", 512 * h, 512 * h + 512), ps(7 * h, 0, 512), AF.Copy)
-        lv(r, "kc")
-        mm([(ps(1, 128, 144), win("Bt1s", 12 - 4 * a), R("kb", a, 64, 4)) for a in range(4)]
-           + [(ps(1, 144, 160), win("Bt", 12 - 4 * a), R("ks", a, 64, 4)) for a in range(4)])
-        kc, bl, kf = R("kl", 0, 16), R("kl", 16, 32), R("kl", 32, 48)
-        ts(kc, ps(1, 144, 160), 2048.0, A.add)
-        ts(bl, ps(1, 128, 144), 128.0, A.add, 255.0, A.min)
+        act(R("Wp"), IND(R("WT"), kw), AF.Copy)
+        for l0, n in OPT["sets"]:
+            c = 4 * (l0 % 128)
+            mm([(ps(3 + l0 // 128, c + n * x, c + n * x + n), SEL(x), R("Wp", l0, l0 + n)) for x in range(4)], each=True)
         lv(r, "of")
-        mm([(ps(2, 256, 512), I, R("CO")), (ps(2, 320, 512), R("N2048") if OPT["hb_act"] else I, R("hbs"))]
-           + [(ps(2, 256 + 64 * k, 320 + 64 * k), I, R("hb0")) for k in range(4)], stop=False)
-        mm([(ps(2, 256 + 64 * k, 320 + 64 * k), win("Bd", 12 - 4 * l), R("G", 4 * l + k, 1024, 16)) for k in range(4) for l in range(4)],
-           start=False)
-        cp(R("of"), ps(2, 256, 512))
+        for h, b in enumerate(OPT["o_banks"]):
+            pO = ps(b, 256 + 128 * h, 384 + 128 * h)
+            mm([(pO, R("N4096" if OPT["wr_act"] else "NI"), R("wr", 128 * h, 128 * h + 128))], start=False, stop=False)
+            mm([(pO, win("Bd", 12 - 4 * k), R("G", 512 * h + k, 512 * h + 512, 4)) for k in range(4)], start=False)
+            ts(R("of", 128 * h, 128 * h + 128), pO, 2040.0 + (100.0 * 4096 if OPT["wr_act"] else 0.0), A.add)
         Fw = R("Ft")
         lv(r, "keys")
-        if OPT["cm_act"]:
-            act(R("CMg"), IND(Mw, kc), AF.Copy, more=MSK)
-        else:
-            cp(R("CMg"), IND(Mw, kc), more=MSK)
-        o = ps(1, 160, 176)
+        act(R("CMg"), IND(Mw, kc), AF.Copy, more=MSK)
+        o = ps(1, 224, 240)
         mm([(o, win("Bt1", 12 - 4 * a), R("kb", a, 64, 4)) for a in range(4)]
            + [(o, EX(rho, "EX0"), R("CMg", rho, 256, 16)) for rho in range(16)])
-        ts(R("Kh"), ps(1, 144, 176), 1.0 / 64, A.mult)
-        ts(kf, o, 2048.0, A.add)
+        ts(R("Kh"), ps(1, 208, 240), 1.0 / 64, A.mult)
+        ts(kf, o, 2048.0, A.add, 4096.0, A.min)
         lv(r, "fold")
         act(R("Fold"), IND(Fw, kf), AF.Copy)
         lv(r, "cold")
@@ -633,201 +661,153 @@ def build(g, T, topo, core):
             if r:
                 ts(R("Hd"), R("CMg"), R16, A.add, -R16, A.add)
         lv(r, "e")
+        eb = OPT["e_banks"]
         for q in range(4):
-            if OPT["dm"]:
-                mm([(ps(2, 15 - x, 512, 16), R("DM", 128 * x, 128 * x + 128), R("Kh")) for x in range(4 * q, 4 * q + 4)], each=True)
-            else:
-                mm([(ps(2, 15 - x, 512, 16), m, R("Kh")) for x in range(4 * q, 4 * q + 4) for m in (SEL(x), R("NI"))],
-                   start=q == 0, stop=q == 3)
-        scan(R("Z0"), ps(2, 0, 512), R("RS0"), 1.0, A.mult, A.add)
-        mm([(ps(1, 176, 448, 17), I, R("RS1", 1, 17))], stop=False)
+            mm([(ps(eb[0], 15 - x, 512, 16), m, R("Kh")) for x in range(4 * q, 4 * q + 4) for m in (SEL(x), R("NI"))],
+               start=q == 0, stop=q == 3)
+        scan(R("Z0"), ps(eb[0], 0, 512), R("RS0"), 1.0, A.mult, A.add)
+        mm([(ps(eb[1], 176, 448, 17), I, R("RS1", 1, 17))], stop=False)
         for q in range(4):
             it = []
             for x in range(4 * q, 4 * q + 4):
-                o = ps(1, 177 + x, 448, 17)
+                o = ps(eb[1], 177 + x, 448, 17)
                 it += [(o, SEL(x), R("Kh", 0, 32, 2)), (o, R("NI"), R("Kh", 1, 32, 2))]
             mm(it, start=False, stop=q == 3)
-        scan(R("Z1"), ps(1, 176, 448), R("RS1"), 1.0, A.mult, A.add)
+        scan(R("Z1"), ps(eb[1], 176, 448), R("RS1"), 1.0, A.mult, A.add)
         ts(R("fl", 0, 32), R("Z0", 15, 512, 16), 0.0, A.is_equal, 8192.0, A.mult)
         ts(R("fl", 32, 48), R("Z1", 16, 272, 17), 0.0, A.is_equal, 8192.0, A.mult)
         mm([(ps(1, 448, 480), R("I64"), R("Kh")), (ps(1, 448, 480), I, R("fl", 0, 32)), (ps(1, 449, 480, 2), I, R("fl", 32, 48))])
-        ts(R("so", 0, 32, 2, key="soE"), ps(1, 448, 480, 2), 2048.0, A.add, spE, A.min)
-        ts(R("so", 1, 32, 2, key="soO"), ps(1, 449, 480, 2), 2048.0, A.add, spO, A.min)
-        SO = [R("so", key="soE"), R("so", key="soO")]
-        if r == 0 and not OPT["pf_early"]:
+        ts(R("so", 0, 32, 2), ps(1, 448, 480, 2), 2048.0, A.add, spE, A.min)
+        ts(R("so", 1, 32, 2), ps(1, 449, 480, 2), 2048.0, A.add, spO, A.min)
+        if r == 0 and not OPT["pf0"]:
             pairs_of(0, (2, 1, 2, 1))
-
-        def train(n2, h):
-            c = 128 * h
-
-            def H(name):
-                return R(name, c, c + 128)
-            lv(r, "fn%d" % n2)
-            o = ps(3 + n2, 0, 128)
-            mm([(o, I, H("Fold")), (o, I, H("gs"))])
-            ts(H("Fnew"), o, 0.0, A.max, 255.0, A.min)
-            lv(r, "u%d" % n2)
-            b = 5 + n2
-            if any(2 * n2 + q in UA for q in range(2)):
-                mm([(ps(3 + n2, 128 * x, 128 * x + 128), I, H("gs")) for x in range(4)], each=True)
-            if not last:
-                o = ps(b, 256, 384)
-                mm([(o, H("Cold"), I)] + ([(o, H("CMg"), R("U1")), (o, H("Hd"), R("U2"))] if r else []))
-            mm([(ps(b, 0, 128), H("gs"), R("GB"))], stop=False)
+        lv(r, "ug")
+        for a, b, eng in OPT["ug"]:
             for q in range(2):
-                u0 = 1024 * h + 512 * q
-                for jj in range(4 * q, 4 * q + 4):
-                    w = IND(R("PF%d" % (r % 2), 256 * jj, 256 * jj + 256), R("kl", 16 + 8 * h, 24 + 8 * h))
-                    up = R("Up", 1024 * h + 128 * jj, 1024 * h + 128 * jj + 128)
-                    if 2 * n2 + q in UA:
-                        lv(r, "ug%d" % n2)
-                        act(R("Ug", up["c0"], up["c1"]), w, AF.Copy)
-                    else:
-                        tt(up, w, H("gs"), A.mult)
-                        mm([(ps(b, jj, 128, 8), up, R("BB"))], start=False, stop=jj == 7)
-                lv(r, "u%d" % n2)
-                if 2 * n2 + q in UA:
-                    tt(R("Up", u0, u0 + 512), R("Ug", u0, u0 + 512), ps(3 + n2, 0, 512), A.mult)
-                    mm([(ps(b, 4 * q + x, 128, 8), R("Up", u0 + 128 * x, u0 + 128 * x + 128), R("BB")) for x in range(4)],
-                       start=False, stop=q == 1)
-            lv(r, "x%d" % n2)
-            r32 = R("R32", 64 * h, 64 * h + 64)
-            ts(r32, ps(b, 0, 64), R8192, A.add, -R8192, A.add)
-            tt(R("Xs", c, c + 128, 2, key="XsE"), ps(b, 0, 64), r32, A.subtract)
-            ts(R("Xs", c + 1, c + 128, 2, key="XsO"), ps(b, 64, 128), R8192, A.add, -R8192, A.add)
-            xs, xo = R("Xs", c, c + 128, key="XsE"), [R("Xs", c, c + 128, key="XsO")]
-            if last:
-                mm([(ps(b, 128, 256), xs, I)], more=xo)
-                act(H("us"), ps(b, 128, 256), AF.Sign)
-                mm([(ps(b, 256, 384), EX(0, "BY"), H("us"))])
-                act(H("d3"), ps(b, 256, 384), AF.Copy)
-                return
-            ts(H("ut"), xs, -1.0, A.max, 1.0, A.min, more=xo)
-            tt(H("key"), ps(b, 256, 384), H("ut"), A.add)
-            scan(H("Km"), R("D0", 0, 128), H("key"), 0.0, A.add, A.max)
-            ki, mi = R("ki", 8 * h, 8 * h + 8), R("mi", 8 * h, 8 * h + 8)
-            ts(ki, R("Km", c + 15, c + 128, 16), 16.0, A.mult)
-            ts(mi, ki, 15, an)
-            ts(R("Mx", c, c + 128, 16), mi, -1.0, A.mult, 15.0, A.add)
-            lv(r, "us%d" % n2)
-            mm([(ps(3 + n2, 0, 128), H("ut"), I)])
-            act(H("us"), ps(3 + n2, 0, 128), AF.Copy)
-            o = ps(b, 384, 512)
-            mm([(o, R("KP"), H("CMg")), (o, R("PK"), H("us"))], stop=False)
-            mm([(o, H("Mx"), I)], start=False)
-            act(H("CMn"), o, AF.Copy)
-        def train_all():
-            gs = R("gs")
-            lv(r, "fn0")
-            o = ps(3, 0, 256)
-            mm([(o, I, R("Fold")), (o, I, gs)])
-            ts(R("Fnew"), o, 0.0, A.max, 255.0, A.min)
-            lv(r, "u1")
-            if UA:
-                mm([(ps(4, 256 * x, 256 * x + 256), I, gs) for x in range(2)], each=True)
-            lv(r, "c0")
+                plus(eng, R("Ug", 1024 * q + 4 * a, 1024 * q + 4 * b), IND(R(PF, 1024 * q, 1024 * q + 1024), R("bl", a // 4, b // 4)), 0.0)
+
+        def train(c, n):
+            hs = range(c // 128, (c + n) // 128)
+            both = OPT["merge"]
+            t = str(hs[-1])
+            bu, bk = (5, 6) if both else (5 + hs[0], 5 + hs[0])
+            bF, cF = (OPT["f_bank"], c) if both else (bk, 128)
+            lv(r, "u" + t)
+            for h in hs:
+                mm([(ps(3 + h, x, 512, 4), I, R("gs", 128 * h, 128 * h + 128)) for x in range(4)], each=True)
+            lv(r, "fn" + t)
+            mm([(ps(bF, cF, cF + n), I, R("Fold", c, c + n)), (ps(bF, cF, cF + n), I, R("gs", c, c + n))])
+            ts(R("Fnew", c, c + n), ps(bF, cF, cF + n), 0.0, A.max, 255.0, A.min)
+            lv(r, "u" + t)
+            for h in hs:
+                gs = R("gs", 128 * h, 128 * h + 128)
+                if both:
+                    if h == 0:
+                        mm([(ps(bu, a, a + 64), I, R("GB", 0, 64)) for a in (0, 64, 192)], stop=False)
+                    mm([(ps(bu, 128 + 64 * h, 192 + 64 * h), gs, R("GB", 64, 128))], start=False, stop=False)
+                else:
+                    mm([(ps(bu, 0, 128), gs, R("GB"))], stop=False)
+                for q in range(2):
+                    u0 = 1024 * q + 512 * h
+                    tt(R("Up", u0, u0 + 512), R("Ug", u0, u0 + 512), ps(3 + h, 0, 512), A.mult)
+                    o0 = 64 * h if both else 0
+                    mm([(ps(bu, o0 + 4 * q + x, o0 + 4 * q + x + (185 if both else 121), 8), R("Up", u0 + x, u0 + 512, 4), R("BB")) for x in range(4)],
+                       start=False, stop=q == 1 and (h == 1 or not both))
+            if not both:
+                probes(c, n, bu, bk, 128, 256, 384)
+            elif c + n == 256:
+                probes(0, 256, bu, bk, 256, 0, 256)
+
+        def probes(c, n, bu, bk, cF, cK, cN):
+            hs = range(c // 128, (c + n) // 128)
+            t = str(hs[-1])
+
+            def H(name, h=None):
+                return R(name, c, c + n) if h is None else R(name, 128 * h, 128 * h + 128)
+
+            def P(b, c0, h=None):
+                return ps(b, c0, c0 + n) if h is None else ps(b, c0 + 128 * h - c, c0 + 128 * h - c + 128)
+            lv(r, "c" + t)
             if not last:
-                mm([(ps(6, 128 * h, 128 * h + 128), R(a, 128 * h, 128 * h + 128), m) for h in range(2)
-                    for a, m in [("Cold", I)] + ([("CMg", R("U1")), ("Hd", R("U2"))] if r else [])], stop=not OPT["key_pe"])
-            lv(r, "u1")
-            mm([(ps(5, 64 * h, 64 * h + 64), I, R("GB", 0, 64)) for h in range(2)]
-               + [(ps(5, 128 + 64 * h, 192 + 64 * h), R("gs", 128 * h, 128 * h + 128), R("GB", 64, 128)) for h in range(2)], stop=False)
-            for q in range(4):
-                for jj in (2 * q, 2 * q + 1):
-                    w = IND(R("PF%d" % (r % 2), 256 * jj, 256 * jj + 256), bl)
-                    if q in UA:
-                        lv(r, "ug1")
-                        act(R("Ug", 256 * jj, 256 * jj + 256), w, AF.Copy)
-                    else:
-                        tt(R("Up", 256 * jj, 256 * jj + 256), w, gs, A.mult)
-                lv(r, "u1")
-                if q in UA:
-                    tt(R("Up", 512 * q, 512 * q + 512), R("Ug", 512 * q, 512 * q + 512), ps(4, 0, 512), A.mult)
-                mm([(ps(5, 64 * h + jj, 64 * h + jj + 185, 8), R("Up", 256 * jj + 128 * h, 256 * jj + 128 * h + 128), R("BB"))
-                    for jj in (2 * q, 2 * q + 1) for h in range(2)], start=False, stop=q == 3)
-            lv(r, "x1")
-            ts(R("R32"), ps(5, 0, 128), R8192, A.add, -R8192, A.add)
-            tt(R("Xs", 0, 256, 2, key="XsE"), ps(5, 0, 128), R("R32"), A.subtract)
-            ts(R("Xs", 1, 256, 2, key="XsO"), ps(5, 128, 256), R8192, A.add, -R8192, A.add)
-            xo = [R("Xs", key="XsO")]
+                mm([(P(bk, cK, h), H(a, h), m) for h in hs for a, m in [("Cold", I)] + ([("CMg", R("U1")), ("Hd", R("U2"))] if r else [])],
+                   stop=not OPT["key_pe"])
+            lv(r, "x" + t)
+            r32 = R("R32", c // 2, (c + n) // 2)
+            ts(r32, ps(bu, 0, n // 2), R8192, A.add, -R8192, A.add)
+            tt(R("Xs", c, c + n, 2), ps(bu, 0, n // 2), r32, A.subtract)
+            ts(R("Xs", c + 1, c + n, 2), ps(bu, n // 2, n), R8192, A.add, -R8192, A.add)
             if last:
-                mm([(ps(3, 128 * h, 128 * h + 128), R("Xs", 128 * h, 128 * h + 128, key="XsE"), I) for h in range(2)], more=xo, each=True)
-                act(R("us"), ps(3, 0, 256), AF.Sign)
-                mm([(ps(6, 0, 256), EX(0, "BY"), R("us"))])
-                act(R("d3"), ps(6, 0, 256), AF.Copy)
+                mm([(P(bk, cF, h), H("Xs", h), I) for h in hs], each=True)
+                act(H("us"), P(bk, cF), AF.Sign)
+                mm([(P(bk, cK), EX(0, "BY"), H("us"))])
+                act(H("d3"), P(bk, cK), AF.Copy)
                 return
-            ts(R("ut"), R("Xs", key="XsE"), -1.0, A.max, 1.0, A.min, more=xo)
+            ts(H("ut"), H("Xs"), -1.0, A.max, 1.0, A.min)
             if OPT["key_pe"]:
-                mm([(ps(6, 0, 256), I, R("ut"))], start=False)
-                scan(R("Km"), R("D0", 0, 256), ps(6, 0, 256), 0.0, A.add, A.max)
+                mm([(P(bk, cK), I, H("ut"))], start=False)
+                scan(H("Km"), R("D0", 0, n), P(bk, cK), 0.0, A.add, A.max)
             else:
-                tt(R("key"), ps(6, 0, 256), R("ut"), A.add)
-                scan(R("Km"), R("D0", 0, 256), R("key"), 0.0, A.add, A.max)
-            ki, mi = R("ki", 0, 16), R("mi", 0, 16)
-            ts(ki, R("Km", 15, 256, 16), 16.0, A.mult)
-            ts(mi, ki, 15, an)
-            ts(R("Mx", 0, 256, 16), mi, -1.0, A.mult, 15.0, A.add)
-            lv(r, "us1")
-            mm([(ps(3, 128 * h, 128 * h + 128), R("ut", 128 * h, 128 * h + 128), I) for h in range(2)], each=True)
-            act(R("us"), ps(3, 0, 256), AF.Copy)
-            o = ps(5, 256, 512)
-            mm([(o, R("KP"), R("CMg")), (o, R("PK"), R("us"))], stop=False)
-            mm([(ps(5, 256 + 128 * h, 384 + 128 * h), R("Mx", 128 * h, 128 * h + 128), I) for h in range(2)], start=False)
-            act(R("CMn"), o, AF.Copy)
+                tt(H("key"), P(bk, cK), H("ut"), A.add)
+                scan(H("Km"), R("D0", 0, n), H("key"), 0.0, A.add, A.max)
+            kr, km = R("kr", c // 16, (c + n) // 16), R("Km", c + 15, c + n, 16)
+            ts(kr, km, R1, A.add, -R1, A.add)
+            tt(R("Mx", c, c + n, 16), kr, km, A.subtract)
+            lv(r, "us" + t)
+            b3 = 3 + hs[0]
+            mm([(P(b3, 0, h), H("ut", h), I) for h in hs], each=True)
+            act(H("us"), P(b3, 0), AF.Copy)
+            mm([(P(bu, cN), R("KP"), H("CMg")), (P(bu, cN), R("PK"), H("us"))], stop=False)
+            mm([(P(bu, cN, h), H("Mx", h), R("I64")) for h in hs], start=False)
+            af(H("CMn"), P(bu, cN), None, b15)
+
+        def signs(c, n, ys):
+            pD = ps(7, c, c + n)
+            t = str((c + n) // 128 - 1)
+            lv(r, "t" + t)
+            mm([(pD, R("I32"), R("Zr", NL * r + c, NL * r + c + n)), (pD, R("TT"), R("V", c, c + n))], stop=False, more=zin)
+            lv(r, "g" + t)
+            for i, (a, y) in enumerate(ys):
+                mm([(ps(7, a, a + y["n"]), R("N256"), y)], start=False, stop=i == len(ys) - 1)
+            act(R("gs", c, c + n), pD, AF.Sign, bias=bG)
+            train(c, n)
+
         yb = NL * r
-        Y = {}
-        for n3, (l0, n) in enumerate(((0, 128), (128, 64), (192, 64))):
-            n2, c0 = l0 // 128, l0 % 128
-            pY = ps(0, l0, l0 + n)
+        Y = []
+        for l0, n in OPT["sets"]:
+            n3 = max(l0 // 64 - 1, 0)
             lv(r, "f%d" % n3)
-            for k0, k1 in OPT["sw"][n3]:
-                for k in range(k0, k1):
-                    lst = R("of", 64 * k + l0 // 4, 64 * k + (l0 + n) // 4)
-                    b = 16 * l0 + 4 * n * k
-                    vg, vp = R("Vg", b, b + 4 * n), R("Vp", b, b + 4 * n)
-                    if 4 * n3 + k in OPT["f_dve"]:
-                        ts(vg, IND(Fw, lst), -128.0, A.add)
-                    else:
-                        af(vg, IND(Fw, lst), None, -128.0)
-                    tt(vp, vg, ps(3 + n2, 4 * c0, 4 * c0 + 4 * n), A.mult)
-                    mm([(ps(5 + n2, 4 * c0 + n * k, 4 * c0 + n * k + n), I, R("Vp", b + x, b + 4 * n, 4)) for x in range(4)])
-                c = 4 * l0
-                tt(R("SW", c + n * k0, c + n * k1), ps(5 + n2, 4 * c0 + n * k0, 4 * c0 + n * k1), R("Wab", c + n * k0, c + n * k1), A.mult)
-                mm(([(pY, I, R("cy", 0, n))] if k0 == 0 else [])
-                   + [(pY, R("I32"), R("SW", c + n * k, c + n * k + n)) for k in range(k0, k1)], start=k0 == 0, stop=k1 == 4)
-            Y[n3] = R("Yb", 192 * me, 192 * me + 64) if n3 == 2 else R("Ys", yb + l0, yb + l0 + n)
-            ts(Y[n3], pY, R256, A.add, -R256, A.add)
+            for a, b, eng in OPT["fp"]:
+                if l0 <= a < l0 + n:
+                    plus(eng, R("Vg", 16 * a, 16 * b), IND(Fw, R("of", a, b)), -128.0)
+            pY = ps(OPT["y_banks"][n3], l0, l0 + n)
+            b, c, w = 16 * l0, 4 * l0, 4 * (l0 % 128)
+            for x0, x1 in OPT["sw"]:
+                for x in range(x0, x1):
+                    scan(R("Hs", b + 4 * n * x, b + 4 * n * x + 4 * n), R("Rt", c, c + 4 * n), R("Vg", b + x, b + 16 * n, 4), 0.0, A.mult, A.add)
+                tt(R("SW", c + n * x0, c + n * x1), R("Hs", b + 4 * n * x0 + 3, b + 4 * n * x1, 4),
+                   ps(3 + l0 // 128, w + n * x0, w + n * x1), A.mult)
+                mm(([(pY, I, R("cy", 0, n))] if x0 == 0 else [])
+                   + [(pY, R("I32"), R("SW", c + n * x, c + n * x + n)) for x in range(x0, x1)], start=x0 == 0, stop=x1 == 4)
+            if l0 + n < 128:
+                continue
+            y0, yn = ((0, 128), (128, 64), (192, 64))[n3]
+            y = R("Yb", 192 * me, 192 * me + 64) if n3 == 2 else R("Ys", yb + y0, yb + y0 + yn)
+            Y.append((y0, y))
+            ts(y, ps(OPT["y_banks"][n3], y0, y0 + yn), R256, A.add, -R256, A.add)
             if n3 < 2:
                 exchange("bk%d" % r, lambda o, yb=yb: T.Ys[:, yb + 64 * place(o, me):yb + 64 * place(o, me) + 64],
-                         lambda o: T.Yb[:, 192 * me:192 * me + 64], "Yin%d%d" % (r, n3), [Y[n3]],
+                         lambda o: T.Yb[:, 192 * me:192 * me + 64], "Yin%d%d" % (r, n3), [y],
                          [o for o in range(N) if place(o, me) == 2] if n3 else [o for o in range(N) if place(o, me) < 2])
-            if OPT["merge"] and n3 == 2:
-                pD = ps(7, 0, 256)
-                lv(r, "t1")
-                mm([(pD, R("I32"), Z), (pD, R("TT"), V)], stop=False, more=zin)
-                lv(r, "g1")
-                mm([(ps(7, 0, 128), R("N256"), Y[0]), (ps(7, 128, 192), R("N256"), Y[1])], start=False, stop=False)
-                mm([(ps(7, 192, 256), R("N256"), Y[2])], start=False)
-                act(R("gs"), pD, AF.Sign, bias=bG)
-                train_all()
-            if n3 == 1 or OPT["merge"]:
-                continue
-            c = 128 * n2
-            pD = ps(7, c, c + 128)
-            lv(r, "t%d" % n2)
-            mm([(pD, R("I32"), R("Zr", NL * r + c, NL * r + c + 128)), (pD, R("TT"), R("V", c, c + 128))], stop=False, more=zin)
-            lv(r, "g%d" % n2)
-            if n2:
-                mm([(ps(7, 128, 192), R("N256"), Y[1]), (ps(7, 192, 256), R("N256"), Y[2])], start=False)
-            else:
-                mm([(pD, R("N256"), Y[0])], start=False)
-            act(R("gs", c, c + 128), pD, AF.Sign, bias=bG)
-            train(n2, n2)
+            if OPT["merge_g"]:
+                if n3 == 2:
+                    signs(0, 256, Y)
+            elif n3 != 1:
+                signs(128 * (n3 // 2), 128, Y[1:] if n3 else Y)
 
         def scatter(w, src, c0, more=()):
             for t in [2 * place(q, me) + x for q in range(N - 1, -1, -1) for x in (1, 0)]:
-                o = IND(w, R("so", c0 + 2 * t, c0 + 2 * t + 2, key="sox"))
-                also = SO + list(more) + [R(src[-1])]
+                o = IND(w, R("so", c0 + 2 * t, c0 + 2 * t + 2))
+                also = [R("so")] + list(more) + [R(src[-1])]
                 if len(src) == 1:
                     cp(o, R(src[0], 32 * t, 32 * t + 32), also)
                 else:
@@ -864,6 +844,12 @@ def build(g, T, topo, core):
     return ops
 
 
+def meet(a, b):
+    if a["c0"] >= b["c1"] or b["c0"] >= a["c1"]:
+        return False
+    return (a["c0"] - b["c0"]) % math.gcd(a["st"], b["st"]) == 0
+
+
 def depend(ops):
     hist = {}
     bank = {}
@@ -883,8 +869,8 @@ def depend(ops):
                 if e == "pe":
                     dep.update(b[1][-2:])
                 b[1].append(i)
-            for j, c0, c1, jw in h:
-                if (w or jw) and c0 < v["c1"] and v["c0"] < c1:
+            for j, u, jw in h:
+                if (w or jw) and meet(u, v):
                     if e == "pe" and ops[j]["eng"] == e:
                         dep.add(j)
                     else:
@@ -892,8 +878,8 @@ def depend(ops):
         for v, w in acc:
             h = hist[v["key"]]
             if w:
-                h[:] = [x for x in h if not (v["c0"] <= x[1] and x[2] <= v["c1"])]
-            h.append((i, v["c0"], v["c1"], w))
+                h[:] = [x for x in h if not (v["c0"] <= x[1]["c0"] and x[1]["c1"] <= v["c1"] and x[1]["st"] % v["st"] == 0 and meet(x[1], v))]
+            h.append((i, v, w))
         wait.discard(i)
         dep.discard(i)
         op["wait"] = wait
@@ -944,7 +930,7 @@ def schedule(ops, p, others=()):
             lev[i] = min([lev[k] for k, d in succ[i]] + [1e4])
         else:
             r, name = ops[i]["lv"]
-            lev[i] = 100 * r + LEVEL.get(name, 0) + LEVEL.get("%s@%d" % (name, r), 0)
+            lev[i] = 100 * r + LEVEL.get(name, 0)
     key = [(lev[i], -tail[i], i) for i in range(n)]
     left = [len(q) for q in pred]
     ready = {e: [i for i in range(n) if eng[i] == e and not left[i]] for e in sorted(set(eng))}
@@ -971,7 +957,7 @@ def schedule(ops, p, others=()):
         for j, d in pred[i]:
             m |= above[j]
         before.append(set(j for j, d in pred[i] if not m >> j & 1))
-        above[i] = m | sum(1 << j for j in before[i])
+        above[i] = m | sum(1 << j for j in before[i] if j in ops[i]["wait"] or ops[j]["lat"] is None)
     after = [set() for _ in range(n)]
     for i in range(n):
         for j in before[i]:
@@ -1040,6 +1026,65 @@ def schedule(ops, p, others=()):
                 top = h2[last[e]] + cost[last[e]] + rest[k]
         return top
 
+    def pack(seq, cost, near):
+        h = [0.0] * n
+        busy = {e: ([], []) for e in set(eng)}
+        for i in seq:
+            t = 0.0
+            for j, d in near[i]:
+                if h[j] + d > t:
+                    t = h[j] + d
+            s, f = busy[eng[i]]
+            k = len(s)
+            while k and s[k - 1] >= t:
+                k -= 1
+            if k and f[k - 1] > t:
+                t = f[k - 1]
+            while k < len(s) and t + cost[i] > s[k]:
+                t = f[k]
+                k += 1
+            s.insert(k, t)
+            f.insert(k, t + cost[i])
+            h[i] = t
+        return h
+
+    def turn(seq, case, noise):
+        cost, near, sinks, far, lat = case
+        h = times(case, seq)[1]
+        back = [[(k, d - cost[i] + cost[k]) for k, d in far[i]] for i in range(n)]
+        fin = [h[i] + cost[i] + noise[i] for i in range(n)]
+        for i in range(n):
+            for j, d in near[i]:
+                fin[i] = max(fin[i], fin[j] + 1e-3)
+        tailed = [b + [] for b in back]
+        for i, c in sinks:
+            tailed[i] = [(i, c - cost[i])]
+        q = pack(sorted(range(n), key=lambda i: -fin[i]), cost, tailed)
+        late = [-(q[i] + cost[i]) for i in range(n)]
+        for i in range(n):
+            for j, d in near[i]:
+                late[i] = max(late[i], late[j] + 1e-3)
+        h = pack(sorted(range(n), key=lambda i: late[i]), cost, near)
+        for i in range(n):
+            for j, d in near[i]:
+                h[i] = max(h[i], h[j] + 1e-3)
+        return sorted(range(n), key=lambda i: h[i])
+
+    base = [times(c, order)[0] for c in cases]
+    rs = np.random.RandomState(OPT["seed"] + 1)
+    top = here = (float(len(cases)), order)
+    names = sorted(set(op["lv"] or (0, "") for op in ops))
+    part_of = np.array([names.index(op["lv"] or (0, "")) for op in ops])
+    for it in range(OPT["turns"]):
+        noise = rs.random_sample(n) * rs.random_sample() * OPT["noise"]
+        noise += ((rs.random_sample(len(names)) - 0.5) * (rs.random_sample(len(names)) < OPT["share"]))[part_of] * OPT["shove"]
+        new = turn(here[1], cases[it % len(cases)], noise.tolist())
+        v = sum(times(c, new)[0] / b for c, b in zip(cases, base))
+        if v < here[0] - math.log(rs.random_sample() + 1e-12) * OPT["warm"] * (1 - it / OPT["turns"]):
+            here = (v, new)
+        if v < top[0]:
+            top = (v, new)
+    order = top[1]
     draws = np.random.RandomState(OPT["seed"]).random_sample((OPT["moves"], 5)).tolist()
     now = [times(c, order) for c in cases]
     rest = [tails(c, order, n - 1, [0.0] * n) for c in cases]
@@ -1095,12 +1140,14 @@ def schedule(ops, p, others=()):
             edges = None
             if end < best[0]:
                 best = (end, order)
+    ALL[:] = [times(c, best[1])[0] for c in cases]
     end, h, by, at = times(cases[0], best[1])
     price(ops, p)
     return best[1], [h[i] + op["cost"] + op["l"] for i, op in enumerate(ops)]
 
 
 ORDERS = {}
+ALL = []
 
 
 def emit(g, T, ops, order, ends):

import math
import numpy as np
from concourse.bass import DstId, RemoteDMATransfer
from concourse.mybir import AluOpType as A
from concourse.mybir import ActivationFunctionType as AF

RO, NS, NL, WC = 4, 192, 256, 4096
TW = 4144
MB = 272
OFFS = (0, 53, 211, 264)
R1, R16, R256, R4096, R8192 = 1.5 * 2 ** 23, 1.5 * 2 ** 27, 1.5 * 2 ** 31, 1.5 * 2 ** 35, 1.5 * 2 ** 36
OPT = dict(
    merge=True, merge_g=False, f_bank=2, key_pe=False,
    gp=((0, 16, "act"), (16, 32, "dve"), (32, 48, "act"), (48, 64, "dve")),
    o_banks=(2, 6), pf0=(3, 4, 3, 4),
    sets=((0, 64), (64, 64), (128, 64), (192, 64)),
    fp=((0, 32, "dve"), (32, 64, "act"), (64, 96, "dve"), (96, 128, "act"), (128, 192, "act"), (192, 256, "act")),
    sw=((0, 4),),
    ug=((0, 128, "act"), (128, 256, "act")),
    pf_banks=(3, 4, 3, 4), pf_dve=((), ()), rt_eng="pool", late_eng="pool", e_banks=(2, 1), wr_act=True, of_split=(0, 256), x_eng="act",
    y_banks=(0, 6, 6), eq_pool=True,
    turns=1500, noise=150.0, share=0.05, shove=5000.0, warm=0.0015, hold=0.4, moves=90000, heat=40.0, drift=0.5, seed=0)
LEVEL = dict(c1=-95, cold=105, e=117, f0=18, f1=28, f2=125, fn0=65, fn1=8, fold=-57, fs=30, g0=25, g1=145, g2=-10, home=10, kc=-7, keys=6,
             late=50, ms=-80, of=2, pf0=10, pf1=-90, r0=-330, rest=-30, rt=-7, scan=-325, t0=225, t1=265, u0=93, u1=108, ug=57, us1=48,
             v=-25, w=-5, x1=-33, yc=100)

SCRATCH = {}
PART = {}


def _s(dt, cols, *names):
    for n in names:
        SCRATCH[n] = ("sbuf", [128, cols], dt)


def _p(dt, cols, whole, *names):
    _s(dt, cols * len(names), whole)
    for i, n in enumerate(names):
        PART[n] = (whole, cols * i, cols)


_s("bfloat16", TW, "Ct", "Ft")
_s("bfloat16", MB + TW, "Ms")
_s("float32", TW, "K")
_s("float32", 2048, "PF0", "PF1", "Up", "Ug")
_s("int32", 16, "ic")
_s("float32", 128, "col")
_p("float32", 16, "sixteen", "OH", "LT", "L4", "L8", "icf", "cv")
_p("bfloat16", 144, "wide", "DI", "DG", "C4", "Big", "B4", "Bd", "Bt", "Bt1", "Bt2", "EX0", "BY", "HS", "HK", "HE", "HX", "H90", "H3", "H4",
   "H5", "HD", "HA", "HB", "HL", "w1", "w2")
_p("bfloat16", 128, "tiles", "CE", "CEb", "CEm", "CK", "C16", "I", "NI", "I64", "I8192", "I256", "N256", "BO", "C8", "GB", "ST", "STA",
   "WR", "HM", "TT", "RA", "RB", "B1", "KP", "PK", "U1", "U2", "YW", "WT", "t1", "t2", "t3", "t4", "t5", "t6", "t7", "t8",
   "EQ1", "EQ2", "EQ3", "EL0", "EL1", "EL2", "EL3", "hb", "HK2", "N4096")
_p("bfloat16", 64, "narrow", "J", "kb", "fl")
_s("float16", 128, "CB")
_s("float16", 64, "ks")
_s("float16", 32, "Kh")
_s("float32", 128, "I32", "R32", "PA")
_s("float32", 24 if OPT["merge"] else 16, "BB")
_s("bfloat16", 2048, "Sel", "DM")
_s("bfloat16", 512, "D0", "Mt", "RS0", "J512")
_s("bfloat16", 272, "RS1")
_s("float32", 512, "Z0")
_s("float32", 272, "Z1")
_s("bfloat16", 256, "V", "wr", "Wp", "gs", "CMg", "Hd", "Cold", "Fold", "CMn", "Fnew", "us", "Xs", "ut", "key", "Mx", "mt")
_s("bfloat16", NS, "CAP", "tb", "Sb", "ycl", "sg", "cum", "P", "DA")
_s("bfloat16", 128, "cy", "CL")
_s("bfloat16", 4 * NS, "Yg", "Sg", "Yb")
_s("int32", NS, "X0", "vi", "hm", "hn")
_s("float32", NS, "Tf", "Sf", "yso", "yxo", "sc")
_s("float32", 64, "em", "tab", "pu")
_s("float32", 16, "kr")
_s("float32", 16 * NS, "Zs")
_s("float32", 4 * NL, "Zr", "SW")
_s("bfloat16", 4 * NL, "Ys", "G", "Rt")
_s("uint16", 64, "dst", "om", "kl", "bl")
_s("uint16", 256, "of")
_s("uint16", 32, "so")
_s("float32", 256, "yco", "ycg", "d3", "Km")
_s("int32", 256, "ki", "mi")
_s("bfloat16", 4096, "Vg")
_s("float16", 4096, "Hs")
for _i in range(8):
    SCRATCH["ps%d" % _i] = ("psum", [128, 512], "float32")

NDMA = 28
SEMAPHORES = ["dve", "act", "pe", "pool", "sent"] + ["fw%d" % r for r in range(RO)] + ["bk%d" % r for r in range(RO)] + [
    "d%d" % i for i in range(NDMA)]
TWO = {"bfloat16", "float16", "uint16"}
GUESS = dict(cyc=0.87, fv=48, fa=95, gat=1.56, sca=3.8, pe=0.52, hop=130, same=70, rem=2900, dma=0.85, tt2=1.0)
OTHERS = (dict(cyc=1.1, pe=0.62, gat=1.9, sca=5.0, tt2=2.0), dict(hop=200, same=100, rem=4200, dma=1.1, pe=0.45, gat=1.2, sca=2.5))


def build(g, T, topo, core):
    me = T.rank_of(core)
    N = len(T.cores)
    ops = []
    ndma = [0]
    level = [None]
    cols = {}

    def R(name, c0=0, c1=None, st=1, key=None):
        buf, o, w = PART.get(name) or (name, 0, SCRATCH[name][1][1])
        if c1 is None:
            c1 = w
        ap = T[buf][:, o + c0:o + c1:st] if st > 1 else T[buf][:, o + c0:o + c1]
        return dict(ap=ap, key=key or name, c0=c0, c1=c1, st=st, n=len(range(c0, c1, st)), dt=SCRATCH[buf][2], ps=SCRATCH[buf][0] == "psum")

    def X(key):
        return dict(key=key, c0=0, c1=1, st=1, ps=False)

    def IND(win, off):
        return dict(ap=win["ap"].indirect(off["ap"]), n=16 * off["n"], ind=(win, off), dt=win["dt"], ps=False)

    def parts(v):
        if not isinstance(v, dict):
            return []
        return list(v["ind"]) if "ind" in v else [v]

    def ap(v):
        return v["ap"] if isinstance(v, dict) else v

    def add(eng, fn, out, ins, size, more=(), sem=None, lat=None):
        rd = []
        for v in ins:
            rd += parts(v)
        wr = []
        for o in out:
            if "ind" in o:
                wr.append(o["ind"][0])
                rd.append(o["ind"][1])
            else:
                wr.append(o)
        ops.append(dict(eng=eng, fn=fn, rd=rd + list(more), wr=wr, size=size, sem=sem, lat=lat, after=[], lv=level[0]))
        return ops[-1]

    def lv(r, name):
        level[0] = (r, name)

    def vsize(out, ins, two=False):
        if "ind" in out:
            return ("sca", out["n"])
        if any("ind" in v for v in ins):
            return ("gat", out["n"])
        half = all(v["dt"] in TWO for v in [out] + ins)
        if two and not any(v["ps"] for v in ins):
            return ("tt2", out["n"]) if half else ("el", 2 * out["n"])
        return ("el", out["n"] // 2 if half else out["n"])

    def ts(out, a, s1, o1, s2=None, o2=None, more=()):
        if o2 is None:
            fn = lambda: g.vector.tensor_scalar(out["ap"], a["ap"], ap(s1), None, o1)
        else:
            fn = lambda: g.vector.tensor_scalar(out["ap"], a["ap"], ap(s1), ap(s2), o1, o2)
        return add("dve", fn, [out], [a, s1, s2], vsize(out, [a]), more)

    def tt(out, a, b, op, more=()):
        return add("dve", lambda: g.vector.tensor_tensor(out["ap"], a["ap"], b["ap"], op), [out], [a, b], vsize(out, [a, b], True), more)

    def cp(out, a, more=()):
        return add("dve", lambda: g.vector.tensor_copy(out["ap"], a["ap"]), [out], [a], vsize(out, [a]), more)

    def ms(out, v):
        return add("dve", lambda: g.vector.memset(out["ap"], v), [out], [], vsize(out, []))

    def scan(out, d0, d1, init, o0, o1):
        add("dve", lambda: g.vector.tensor_tensor_scan(out["ap"], d0["ap"], d1["ap"], ap(init), o0, o1), [out], [d0, d1, init],
            vsize(out, [d0, d1]))

    def act(out, a, f, bias=None, scale=None, more=()):
        kw = {}
        if bias is not None:
            kw["bias"] = ap(bias)
        if scale is not None:
            kw["scale"] = ap(scale)
        return add("act", lambda: g.scalar.activation(out["ap"], a["ap"], f, **kw), [out], [a, bias, scale],
                   ("gat" if "ind" in a else "el", out["n"]), more)

    def af(out, a, scale=None, bias=None):
        return act(out, a, AF.Identity, bias=bias, scale=scale)

    def plus(eng, out, a, c, more=()):
        if eng == "pool":
            return add("pool", lambda: g.affine_select(out["ap"], a["ap"], [[0, out["n"]]], A.is_ge, 0.0, 0, 0), [out], [a],
                       ("iota", out["n"] + 20), more)
        return act(out, a, AF.Identity, bias=c, more=more) if eng == "act" else ts(out, a, c, A.add, more=more)

    def mm(items, start=True, stop=True, more=(), each=False):
        def fn():
            ins = None
            for i, (o, l, r) in enumerate(items):
                ins = g.tensor.matmul(o["ap"], l["ap"], r["ap"], each or (start and i == 0), each or (stop and i == len(items) - 1))
            return ins
        c = sum(max(64, r["n"]) * (4 if r["dt"] == "float32" else 1) for o, l, r in items)
        rd = []
        for o, l, r in items:
            rd += [l, r]
        return add("pe", fn, [o for o, l, r in items], rd, ("mm", c), more)

    def iota(out, pat, base, cm):
        if out["dt"] == "int32":
            fn = lambda: g.iota(out["ap"], pat, base, cm)
        else:
            fn = lambda: g.iota(out["ap"], pat, base, cm, allow_small_or_imprecise_dtypes=True)
        return add("pool", fn, [out], [], ("iota", out["n"]))

    def fill(out, v):
        return iota(out, [[0, out["n"]]], v, 0)

    def dma(q, pairs, wr, rd, lat, acc=False):
        sem = "d%d" % ndma[0]
        ndma[0] += 1

        def fn():
            for o, i in pairs:
                if acc:
                    g.dma_start(o, i, accum_op=A.add).then_inc(T.sem[sem], 16)
                else:
                    (g.sync if q == "sp" else g.scalar).dma_start(o, i).then_inc(T.sem[sem], 16)
        return add(q, fn, wr, rd, ("fix", (800 if acc else 60) * len(pairs)), sem=(sem, 16 * len(pairs)), lat=("dma", lat))

    def exchange(sem, src, dst, key, rd, peers):
        eng = topo.engines(core, T.cores[peers[0]])
        half = len(eng) // 2
        m0 = sum(1 << e for e in eng[:half])
        m1 = sum(1 << e for e in eng[half:])
        far = [o for o in peers if o // 2 != me // 2]
        near = [o for o in peers if o // 2 == me // 2]

        def fn():
            tr = []
            for o, m in zip(far, (m0, m1)):
                rid, pid, _e = topo.addr(T.cores[o])
                tr.append(RemoteDMATransfer(dst_ids=[DstId(rid=rid, pnc=pid)], dma_engine_mask=m, remote_sem=T.sem[sem],
                                            src=src(o), dst=dst(o)))
            if tr:
                g.remote_dma_fused(tr, local_sem=T.sem["sent"])
            for o in near:
                rid, pid, _e = topo.addr(T.cores[o])
                g.remote_dma(dst(o), src(o), T.sem[sem], T.sem["sent"], pid, rid, m0 | m1)
        calls = len(far) // 2 + len(near)
        op = add("pool", fn, [X(key)], rd, ("fix", 200 * calls), sem=(sem, 2 * len(eng)), lat=("rem", 0.55 + 0.15 * len(peers)))
        op["sent"] = calls * len(eng)
        return op

    def place(q, o):
        return 3 if q == o else 2 if q // 2 == o // 2 else q % 2

    def C(name):
        i = cols.setdefault(name, len(cols))
        return R("col", i, i + 1)

    def lin(name, a, scale=None, bias=None):
        af(C(name), a, scale, bias)
        return C(name)

    def OH(i):
        return R("OH", i, i + 1)

    def LT(i):
        return R("LT", i, i + 1)

    def ic(i):
        return R("ic", i, i + 1)

    def win(name, s):
        return R(name, s, s + 128)

    def EX(rho, name="Big"):
        return win(name, 15 - rho)

    def ps(b, c0, c1, st=1):
        return R("ps%d" % b, c0, c1, st)

    def SEL(i):
        return R("Sel", 128 * i, 128 * i + 128)

    def pick(out, index, target, coef=None):
        if coef is None:
            ts(out, index, target, A.is_equal)
        else:
            ts(out, index, target, A.is_equal, coef, A.mult)

    def two(out, index, a, b, t):
        pick(R(t[0]), index, *a)
        pick(R(t[1]), index, *b)
        tt(out, R(t[0]), R(t[1]), A.add)

    I = R("I")
    add("dve", lambda: g.vector.memset(T.X0[:], 0), [X("X0z")], [], ("el", NS))
    prev = None
    for k in range(4):
        op = dma("sp", [(T.Ct[:, 1024 * k:1024 * k + 1024], T.cf[:, 1024 * k:1024 * k + 1024])], [R("Ct", 1024 * k, 1024 * k + 1024)], [],
                 2600 + 1100 * k)
        op["after"] = [prev] if prev else []
        prev = op
    dma("act", [(T.X0[e::16, :], T.x0[e::4, :]) for e in range(4)], [R("X0")], [X("X0z")], 2200)
    dma("act", [(T.tb[:], T.tg[:])], [R("tb")], [], 2200)
    ms(R("Ms", 0, 1104), 0.0)
    op = dma("sp", [(T.Ms[:, 1104 * k:1104 * k + 1104], T.Ms[:, 0:1104]) for k in range(1, 4)], [R("Ms", 1104, MB + TW)],
             [R("Ms", 0, 1104)], 8600)
    op["after"] = [prev]
    prev = op
    for k in range(2):
        op = dma("sp", [(T.Ft[:, 2048 * k:2048 * k + 2048], T.ft[:, 2048 * k:2048 * k + 2048])], [R("Ft", 2048 * k, 2048 * k + 2048)], [],
                 10800 + 2200 * k)
        op["after"] = [prev]
        prev = op
    iota(R("ic", 0, 2), [[-48, 2]], 48, 16)
    iota(R("ic", 2, 3), [[0, 1]], 0, 4)
    iota(R("ic", 3, 4), [[0, 1]], 0, 8)
    iota(R("ic", 4, 5), [[0, 1]], 0, 1)
    iota(R("icf", 0, 1), [[0, 1]], 0, 1)
    iota(R("J", 0, 16), [[1, 16]], 0, 0)
    iota(R("DI"), [[1, 144]], 0, -1)
    iota(R("CE"), [[16, 8], [0, 4], [1, 4]], 0, 0)
    iota(R("CEb"), [[16, 8], [-8, 2], [0, 8]], 8, 0)
    iota(R("C4"), [[1, 36], [0, 4]], 0, 0)
    iota(R("C16"), [[1, 8], [0, 16]], 0, 0)
    iota(R("C8"), [[1, 16], [0, 8]], -8, 0)
    iota(R("J512"), [[0, 32], [-1, 16]], 15, 0)
    sh, an = A.arith_shift_right, A.bitwise_and
    ts(R("ic", 5, 8), R("ic", 0, 3), 4, sh, 3, an)
    ts(R("ic", 8, 11), R("ic", 1, 4), 4, sh, 1, an)
    ts(ic(11), ic(4), 4, sh)
    cp(R("icf", 5, 12), R("ic", 5, 12))
    p_, e1_, e_, s_, b0, b2, b1, gr = [R("icf", i, i + 1) for i in (0, 5, 6, 7, 8, 9, 10, 11)]
    r_ = C("r")
    ts(r_, gr, -16.0, A.mult, p_, A.add)
    g16 = lin("g16", gr, 16.0)
    w_ = lin("w", s_, 2.0, b1)

    def diag(out, pat, base, v):
        n = out["n"]
        add("pool", lambda: g.affine_select(out["ap"], R("DM", 0, n)["ap"], pat, A.not_equal, v, base, -1), [out], [R("DM", 0, n)],
            ("iota", n + 20))
    ms(R("DM", 0, 512), 0.0)
    J16 = R("J", 0, 16)
    ts(R("OH"), J16, r_, A.is_equal)
    ts(R("LT"), J16, r_, A.is_gt)
    ts(R("DG"), R("DI"), r_, A.add)
    DI, DG, DG1 = R("DI", 0, 128), R("DG"), R("DG", 0, 128)
    pick(I, DI, 0.0)
    pick(R("Big"), DG, 15.0)
    pick(R("ST"), R("CE"), p_)
    tt(R("CEm"), R("CE"), R("CEb"), A.min)
    pick(R("STA"), R("CEm"), p_)
    tE = lin("tE", g16, None, e_)
    tE1 = lin("tE1", g16, None, e1_)
    pick(R("WR"), R("CE"), tE, lin("cWR", LT(8), -32768.0))
    ts(R("L4"), R("LT"), LT(4), A.subtract)
    ts(R("L8"), R("LT"), LT(8), A.subtract)
    r45, r47, r411, r414 = [R("L4", j, j + 1) for j in (6, 8, 12, 15)]
    r811, r812, r813 = [R("L8", j, j + 1) for j in (12, 13, 14)]
    cP = lin("cP", OH(15), -0.5, lin("cP0", r812, 0.5))
    two(R("HM"), R("CE"), (tE, cP), (tE1, lin("cM", r813, -0.5)), ("t1", "t2"))
    act(C("r8"), r_, AF.Relu, bias=-8.0)
    bsg = lin("bsg", C("r8"), -16384.0, lin("bsg0", r47, -65536.0, 128.0))
    o192 = lin("o192", lin("h192", LT(12), -192.0, 192.0), e_)
    init = lin("init", r811, -1.0, o192)
    cap = lin("cap", r811, 1024.0, o192)
    rows = {"b0": ((-464, -176), (4, -640), (5888, -5120), (15, 1), (-1, 14), (3, 1), (2, -1), (-6, -2)),
            "b1": ((2, -319), (-1, 1), (-60, 64)),
            "r": ((1, 4112), (1, 4128), (1, 1), (2, -8), (2, -7))}
    at, made = 0, []
    for x, name in ((b0, "b0"), (b1, "b1"), (r_, "r")):
        n = len(rows[name])
        for i, (a, b) in enumerate(rows[name]):
            iota(R("tab", at + i, at + i + 17, 16), [[b - a, 2]], a, 0)
            made.append(R("tab", 32 + at + i, 33 + at + i))
        af(R("tab", 48 + at, 48 + at + n), R("tab", at, at + n), x)
        tt(R("tab", 32 + at, 32 + at + n), R("tab", 48 + at, 48 + at + n), R("tab", 16 + at, 16 + at + n), A.add)
        at += n
    aBest0, aBlk, lBest0, cPK, tPY, qa, sa, cRB, bVar, nb1, qb, spE, spO, r1, tU, tU1 = made
    act(C("e0"), e_, AF.Relu, bias=1.0, scale=-1.0)
    bT = lin("bT", s_, 256.0, lin("bT0", C("e0"), 16384.0))
    af(R("CAP"), R("tb"), 0.0, cap)
    af(R("Tf"), R("tb"), None, bT)
    ms(R("D0"), 1.0 / 64)
    ms(R("D0", 0, 512, 16), -1024.0)
    for o in range(N):
        fill(R("Zs", 192 * o, 192 * o + 64), 0)
        fill(R("Yb", 192 * o + 64, 192 * o + 192), 0)
    dma("sp", [(T[n][:, WC:TW], T.DM[:, 0:TW - WC]) for n in ("Ct", "Ft")] + [(R("HE")["ap"], T.DM[:, 0:144])],
        [R("Ct", WC, TW), R("Ft", WC, TW), R("HE")], [R("DM", 0, 144)], 2400)
    fill(R("K", WC, TW), 0)
    pick(R("B4"), R("C4"), lin("g43", gr, 4.0, 3.0))
    B4 = R("B4")
    tt(R("cv", 0, 4), R("OH", 0, 4), R("OH", 12, 16), A.add)
    tt(R("cv", 4, 6), R("cv", 0, 2), R("OH", 4, 6), A.subtract)
    tt(R("cv", 6, 7), R("cv", 0, 1), OH(8), A.subtract)
    tt(R("cv", 7, 8), OH(5), R("cv", 5, 6), A.subtract)
    smA, smB, a2, dB = [R("cv", j, j + 1) for j in (4, 5, 6, 7)]
    sgn = lin("sgn", b2, 2.0, -1.0)
    af(R("HS"), B4, lin("nod", lin("nod0", sgn, -1.0), C("e0")))
    for k, c in enumerate((OH(4), OH(8), a2, smA)):
        af(R("HK", k, 144, 4), R("B4", k, 144, 4), c)
    ts(R("HE", 1, 144, 4), R("B4", 1, 144, 4), dB, A.mult, 2.0, A.mult)
    ts(R("HE", 2, 144, 4), R("B4", 2, 144, 4), dB, A.mult, -2.0, A.mult)
    ts(R("HX", 0, 144, 2), R("B4", 0, 144, 2), OH(5), A.mult, 2.0, A.mult)
    ts(R("HX", 1, 144, 2), R("B4", 1, 144, 2), smB, A.mult, 2.0, A.mult)
    q4 = lin("q4", b0, lin("q4a", b1, 56.0, 576.0), lin("q4b", b1, -1340.0, 1552.0))
    af(R("H3"), B4, lin("h3", lin("h3a", q4, LT(4)), b1))
    ts(R("H4"), B4, OH(2), A.mult, 4.0, A.mult)
    ts(R("H5"), B4, OH(3), A.mult, 2.0, A.mult)
    ts(R("HD"), B4, OH(0), A.mult, -256.0, A.mult)
    tL = lin("tL", r45, None, 12.0)
    tA = lin("tA", r45, -1.0, 13.0)
    pick(R("HA"), DG, tA, lin("ha", OH(6), 4.0, OH(4)))
    pick(R("HB"), DG, tA, lin("hb", b0, lin("hba", r47, 2.0)))
    cs = lin("cs", LT(4), -4.0, 1.0)
    cI = lin("cI", lin("cI2", lin("cI1", lin("cI0", sgn, -1.0, cs), b1, sgn), qa), qb)
    two(R("HL"), DG, (tL, lin("hl", q4, r47)), (14.0, cI), ("w1", "w2"))
    aBest, lBest = lin("aBest", aBest0, nb1), lin("lBest", lBest0, nb1)
    z64 = R("Big", 0, 64)
    ts(R("CB", 0, 64), z64, 0.0, A.mult, -319.0, A.add)
    ts(R("CB", 64, 128), z64, 0.0, A.mult, bVar, A.add)
    fill(R("CL", 0, 64), -5120)
    af(R("CL", 64, 128), z64, 0.0, lBest)
    fill(R("DA", 0, NS, 3), 0)
    fill(R("Rt", 0, 1024, 4), 0)
    af(R("cy"), R("Big", 0, 128), 0.0, -127.5)
    pick(R("Bd"), R("DI"), 12.0, LT(4))
    pick(R("Bt"), DG, lin("tBt", r_, 0.25, 12.0))
    pick(R("Bt1"), DG, lin("tBt1", r_, 0.25, 11.75))
    pick(R("Bt2"), DG, lin("tBt2", r_, 0.25, 11.5))
    pick(R("B1"), R("C4", 0, 128), lin("tB1", p_, 0.25, -0.25), 0.0625)
    cB1 = lin("cB1", e_, 256.0, 128.0)
    af(R("EX0"), R("Big"), OH(0))
    for l in range(4):
        if l and OPT["eq_pool"]:
            diag(R("EQ%d" % l), [[16, 8], [0, 4], [1, 4]], 4 * l, 1.0)
        elif l:
            ts(R("EQ%d" % l), R("CE"), 4.0 * l, A.add, p_, A.is_equal)
        diag(R("EL%d" % l), [[16, 8], [1, 4], [0, 4]], 4 * l, 1064.0)
    mm([(ps(7, 256, 384), win("HK", 12), I)])
    af(R("t8"), ps(7, 256, 384), 97.0)
    diag(R("CK"), [[16, 8], [1, 4], [0, 4]], 0, 16.0)
    mm([(ps(7, 384, 512), R("t8"), R("CK"))])
    act(R("HK2"), ps(7, 384, 512), AF.Copy)
    pick(R("BO"), R("C16"), gr)
    BO = R("BO")
    od = lin("od", sgn, nb1)
    ts(R("RA"), BO, od, A.mult, -2.0, A.mult)
    ts(R("RB"), BO, od, A.mult, lin("cRB", cRB, None, 4.0), A.mult)
    iota(R("t3"), [[0, 32], [1, 4]], -2, 0)
    iota(R("t4"), [[0, 8], [1, 4], [0, 4]], -2, 0)
    iota(R("t5"), [[0, 2], [-1, 4], [0, 16]], 2, 0)
    iota(R("t6"), [[-1, 2], [0, 64]], 2, 0)
    af(R("t3"), R("t3"), sa, 2.0)
    af(R("t4"), R("t4"), lin("sb", nb1, -2.0, 1.0), 2.0)
    tt(R("t5"), R("t5"), R("t6"), A.mult)
    tt(R("t3"), R("t3"), R("t4"), A.mult)
    tt(R("WT"), R("t3"), R("t5"), A.mult)
    for q in range(4):
        diag(R("Sel", 512 * q, 512 * q + 512), [[1, 4], [16, 8], [0, 16]], 4 * q, 1.0)
    for name, v in (("I32", 1.0), ("I256", 1.0 / 256), ("N256", -1.0 / 256), ("NI", -1.0), ("I64", 64.0), ("I8192", 8192.0), ("N4096", -4096.0)):
        diag(R(name), [[1, 128]], 0, v)
    pick(R("TT"), R("CE"), tE, -256.0)
    bG = lin("bG", s_, -256.0, 163840.0 - 128.0)
    pick(R("RS0"), R("J512"), r_)
    fill(R("RS1"), 0)
    fill(R("RS1", 0, 272, 17), 1)
    if OPT["merge"]:
        iota(R("J", 32, 64), [[0, 2], [1, 16]], 0, 0)
        pick(R("BB"), R("J", 32, 56), gr)
    else:
        iota(R("J", 32, 48), [[0, 2], [1, 8]], 0, 0)
        pick(R("BB"), R("J", 32, 48), gr)
    pick(R("GB"), R("C8"), gr, 2.0 ** 20)
    af(R("KP"), I, r414)
    two(R("PK"), DG1, (lin("tPK", w_, None, 4.0), cPK), (tPY, r1), ("t1", "t2"))
    pick(R("U1"), DG1, tU, r411)
    pick(R("t7"), DG1, tU1, lin("cU", r411, 0.0625))
    tt(R("U2"), R("t7"), R("U1"), A.subtract)
    fill(R("Mx"), 0)
    b15 = lin("b15", OH(0), 15.0)
    af(R("BY"), R("Big"), r1)
    af(R("YW"), BO, lin("yw", r811, -64.0))

    MSK = [X("Ms%d" % x) for x in range(4)]
    Mw = R("Ms", MB, MB + TW)

    def shift():
        pairs = [(T.Ms[x::16, MB - OFFS[x]:MB - OFFS[x] + WC], T.Ms[0::16, MB:MB + WC]) for x in (1, 2, 3)]
        pairs += [(T.Ms[x::16, MB + WC - OFFS[x]:MB + WC], T.Ms[0::16, MB:MB + OFFS[x]]) for x in (1, 2, 3)]
        dma("sp", pairs, MSK[1:4], [MSK[0], R("Ms")], 2800)

    def pairs_of(r, banks):
        for c in range(4):
            lv(r, "pf%d" % (c // 2))
            for jj in (2 * c, 2 * c + 1):
                o = ps(banks[c], 256 * (jj % 2), 256 * (jj % 2) + 256)
                mm([(o, I, R("Ft", 2 * jj, WC, 16)), (o, R("I8192"), R("Ft", 2 * jj + 1, WC, 16))])
            plus("dve" if c in OPT["pf_dve"][min(r, 1)] else "act", R("PF%d" % (r % 2), 512 * c, 512 * c + 512), ps(banks[c], 0, 512), -2.0 ** 20)

    lv(0, "scan")
    for b in range(8):
        bank = 3 + b % 4
        mm([(ps(bank, 128 * c, 128 * c + 128), R("Ct", 512 * b + 128 * c, 512 * b + 128 * c + 128), I) for c in range(4)], each=True)
        scan(R("K", 512 * b, 512 * b + 512), R("D0"), ps(bank, 0, 512), 0.0, A.add, A.max)
    for q in range(8):
        ts(R("ki", 32 * q, 32 * q + 32), R("K", 16 * q + 15, 4096, 128), 64.0, A.mult)
    ts(R("mi"), R("ki"), 15, A.bitwise_and)
    ts(R("mt"), R("mi"), -1.0, A.mult, 15.0, A.add)
    mm([(ps(3, 128 * h, 128 * h + 128), R("mt", h, 256, 2), I) for h in range(2)], each=True)
    act(R("Mt", 0, 256), ps(3, 0, 256), AF.Copy)

    def first(x):
        b = MB - OFFS[x]
        pr = [(T.Ms[x::16, b:b + WC], T.Mt[:, 0:256])]
        n = min(OFFS[x], 256)
        if n:
            pr.append((T.Ms[x::16, b + WC:b + WC + n], T.Mt[0::16, 0:n]))
        if OFFS[x] > n:
            pr.append((T.Ms[x::16, b + WC + n:MB + WC], T.Mt[1::16, 0:OFFS[x] - n]))
        return pr
    dma("sp", first(0) + first(3), [MSK[0], MSK[3]], [R("Mt", 0, 256), R("Ms")], 2400)
    dma("act", first(1) + first(2), MSK[1:3], [R("Mt", 0, 256), R("Ms")], 2400)

    lv(0, "yc")
    for q in range(8):
        mm([(ps(0, 0, 256), EX(h, "BY"), R("Ct", 256 * h, 256 * h + 256)) for h in (2 * q, 2 * q + 1)], start=q == 0, stop=q == 7)
    act(R("yco"), ps(0, 0, 256), AF.Copy)
    dma("sp", [(T.K[0::16, 0:WC], T.yco[:])], [R("K")], [R("yco")], 2400)

    def route(r):
        src = [R("Sb")] + ([R("ycl")] if r else [])
        for i, v in enumerate(src):
            mm([(ps(7, 0, NS), R("STA"), v)], start=i == 0, stop=i == len(src) - 1)
        act(R("sg"), ps(7, 0, NS), AF.Sign, bias=bsg)
        if r < RO:
            mm([(ps(7, NS, 2 * NS), R("HM"), R("sg"))])
        pX = ps(2, 0, NS)
        mm([(pX, R("ST"), v) for v in src] + [(pX, R("WR"), R("sg"))])
        if r == RO:
            act(R("yxo"), pX, AF.Copy, scale=1.0 / 256)
            return None
        act(R("Sf"), pX, AF.Copy)
        scan(R("cum"), ps(7, NS, 2 * NS), R("CAP"), init, A.add, A.min)
        tt(R("P"), ps(7, NS, 2 * NS), R("cum"), A.mult)
        mm([(ps(7, 448, 460), EX(rho), R("P", rho, NS, 16)) for rho in range(16)])
        d = R("dst", 16 * r, 16 * r + 12)
        cp(d, ps(7, 448, 460))
        w = R("Zs", 768 * r, 768 * r + 768)
        tt(IND(w, d), R("Tf"), R("Sf"), A.add)
        b = 768 * r
        op = exchange("fw%d" % r, lambda o: T.Zs[:, b + 192 * o:b + 192 * o + 64],
                      lambda o: T.Zr[:, NL * r + 64 * place(me, o):NL * r + 64 * place(me, o) + 64],
                      "Zin%d" % r, [w] + ([R("Yg", NS * (r - 1), NS * r)] if r else []), [o for o in range(N) if o != me])
        plus(OPT["late_eng"], R("Zr", NL * r + 192, NL * r + 256), R("Zs", b + 192 * me, b + 192 * me + 64), 0.0)["after"] = [op]
        lv(max(r - 1, 0), "late")
        plus(OPT["late_eng"], R("Sb"), R("Sf"), 0.0)["after"] = [op]
        act(R("Sg", NS * r, NS * r + NS), R("P"), AF.Sign, bias=-63.5)
        return op

    lv(0, "r0")
    ts(R("Sb"), R("X0"), 256.0, A.mult)
    sent0 = route(0)
    level[0] = None
    for r in range(1, RO):
        for o in range(N):
            fill(R("Zs", 768 * r + 192 * o, 768 * r + 192 * o + 64), 0)["after"] = [sent0]

    if OPT["pf0"]:
        pairs_of(0, OPT["pf0"])
    for r in range(RO):
        last = r == RO - 1
        PF = "PF%d" % (r % 2)
        Z = R("Zr", NL * r, NL * r + NL)
        zin = [X("Zin%d" % r)]
        V = R("V")
        lv(r, "v")
        act(V, Z, AF.Identity, bias=159.5005, scale=1.0 / 1024, more=zin)

        def sel(o, nm):
            return [(o, win(nm, 12 - 4 * l), R("V", l, 256, 4)) for l in range(4)]
        mm(sel(ps(0, 0, 64), "HK"))
        mm(sel(ps(7, 0, 64), "HS"))
        mm([(ps(1, 1, NS, 3), I, R("CB", 0, 64)), (ps(1, 2, NS, 3), I, R("CL", 0, 64))], stop=False)
        mm(sel(ps(1, 0, NS, 3), "HE") + sel(ps(1, 1, NS, 3), "HX") + sel(ps(1, 2, NS, 3), "H3"), start=False)
        ts(R("DA", 2, NS, 3), ps(0, 0, 64), -176.0, A.add)
        af(R("DA", 1, NS, 3), ps(7, 0, 64), None, 1.0)
        mm(sel(ps(7, 64, 128), "H4"))
        mm(sel(ps(7, 128, 192), "HA"))
        scan(R("sc"), R("DA"), ps(1, 0, NS), 0.0, A.mult, A.add)
        cp(R("ki", 64, 128), R("sc", 2, NS, 3))
        ts(R("hm", 0, 64), R("ki", 64, 128), 2, sh, 4095, an)
        cp(R("om"), R("hm", 0, 64))
        for a, b, eng in OPT["gp"]:
            lv(r, "g2" if a else "v")
            plus(eng, R("G", 16 * a, 16 * b), IND(Mw, R("om", a, b)), 0.0, more=MSK)
        lv(r, "rt")
        mm([(ps(6, 0, 256), R("RA"), V), (ps(6, 256, 512), R("RB"), V)], each=True)
        act(R("Rt", 1, 1024, 4), ps(6, 0, 256), AF.Abs, bias=1.0)
        act(R("Rt", 2, 1024, 4), ps(6, 256, 512), AF.Abs, bias=1.0)
        plus(OPT["rt_eng"], R("Rt", 3, 1024, 4), R("Rt", 1, 1024, 4), 0.0)
        lv(r, "rest")
        af(R("PA", 64, 128), ps(7, 64, 128), None, aBlk)
        mm([(ps(5, 0, 64), I, R("CB", 64, 128))] + sel(ps(5, 0, 64), "H5"))
        tt(R("vi", 64, 128), R("PA", 64, 128), ps(5, 0, 64), A.mult)
        ts(R("hn", 64, 128), R("vi", 64, 128), 4080, an)
        ts(R("hb", 0, 64), R("hn", 64, 128), -1824.0, A.add)
        plus(OPT["x_eng"], R("hb", 64, 128), R("sc", 1, NS, 3), 0.0)
        mm([(ps(5, 256, 512), R("HK2"), V)], stop=False)
        mm([(ps(5, 256 + l, 512, 4), R("EL%d" % l), R("hb", 64, 128)) for l in range(4)], start=False, stop=False)
        mm([(ps(5, 256 + l, 512, 4), R("EQ%d" % l if l else "ST"), R("hb", 0, 64)) for l in range(4)], start=False)
        if OPT["wr_act"]:
            af(R("wr"), ps(5, 256, 512), 1.0 / 4096, 100.0)
        else:
            ts(R("wr"), ps(5, 256, 512), R4096, A.add, -R4096, A.add)
        for h, b in enumerate(OPT["o_banks"]):
            c = 256 + 128 * h
            mm([(ps(b, c, c + 128), R("HK2"), R("V", 128 * h, 128 * h + 128))]
               + [(ps(b, c + l, c + 128, 4), R(m), R("hb", a + 32 * h, a + 32 * h + 32)) for l in range(4)
                  for m, a in (("EL%d" % l, 64), ("EQ%d" % l if l else "ST", 0))], stop=False)
        lv(r, "kc")
        af(R("PA", 0, 64), ps(7, 128, 192), None, aBest)
        mm([(ps(0, 64, 128), I, R("CB", 0, 64))] + sel(ps(0, 64, 128), "HB"))
        mm([(ps(0, 128, 192), I, R("CL", 64, 128))] + sel(ps(0, 128, 192), "HL"))
        mm(sel(ps(0, 192, 256), "HD"))
        tt(R("pu"), R("PA", 0, 64), ps(0, 64, 128), A.mult)
        tt(R("vi", 0, 64), R("pu"), ps(0, 128, 192), A.add)
        ts(R("hn", 0, 64), R("vi", 0, 64), 4080, an)
        ts(R("em"), ps(0, 192, 256), 43008.0, A.add, -2048.0, A.max)
        ts(R("hm", 64, 128), R("vi", 0, 64), 2, sh, 4095, an)
        tt(R("ks"), R("hm", 64, 128), R("em"), A.add)
        tt(R("kb"), R("hn", 0, 64), R("em"), A.add)
        mm([(ps(1, 192, 208), win("Bt2", 12 - 4 * a), R("ks", a, 64, 4)) for a in range(4)]
           + [(ps(1, 208, 224), win("Bt", 12 - 4 * a), R("ks", a, 64, 4)) for a in range(4)] + [(ps(1, 256, 320), R("B1"), R("kb"))])
        kc, kw, kf = R("kl", 0, 16), R("kl", 16, 32), R("kl", 32, 48)
        ts(kw, ps(1, 192, 208), 2048.0, A.add, 127.0, A.min)
        ts(kc, ps(1, 208, 224), 2048.0, A.add, 4096.0, A.min)
        ts(R("bl"), ps(1, 256, 320), cB1, A.add, 1023.0, A.min)
        lv(r, "w")
        act(R("Wp"), IND(R("WT"), kw), AF.Copy)
        for l0, n in OPT["sets"]:
            c = 4 * (l0 % 128)
            mm([(ps(3 + l0 // 128, c + n * x, c + n * x + n), SEL(x), R("Wp", l0, l0 + n)) for x in range(4)], each=True)
        lv(r, "of")
        for h, b in enumerate(OPT["o_banks"]):
            pO = ps(b, 256 + 128 * h, 384 + 128 * h)
            mm([(pO, R("N4096" if OPT["wr_act"] else "NI"), R("wr", 128 * h, 128 * h + 128))], start=False, stop=False)
            mm([(pO, win("Bd", 12 - 4 * k), R("G", 512 * h + k, 512 * h + 512, 4)) for k in range(4)], start=False)
            ts(R("of", 128 * h, 128 * h + 128), pO, 2040.0 + (100.0 * 4096 if OPT["wr_act"] else 0.0), A.add)
        Fw = R("Ft")
        lv(r, "keys")
        act(R("CMg"), IND(Mw, kc), AF.Copy, more=MSK)
        o = ps(1, 224, 240)
        mm([(o, win("Bt1", 12 - 4 * a), R("kb", a, 64, 4)) for a in range(4)]
           + [(o, EX(rho, "EX0"), R("CMg", rho, 256, 16)) for rho in range(16)])
        ts(R("Kh"), ps(1, 208, 240), 1.0 / 64, A.mult)
        ts(kf, o, 2048.0, A.add, 4096.0, A.min)
        lv(r, "fold")
        act(R("Fold"), IND(Fw, kf), AF.Copy)
        lv(r, "cold")
        if last:
            act(R("ycg"), IND(R("K"), kc), AF.Copy, more=[X("Ky")])
        else:
            act(R("Cold"), IND(R("Ct"), kc), AF.Copy)
            if r:
                ts(R("Hd"), R("CMg"), R16, A.add, -R16, A.add)
        lv(r, "e")
        eb = OPT["e_banks"]
        for q in range(4):
            mm([(ps(eb[0], 15 - x, 512, 16), m, R("Kh")) for x in range(4 * q, 4 * q + 4) for m in (SEL(x), R("NI"))],
               start=q == 0, stop=q == 3)
        scan(R("Z0"), ps(eb[0], 0, 512), R("RS0"), 1.0, A.mult, A.add)
        mm([(ps(eb[1], 176, 448, 17), I, R("RS1", 1, 17))], stop=False)
        for q in range(4):
            it = []
            for x in range(4 * q, 4 * q + 4):
                o = ps(eb[1], 177 + x, 448, 17)
                it += [(o, SEL(x), R("Kh", 0, 32, 2)), (o, R("NI"), R("Kh", 1, 32, 2))]
            mm(it, start=False, stop=q == 3)
        scan(R("Z1"), ps(eb[1], 176, 448), R("RS1"), 1.0, A.mult, A.add)
        ts(R("fl", 0, 32), R("Z0", 15, 512, 16), 0.0, A.is_equal, 8192.0, A.mult)
        ts(R("fl", 32, 48), R("Z1", 16, 272, 17), 0.0, A.is_equal, 8192.0, A.mult)
        mm([(ps(1, 448, 480), R("I64"), R("Kh")), (ps(1, 448, 480), I, R("fl", 0, 32)), (ps(1, 449, 480, 2), I, R("fl", 32, 48))])
        ts(R("so", 0, 32, 2), ps(1, 448, 480, 2), 2048.0, A.add, spE, A.min)
        ts(R("so", 1, 32, 2), ps(1, 449, 480, 2), 2048.0, A.add, spO, A.min)
        if r == 0 and not OPT["pf0"]:
            pairs_of(0, (2, 1, 2, 1))
        lv(r, "ug")
        for a, b, eng in OPT["ug"]:
            for q in range(2):
                plus(eng, R("Ug", 1024 * q + 4 * a, 1024 * q + 4 * b), IND(R(PF, 1024 * q, 1024 * q + 1024), R("bl", a // 4, b // 4)), 0.0)

        def train(c, n):
            hs = range(c // 128, (c + n) // 128)
            both = OPT["merge"]
            t = str(hs[-1])
            bu, bk = (5, 6) if both else (5 + hs[0], 5 + hs[0])
            bF, cF = (OPT["f_bank"], c) if both else (bk, 128)
            lv(r, "u" + t)
            for h in hs:
                mm([(ps(3 + h, x, 512, 4), I, R("gs", 128 * h, 128 * h + 128)) for x in range(4)], each=True)
            lv(r, "fn" + t)
            mm([(ps(bF, cF, cF + n), I, R("Fold", c, c + n)), (ps(bF, cF, cF + n), I, R("gs", c, c + n))])
            ts(R("Fnew", c, c + n), ps(bF, cF, cF + n), 0.0, A.max, 255.0, A.min)
            lv(r, "u" + t)
            for h in hs:
                gs = R("gs", 128 * h, 128 * h + 128)
                if both:
                    if h == 0:
                        mm([(ps(bu, a, a + 64), I, R("GB", 0, 64)) for a in (0, 64, 192)], stop=False)
                    mm([(ps(bu, 128 + 64 * h, 192 + 64 * h), gs, R("GB", 64, 128))], start=False, stop=False)
                else:
                    mm([(ps(bu, 0, 128), gs, R("GB"))], stop=False)
                for q in range(2):
                    u0 = 1024 * q + 512 * h
                    tt(R("Up", u0, u0 + 512), R("Ug", u0, u0 + 512), ps(3 + h, 0, 512), A.mult)
                    o0 = 64 * h if both else 0
                    mm([(ps(bu, o0 + 4 * q + x, o0 + 4 * q + x + (185 if both else 121), 8), R("Up", u0 + x, u0 + 512, 4), R("BB")) for x in range(4)],
                       start=False, stop=q == 1 and (h == 1 or not both))
            if not both:
                probes(c, n, bu, bk, 128, 256, 384)
            elif c + n == 256:
                probes(0, 256, bu, bk, 256, 0, 256)

        def probes(c, n, bu, bk, cF, cK, cN):
            hs = range(c // 128, (c + n) // 128)
            t = str(hs[-1])

            def H(name, h=None):
                return R(name, c, c + n) if h is None else R(name, 128 * h, 128 * h + 128)

            def P(b, c0, h=None):
                return ps(b, c0, c0 + n) if h is None else ps(b, c0 + 128 * h - c, c0 + 128 * h - c + 128)
            lv(r, "c" + t)
            if not last:
                mm([(P(bk, cK, h), H(a, h), m) for h in hs for a, m in [("Cold", I)] + ([("CMg", R("U1")), ("Hd", R("U2"))] if r else [])],
                   stop=not OPT["key_pe"])
            lv(r, "x" + t)
            r32 = R("R32", c // 2, (c + n) // 2)
            ts(r32, ps(bu, 0, n // 2), R8192, A.add, -R8192, A.add)
            tt(R("Xs", c, c + n, 2), ps(bu, 0, n // 2), r32, A.subtract)
            ts(R("Xs", c + 1, c + n, 2), ps(bu, n // 2, n), R8192, A.add, -R8192, A.add)
            if last:
                mm([(P(bk, cF, h), H("Xs", h), I) for h in hs], each=True)
                act(H("us"), P(bk, cF), AF.Sign)
                mm([(P(bk, cK), EX(0, "BY"), H("us"))])
                act(H("d3"), P(bk, cK), AF.Copy)
                return
            ts(H("ut"), H("Xs"), -1.0, A.max, 1.0, A.min)
            if OPT["key_pe"]:
                mm([(P(bk, cK), I, H("ut"))], start=False)
                scan(H("Km"), R("D0", 0, n), P(bk, cK), 0.0, A.add, A.max)
            else:
                tt(H("key"), P(bk, cK), H("ut"), A.add)
                scan(H("Km"), R("D0", 0, n), H("key"), 0.0, A.add, A.max)
            kr, km = R("kr", c // 16, (c + n) // 16), R("Km", c + 15, c + n, 16)
            ts(kr, km, R1, A.add, -R1, A.add)
            tt(R("Mx", c, c + n, 16), kr, km, A.subtract)
            lv(r, "us" + t)
            b3 = 3 + hs[0]
            mm([(P(b3, 0, h), H("ut", h), I) for h in hs], each=True)
            act(H("us"), P(b3, 0), AF.Copy)
            mm([(P(bu, cN), R("KP"), H("CMg")), (P(bu, cN), R("PK"), H("us"))], stop=False)
            mm([(P(bu, cN, h), H("Mx", h), R("I64")) for h in hs], start=False)
            af(H("CMn"), P(bu, cN), None, b15)

        def signs(c, n, ys):
            pD = ps(7, c, c + n)
            t = str((c + n) // 128 - 1)
            lv(r, "t" + t)
            mm([(pD, R("I32"), R("Zr", NL * r + c, NL * r + c + n)), (pD, R("TT"), R("V", c, c + n))], stop=False, more=zin)
            lv(r, "g" + t)
            for i, (a, y) in enumerate(ys):
                mm([(ps(7, a, a + y["n"]), R("N256"), y)], start=False, stop=i == len(ys) - 1)
            act(R("gs", c, c + n), pD, AF.Sign, bias=bG)
            train(c, n)

        yb = NL * r
        Y = []
        for l0, n in OPT["sets"]:
            n3 = max(l0 // 64 - 1, 0)
            lv(r, "f%d" % n3)
            for a, b, eng in OPT["fp"]:
                if l0 <= a < l0 + n:
                    plus(eng, R("Vg", 16 * a, 16 * b), IND(Fw, R("of", a, b)), -128.0)
            pY = ps(OPT["y_banks"][n3], l0, l0 + n)
            b, c, w = 16 * l0, 4 * l0, 4 * (l0 % 128)
            for x0, x1 in OPT["sw"]:
                for x in range(x0, x1):
                    scan(R("Hs", b + 4 * n * x, b + 4 * n * x + 4 * n), R("Rt", c, c + 4 * n), R("Vg", b + x, b + 16 * n, 4), 0.0, A.mult, A.add)
                tt(R("SW", c + n * x0, c + n * x1), R("Hs", b + 4 * n * x0 + 3, b + 4 * n * x1, 4),
                   ps(3 + l0 // 128, w + n * x0, w + n * x1), A.mult)
                mm(([(pY, I, R("cy", 0, n))] if x0 == 0 else [])
                   + [(pY, R("I32"), R("SW", c + n * x, c + n * x + n)) for x in range(x0, x1)], start=x0 == 0, stop=x1 == 4)
            if l0 + n < 128:
                continue
            y0, yn = ((0, 128), (128, 64), (192, 64))[n3]
            y = R("Yb", 192 * me, 192 * me + 64) if n3 == 2 else R("Ys", yb + y0, yb + y0 + yn)
            Y.append((y0, y))
            ts(y, ps(OPT["y_banks"][n3], y0, y0 + yn), R256, A.add, -R256, A.add)
            if n3 < 2:
                exchange("bk%d" % r, lambda o, yb=yb: T.Ys[:, yb + 64 * place(o, me):yb + 64 * place(o, me) + 64],
                         lambda o: T.Yb[:, 192 * me:192 * me + 64], "Yin%d%d" % (r, n3), [y],
                         [o for o in range(N) if place(o, me) == 2] if n3 else [o for o in range(N) if place(o, me) < 2])
            if OPT["merge_g"]:
                if n3 == 2:
                    signs(0, 256, Y)
            elif n3 != 1:
                signs(128 * (n3 // 2), 128, Y[1:] if n3 else Y)

        def scatter(w, src, c0, more=()):
            for t in [2 * place(q, me) + x for q in range(N - 1, -1, -1) for x in (1, 0)]:
                o = IND(w, R("so", c0 + 2 * t, c0 + 2 * t + 2))
                also = [R("so")] + list(more) + [R(src[-1])]
                if len(src) == 1:
                    cp(o, R(src[0], 32 * t, 32 * t + 32), also)
                else:
                    tt(o, R(src[0], 32 * t, 32 * t + 32), R(src[1], 32 * t, 32 * t + 32), A.add, also)
        lv(r, "fs")
        scatter(Fw, ["Fnew"], 16)
        if last:
            dma("sp", [(T.yf[:, 2048 * h:2048 * h + 2048], T.Ft[:, 2048 * h:2048 * h + 2048]) for h in range(2)], [], [Fw], 6000)
            lv(r, "ms")
            scatter(R("K"), ["ycg", "d3"], 0, [X("Ky")])
            dma("sp", [(T.yc[:], T.K[0::16, 0:WC])], [], [R("K")], 2200)
        else:
            lv(r, "ms")
            scatter(Mw, ["CMn"], 0, MSK)
            shift()
            pairs_of(r + 1, OPT["pf_banks"])
            lv(r, "yc")
            if r == 2:
                for x in (13, 14):
                    dma("pool", [(T.K[0::16, 2048 * h:2048 * h + 2048], T.Ms[x::16, MB + 2048 * h:MB + 2048 * h + 2048]) for h in range(2)],
                        [R("K"), X("Ky")], [R("Ms")], 3500, acc=True)
        lv(r, "home")
        yin = [X("Yin%d0" % r), X("Yin%d1" % r)]
        d = IND(R("Yb"), R("dst", 16 * r, 16 * r + 12))
        ts(R("ycl"), d, -2048.0, A.max, 2048.0, A.min, more=yin)
        act(R("Yg", NS * r, NS * r + NS), d, AF.Copy, more=yin)
        route(r + 1)

    dma("sp", [(T.yx[e::4, :], T.yxo[e::16, :]) for e in range(4)], [], [R("yxo")], 2200)
    o = ps(7, 256, 256 + NS)
    mm([(o, R("YW"), R("Sg", NS * r, NS * r + NS)) for r in range(RO)] + [(o, R("I256"), R("Yg", NS * r, NS * r + NS)) for r in range(RO)])
    af(R("yso"), o, None, -512.0)
    dma("sp", [(T.ys[:], T.yso[:])], [], [R("yso")], 2200)
    return ops


def meet(a, b):
    if a["c0"] >= b["c1"] or b["c0"] >= a["c1"]:
        return False
    return (a["c0"] - b["c0"]) % math.gcd(a["st"], b["st"]) == 0


def depend(ops):
    hist = {}
    bank = {}
    for i, op in enumerate(ops):
        op["i"] = i
        dep = set(a["i"] for a in op["after"])
        wait = set()
        e = op["eng"]
        acc = [(v, False) for v in op["rd"]] + [(v, True) for v in op["wr"]]
        for v, w in acc:
            h = hist.setdefault(v["key"], [])
            if v["ps"]:
                b = bank.setdefault(v["key"], [e, [], []])
                if b[0] != e:
                    b[:] = [e, [], b[1]]
                wait.update(b[2])
                if e == "pe":
                    dep.update(b[1][-2:])
                b[1].append(i)
            for j, u, jw in h:
                if (w or jw) and meet(u, v):
                    if e == "pe" and ops[j]["eng"] == e:
                        dep.add(j)
                    else:
                        wait.add(j)
        for v, w in acc:
            h = hist[v["key"]]
            if w:
                h[:] = [x for x in h if not (v["c0"] <= x[1]["c0"] and x[1]["c1"] <= v["c1"] and x[1]["st"] % v["st"] == 0 and meet(x[1], v))]
            h.append((i, v, w))
        wait.discard(i)
        dep.discard(i)
        op["wait"] = wait
        op["dep"] = sorted(dep | wait)


def price(ops, p):
    for op in ops:
        k, n = op["size"]
        f = p["fa"] if op["eng"] == "act" else p["fv"]
        if k == "el":
            c = f + max(n, 32 if op["eng"] == "act" else 64) * p["cyc"]
        elif k in ("gat", "sca"):
            c = f + n * p[k] * p["cyc"]
        elif k == "tt2":
            c = f + max(64, n * p[k]) * p["cyc"]
        elif k == "mm":
            c = n * p["pe"]
        elif k == "iota":
            c = (130 + 2 * n) * p["cyc"]
        else:
            c = n
        op["cost"] = c
        op["l"] = 0 if op["lat"] is None else p[op["lat"][0]] * op["lat"][1]


def gap(ops, j, i, p):
    if j not in ops[i]["wait"]:
        return -ops[j]["l"]
    return p["same"] if ops[j]["eng"] == ops[i]["eng"] and ops[j]["lat"] is None else p["hop"]


def schedule(ops, p, others=()):
    n = len(ops)
    price(ops, p)
    cost = [op["cost"] for op in ops]
    eng = [op["eng"] for op in ops]
    pred = [[(j, ops[j]["l"] + gap(ops, j, i, p)) for j in op["dep"]] for i, op in enumerate(ops)]
    succ = [[] for _ in range(n)]
    for i in range(n):
        for j, d in pred[i]:
            succ[j].append((i, d))
    tail = [0.0] * n
    lev = [0.0] * n
    for i in range(n - 1, -1, -1):
        tail[i] = cost[i] + max([d + tail[k] for k, d in succ[i]] + [ops[i]["l"]])
        if ops[i]["lv"] is None:
            lev[i] = min([lev[k] for k, d in succ[i]] + [1e4])
        else:
            r, name = ops[i]["lv"]
            lev[i] = 100 * r + LEVEL.get(name, 0)
    key = [(lev[i], -tail[i], i) for i in range(n)]
    left = [len(q) for q in pred]
    ready = {e: [i for i in range(n) if eng[i] == e and not left[i]] for e in sorted(set(eng))}
    est = [0.0] * n
    free = {e: 0.0 for e in ready}
    order = []
    for _ in range(n):
        t, e = min((max(free[e], min(est[i] for i in lst)), e) for e, lst in ready.items() if lst)
        i = min((k for k in ready[e] if est[k] <= t + 20), key=lambda k: key[k])
        i = min([i] + [k for k in ready[e] if est[k] < t + OPT["hold"] * cost[i]], key=lambda k: key[k])
        ready[e].remove(i)
        free[e] = max(t, est[i]) + cost[i]
        order.append(i)
        for k, d in succ[i]:
            est[k] = max(est[k], free[e] + d)
            left[k] -= 1
            if not left[k]:
                ready[eng[k]].append(k)

    above = [0] * n
    before = []
    for i in range(n):
        m = 0
        for j, d in pred[i]:
            m |= above[j]
        before.append(set(j for j, d in pred[i] if not m >> j & 1))
        above[i] = m | sum(1 << j for j in before[i] if j in ops[i]["wait"] or ops[j]["lat"] is None)
    after = [set() for _ in range(n)]
    for i in range(n):
        for j in before[i]:
            after[j].add(i)
    cases = []
    for q in [p] + [dict(p, **x) for x in others]:
        price(ops, q)
        cases.append(([op["cost"] for op in ops],
                      [[(j, ops[j]["cost"] + ops[j]["l"] + gap(ops, j, i, q)) for j in sorted(before[i])] for i in range(n)],
                      [(i, ops[i]["cost"] + ops[i]["l"]) for i in range(n) if not succ[i]],
                      [[(k, ops[i]["cost"] + ops[i]["l"] + gap(ops, i, k, q)) for k in sorted(after[i])] for i in range(n)],
                      [op["cost"] + op["l"] for op in ops]))

    def times(case, seq, a=0, old=None):
        cost, near, sinks, far, lat = case
        h, by = (list(old[1]), list(old[2])) if a else ([0.0] * n, [-1] * n)
        last = {eng[k]: k for k in seq[:a]}
        for i in seq[a:]:
            b = last.get(eng[i], -1)
            t = h[b] + cost[b] if b >= 0 else 0.0
            for j, d in near[i]:
                x = h[j] + d
                if x > t:
                    t, b = x, j
            h[i], by[i], last[eng[i]] = t, b, i
        end, at = max((h[i] + c, i) for i, c in sinks)
        return end, h, by, at

    def tails(case, seq, b, old):
        cost, near, sinks, far, lat = case
        q = list(old)
        nxt = {eng[k]: k for k in seq[:b:-1]}
        for i in seq[b::-1]:
            k = nxt.get(eng[i], -1)
            t = cost[i] + q[k] if k >= 0 else 0.0
            if lat[i] > t:
                t = lat[i]
            for k, d in far[i]:
                x = q[k] + d
                if x > t:
                    t = x
            q[i], nxt[eng[i]] = t, i
        return q

    def through(case, now, rest, part, first, final):
        cost, near, sinks, far, lat = case
        h, h2, last = now[1], {}, dict(first)
        for i in part:
            b = last[eng[i]]
            t = h2.get(b, h[b]) + cost[b] if b >= 0 else 0.0
            for j, d in near[i]:
                x = h2.get(j, h[j]) + d
                if x > t:
                    t = x
            h2[i], last[eng[i]] = t, i
        top = 0.0
        for i, t in h2.items():
            x = lat[i]
            for k, d in far[i]:
                if k not in h2 and rest[k] + d > x:
                    x = rest[k] + d
            if t + x > top:
                top = t + x
        for e, k in final.items():
            if k >= 0 and h2[last[e]] + cost[last[e]] + rest[k] > top:
                top = h2[last[e]] + cost[last[e]] + rest[k]
        return top

    def pack(seq, cost, near):
        h = [0.0] * n
        busy = {e: ([], []) for e in set(eng)}
        for i in seq:
            t = 0.0
            for j, d in near[i]:
                if h[j] + d > t:
                    t = h[j] + d
            s, f = busy[eng[i]]
            k = len(s)
            while k and s[k - 1] >= t:
                k -= 1
            if k and f[k - 1] > t:
                t = f[k - 1]
            while k < len(s) and t + cost[i] > s[k]:
                t = f[k]
                k += 1
            s.insert(k, t)
            f.insert(k, t + cost[i])
            h[i] = t
        return h

    def turn(seq, case, noise):
        cost, near, sinks, far, lat = case
        h = times(case, seq)[1]
        back = [[(k, d - cost[i] + cost[k]) for k, d in far[i]] for i in range(n)]
        fin = [h[i] + cost[i] + noise[i] for i in range(n)]
        for i in range(n):
            for j, d in near[i]:
                fin[i] = max(fin[i], fin[j] + 1e-3)
        tailed = [b + [] for b in back]
        for i, c in sinks:
            tailed[i] = [(i, c - cost[i])]
        q = pack(sorted(range(n), key=lambda i: -fin[i]), cost, tailed)
        late = [-(q[i] + cost[i]) for i in range(n)]
        for i in range(n):
            for j, d in near[i]:
                late[i] = max(late[i], late[j] + 1e-3)
        h = pack(sorted(range(n), key=lambda i: late[i]), cost, near)
        for i in range(n):
            for j, d in near[i]:
                h[i] = max(h[i], h[j] + 1e-3)
        return sorted(range(n), key=lambda i: h[i])

    base = [times(c, order)[0] for c in cases]
    rs = np.random.RandomState(OPT["seed"] + 1)
    top = here = (float(len(cases)), order)
    names = sorted(set(op["lv"] or (0, "") for op in ops))
    part_of = np.array([names.index(op["lv"] or (0, "")) for op in ops])
    for it in range(OPT["turns"]):
        noise = rs.random_sample(n) * rs.random_sample() * OPT["noise"]
        noise += ((rs.random_sample(len(names)) - 0.5) * (rs.random_sample(len(names)) < OPT["share"]))[part_of] * OPT["shove"]
        new = turn(here[1], cases[it % len(cases)], noise.tolist())
        v = sum(times(c, new)[0] / b for c, b in zip(cases, base))
        if v < here[0] - math.log(rs.random_sample() + 1e-12) * OPT["warm"] * (1 - it / OPT["turns"]):
            here = (v, new)
        if v < top[0]:
            top = (v, new)
    order = top[1]
    draws = np.random.RandomState(OPT["seed"]).random_sample((OPT["moves"], 5)).tolist()
    now = [times(c, order) for c in cases]
    rest = [tails(c, order, n - 1, [0.0] * n) for c in cases]
    weight = [now[0][0] / x[0] / len(cases) for x in now]
    order.sort(key=lambda k: now[0][1][k])
    end = now[0][0]
    best = (end, order)
    edges = None
    for it, (x0, x1, x2, x3, x4) in enumerate(draws):
        if edges is None:
            edges = []
            for _e, h, by, i in now:
                while by[i] >= 0:
                    if eng[by[i]] == eng[i] and by[i] not in before[i]:
                        edges.append((by[i], i))
                    i = by[i]
            pos, ahead, behind, last = [0] * n, [-1] * n, [-1] * n, {}
            for q, k in enumerate(order):
                pos[k] = q
                j = ahead[k] = last.get(eng[k], -1)
                behind[j] = k if j >= 0 else behind[j]
                last[eng[k]] = k
        if not edges:
            break
        j, i = edges[int(x0 * len(edges))]
        a, b = pos[j], pos[i]
        up = x1 < 0.5
        far = 1 + int(7 * x2) if x3 < 0.5 else 0
        while far and 0 < a and b < n - 1:
            a, b = (a - 1, b) if up else (a, b + 1)
            far -= eng[order[a if up else b]] == eng[i]
        seg = order[a:b + 1]
        need = {i if up else j}
        for k in (seg[::-1] if up else seg):
            if not need.isdisjoint(after[k] if up else before[k]):
                need.add(k)
        if seg[0 if up else -1] in need:
            continue
        move, stay = [k for k in seg if k in need], [k for k in seg if k not in need]
        part = move + stay if up else stay + move
        room = -math.log(x4 + 1e-12) * OPT["heat"] * (1.02 - it / OPT["moves"])
        first, final = {eng[k]: ahead[k] for k in seg[::-1]}, {eng[k]: behind[k] for k in seg}
        more = sum(w * (through(c, x, y, part, first, final) - x[0]) for c, x, y, w in zip(cases, now, rest, weight))
        if more > room or (more > -1 and x2 * 64 % 1 > OPT["drift"]):
            continue
        new = order[:a] + part + order[b + 1:]
        then = [times(c, new, a, x) for c, x in zip(cases, now)]
        more = sum(w * (y[0] - x[0]) for x, y, w in zip(now, then, weight))
        if more <= room:
            rest = [tails(c, new, b, y) for c, y in zip(cases, rest)]
            now, end = then, end + more
            order = sorted(new, key=lambda k: now[0][1][k])
            edges = None
            if end < best[0]:
                best = (end, order)
    ALL[:] = [times(c, best[1])[0] for c in cases]
    end, h, by, at = times(cases[0], best[1])
    price(ops, p)
    return best[1], [h[i] + op["cost"] + op["l"] for i, op in enumerate(ops)]


ORDERS = {}
ALL = []


def emit(g, T, ops, order, ends):
    queue = {"dve": g.vector, "act": g.scalar, "pe": g.tensor, "pool": g, "sp": g.sync}
    count = {}
    known = {e: {} for e in queue}
    total = {}
    needed = set()
    for op in ops:
        needed.update(op["wait"])
    for i in order:
        op = ops[i]
        e = op["eng"]
        kn = known[e]
        want = {}
        for j in op["wait"]:
            s, v = ops[j]["sig"]
            if v > want.get(s, (0, 0))[0]:
                want[s] = (v, j)
        for s in sorted(want, key=lambda k: -ends[want[k][1]]):
            v, j = want[s]
            if kn.get(s, 0) < v:
                queue[e].wait_ge(T.sem[s], v)
                kn[s] = v
                for s2, v2 in ops[j]["clock"].items():
                    if kn.get(s2, 0) < v2:
                        kn[s2] = v2
        ins = op["fn"]()
        if op["sem"] is not None:
            op["sig"] = op["sem"]
            total[op["sem"][0]] = op["sem"][1]
            if "sent" in op:
                total["sent"] = total.get("sent", 0) + op["sent"]
            op["clock"] = {} if "sent" in op else dict(kn)
        else:
            if i in needed:
                count[e] = count.get(e, 0) + 1
                ins.then_inc(T.sem[e], 1)
                total[e] = count[e]
            op["sig"] = (e, count.get(e, 0))
            op["clock"] = dict(kn)
    for s in sorted(total):
        g.wait_ge(T.sem[s], total[s])


def rank_program(g, core, T, topo):
    if T.rank_of(core) is None:
        return
    ops = build(g, T, topo, core)
    depend(ops)
    shape = tuple((op["eng"], op["size"], tuple(op["dep"])) for op in ops)
    if shape not in ORDERS:
        ORDERS[shape] = schedule(ops, GUESS, OTHERS)
    emit(g, T, ops, *ORDERS[shape])
